import numpy as np
import ml_dtypes


def mxq(x, axis, fmt="e4m3"):
    dtype, down = {"e4m3": (ml_dtypes.float8_e4m3fn, 7), "e5m2": (ml_dtypes.float8_e5m2, 14)}[fmt]
    v = np.moveaxis(np.asarray(x, np.float32).astype(ml_dtypes.bfloat16).astype(np.float64), axis, -1)
    blocks = v.reshape(v.shape[:-1] + (-1, 32))
    amax = np.abs(blocks).max(-1, keepdims=True)
    byte = np.maximum(np.where(amax > 0, np.frexp(amax)[1] - 1 + 127, 0) - down, 1)
    scale = np.exp2(byte - 127.0)
    codes = (blocks / scale).astype(np.float32).astype(dtype).astype(np.float64)
    return np.moveaxis((codes * scale).reshape(v.shape), -1, axis)


WIDE = False


def mx_kscale(k):
    if not WIDE:
        return np.ones(k)
    levels = np.array([10, -10, 5, -5, 0])
    if k % 512:
        return np.exp2(np.random.permutation(np.resize(levels, k // 32))).repeat(32)
    a = np.empty((k // 512, 16))
    for p in range(k // 512):
        a[p, :8] = np.random.permutation(np.resize(levels, 8))
        for g in range(8):
            far = levels[np.abs(levels - a[p, g]) >= 10]
            a[p, g + 8] = far[np.random.randint(len(far))]
    return np.exp2(a.ravel()).repeat(32)


def f64(x):
    return np.asarray(x).astype(np.float64)


def striped(idx):
    return np.tile(idx.reshape(-1, 16).T, (8, 1)).astype(np.uint16)


def unstriped(offs):
    return offs[:16].T.reshape(-1).astype(np.int64)


E2M1 = np.array([0.0, 0.5, 1.0, 1.5, 2.0, 3.0, 4.0, 6.0, -0.0, -0.5, -1.0, -1.5, -2.0, -3.0, -4.0, -6.0])


def pack_weight(w, fmt):
    k, n = w.shape
    w = f64(np.asarray(w, np.float32).astype(ml_dtypes.bfloat16)).reshape(k // 32, 32, n)
    amax = np.abs(w).max(1)
    if fmt == "e4m3":
        byte = np.frexp(amax)[1] - 1 + 127 - 7
    else:
        mant, ex = np.frexp(amax / 6.0)
        byte = np.where(mant > 0.5, ex, ex - 1) + 127
    byte = np.clip(np.where(amax > 0, byte, 1), 1, 254)
    scaled = (w * np.exp2(127.0 - byte)[:, None, :]).reshape(k, n).astype(np.float32)
    by_word = np.ascontiguousarray(scaled.reshape(k // 512, 128, 4, n).transpose(0, 1, 3, 2))
    if fmt == "e4m3":
        words = by_word.astype(ml_dtypes.float8_e4m3fn).view(np.uint8)
    else:
        c = by_word.astype(ml_dtypes.float4_e2m1fn).view(np.uint8) & 0xF
        words = (c[..., 0::2] | (c[..., 1::2] << 4)).reshape(k // 512, 128, 2 * n)
    return np.ascontiguousarray(words), np.ascontiguousarray(byte.astype(np.uint8).reshape(k // 512, 16, n))


def unpack_weight(words, scales, fmt):
    g, _, n = scales.shape
    words = np.ascontiguousarray(words).reshape(g, 128, n, -1)
    if fmt == "e4m3":
        vals = words.view(ml_dtypes.float8_e4m3fn).astype(np.float64)
    else:
        nib = np.empty((g, 128, n, 4), np.uint8)
        nib[..., 0::2] = words & 0xF
        nib[..., 1::2] = words >> 4
        vals = E2M1[nib]
    vals = vals * np.repeat(np.exp2(scales.astype(np.float64) - 127.0), 8, axis=1)[..., None]
    return vals.transpose(0, 1, 3, 2).reshape(g * 512, n)


def gelu(v):
    return 0.5 * v * (1.0 + np.tanh(np.sqrt(2.0 / np.pi) * (v + 0.044715 * v**3)))


K, T, T2, S, H, N = 512, 2048, 2048, 1024, 1536, 768

def setup_inputs():
    n = np.random.standard_normal
    s = mx_kscale(K)[:, None]
    u = mx_kscale(H)[:, None]
    tab_words, tab_scales = pack_weight(n((K, T)) * s, "e4m3")
    wc_words, wc_scales = pack_weight(n((K, H)) / np.sqrt(K) / s, "e2m1")
    xT = (np.round(16 * n((K, T2))) / 16 * s).astype(np.float32)
    wd = (n((K, H)) * 0.7 / np.sqrt(K) / s).astype(np.float32)
    gain = (np.random.uniform(0.6, 1.6, H) * u[:, 0]).astype(np.float32)
    wo_words, wo_scales = pack_weight(1.5 * n((H, N)) / np.sqrt(H) / u, "e4m3")
    obs = (0.7 * n((N, S))).astype(np.float32)
    order = np.random.permutation(T2)
    return {"tab_words": tab_words, "tab_scales": tab_scales,
            "wc_words": wc_words, "wc_scales": wc_scales,
            "xT": xT, "wd": wd, "gain": gain,
            "wo_words": wo_words, "wo_scales": wo_scales, "obs": obs,
            "offs": striped(np.random.permutation(T)[:S]),
            "offs2": striped(order[1:S + 1]), "offs3": striped(order[:S])}

def reference(tab_words, tab_scales, wc_words, wc_scales, xT, wd, gain,
              wo_words, wo_scales, obs, offs, offs2, offs3):
    v = unpack_weight(tab_words, tab_scales, "e4m3")[:, unstriped(offs)]
    wc = unpack_weight(wc_words, wc_scales, "e2m1")
    wo = unpack_weight(wo_words, wo_scales, "e4m3")
    x = f64(xT)[:, unstriped(offs2)] - f64(xT)[:, unstriped(offs3)]
    clim = wc.T @ v
    drift = mxq(f64(wd), 0, "e4m3").T @ mxq(x, 0, "e4m3")
    h = f64(gain)[:, None] * np.tanh(clim * drift)
    corr = wo.T @ mxq(h, 0, "e4m3")
    return f64(obs) - corr

@@ -1,0 +1,233 @@
+from contextlib import ExitStack
+
+import concourse.mybir as mybir
+
+K, T, S, H, N = 512, 2048, 1024, 1536, 768
+FLOPS = 2 * S * (2 * K * H + H * N)
+
+F32 = mybir.dt.float32
+BF16 = mybir.dt.bfloat16
+I32 = mybir.dt.int32
+U32 = mybir.dt.uint32
+U16 = mybir.dt.uint16
+U8 = mybir.dt.uint8
+FP8X4 = mybir.dt.float8_e4m3fn_x4
+FP4X4 = mybir.dt.float4_e2m1fn_x4
+MULT = mybir.AluOpType.mult
+SUBTRACT = mybir.AluOpType.subtract
+TANH = mybir.ActivationFunctionType.Tanh
+
+P = 128
+PACK = 4
+PASS = P * PACK
+HALF = 512
+HALVES = S // HALF
+R_PASSES = H // PASS
+N_TILES = N // P
+LIST_COLS = HALF // 16
+
+
+def tile_list_argo_cast_check_kernel(
+    tc, tab_words, tab_scales, wc_words, wc_scales, xT, wd, gain, wo_words, wo_scales, obs, offs, offs2, offs3, out
+):
+    nc = tc.nc
+    with ExitStack() as ctx:
+        keep = ctx.enter_context(tc.tile_pool(name="keep", bufs=1))
+        ring = ctx.enter_context(tc.tile_pool(name="ring", bufs=2))
+        psum = ctx.enter_context(tc.psum_pool(name="psum", bufs=1))
+
+        def held(shape, dtype, name):
+            return keep.tile(shape, dtype, name=name, align_bytes=64)
+
+        banks = [psum.tile([P, HALF], F32, name=f"bank{b}") for b in range(8)]
+
+        list1 = keep.tile([P, S // 16], U16, name="list1")
+        list2 = keep.tile([P, S // 16], U16, name="list2")
+        list3 = keep.tile([P, S // 16], U16, name="list3")
+        tab_w = held([P, T], I32, "tab_w")
+        tab_s = held([P, T], U8, "tab_s")
+        wc_w_raw = held([P, 2 * H], U8, "wc_w_raw")
+        wc_s_raw = held([P, H], U8, "wc_s_raw")
+        wc_w = held([P, 2 * H], U8, "wc_w")
+        wc_s = held([P, H], U8, "wc_s")
+        wo_w = held([P, R_PASSES, N], I32, "wo_w")
+        wo_s = held([P, R_PASSES, N], U8, "wo_s")
+        gains = held([P, R_PASSES, PACK], F32, "gains")
+        x_planes = [held([P, T], F32, f"x_plane{t}") for t in range(PACK)]
+        wd_raw = [held([P, PACK, PASS], F32, f"wd_raw{a}") for a in range(R_PASSES)]
+        obs_sb = [held([P, S], F32, f"obs{n}") for n in range(N_TILES)]
+
+        nc.vector.memset(wc_s_raw[:].bitcast(I32), 0)
+        nc.vector.memset(tab_s[:].bitcast(I32), 0)
+        nc.vector.memset(wo_s[:].rearrange("p a n -> p (a n)").bitcast(I32), 0)
+
+        x_rows = xT.rearrange("(p t) c -> p t c", t=PACK)
+        wd_rows = wd.rearrange("(p j) c -> p j c", j=PACK)
+        nc.sync.dma_start(out=list1[:], in_=offs)
+        nc.sync.dma_start(out=wc_w_raw[:].bitcast(I32), in_=wc_words[0].bitcast(I32))
+        for q in range(4):
+            nc.sync.dma_start(
+                out=wc_s_raw[32 * q : 32 * q + 4, :].bitcast(I32), in_=wc_scales[0, 4 * q : 4 * q + 4, :].bitcast(I32)
+            )
+        nc.sync.dma_start(out=tab_w[:], in_=tab_words[0].rearrange("p c i -> p (c i)").bitcast(I32))
+        for q in range(4):
+            nc.sync.dma_start(
+                out=tab_s[32 * q : 32 * q + 4, :].bitcast(I32), in_=tab_scales[0, 4 * q : 4 * q + 4, :].bitcast(I32)
+            )
+        nc.sync.dma_start(out=list3[:], in_=offs3)
+        nc.sync.dma_start(out=list2[:], in_=offs2)
+
+        def load_x(t):
+            nc.sync.dma_start(out=x_planes[t][:], in_=x_rows[:, t, :])
+
+        def load_wd(a):
+            nc.sync.dma_start(out=wd_raw[a][:], in_=wd_rows[:, :, a * PASS : (a + 1) * PASS])
+
+        load_x(0)
+        load_wd(0)
+        load_x(1)
+        load_wd(1)
+        load_x(2)
+        load_x(3)
+        load_wd(2)
+        nc.sync.dma_start(out=gains[:], in_=gain.rearrange("(a p t) -> p a t", p=P, t=PACK))
+        for q in range(4):
+            nc.sync.dma_start(
+                out=wo_s[32 * q : 32 * q + 4, :, :].bitcast(I32),
+                in_=wo_scales[:, 4 * q : 4 * q + 4, :].rearrange("a r n -> r a n").bitcast(I32),
+            )
+        nc.sync.dma_start(out=wo_w[:], in_=wo_words.rearrange("a p c i -> p a (c i)").bitcast(I32))
+        for n in range(N_TILES):
+            nc.sync.dma_start(out=obs_sb[n][:], in_=obs[n * P : (n + 1) * P, :])
+
+        nc.vector.tensor_copy(
+            out=wc_w[:].bitcast(U16).rearrange("p (a t m) -> p a t m", a=R_PASSES, t=PACK),
+            in_=wc_w_raw[:].bitcast(U16).rearrange("p (a m t) -> p a t m", a=R_PASSES, t=PACK),
+        )
+        nc.vector.tensor_copy(
+            out=wc_s[:].rearrange("p (a t m) -> p a t m", a=R_PASSES, t=PACK),
+            in_=wc_s_raw[:].rearrange("p (a m t) -> p a t m", a=R_PASSES, t=PACK),
+        )
+
+        def list_half(lst, h):
+            return lst[:, h * LIST_COLS : (h + 1) * LIST_COLS]
+
+        v_w = [held([P, HALF], U32, f"v_w{h}") for h in range(HALVES)]
+        v_s = [held([P, HALF], U8, f"v_s{h}") for h in range(HALVES)]
+        for h in range(HALVES):
+            nc.vector.tensor_copy(out=v_w[h][:], in_=tab_w[:].bitcast(U32).indirect(list_half(list1, h)))
+            nc.vector.tensor_copy(out=v_s[h][:], in_=tab_s[:].indirect(list_half(list1, h)))
+
+        x_diff = [held([P, PACK, HALF], F32, f"x_diff{h}") for h in range(HALVES)]
+        for t in range(PACK):
+            for h in range(HALVES):
+                before = ring.tile([P, HALF], F32, name="before")
+                nc.vector.tensor_copy(out=before[:], in_=x_planes[t][:].indirect(list_half(list3, h)))
+                nc.vector.tensor_tensor(
+                    out=x_diff[h][:, t, :], in0=x_planes[t][:].indirect(list_half(list2, h)), in1=before[:], op=SUBTRACT
+                )
+
+        wd_w = [held([P, PASS], U32, f"wd_w{a}") for a in range(R_PASSES)]
+        wd_s = [held([P, PASS], U8, f"wd_s{a}") for a in range(R_PASSES)]
+        for a in range(R_PASSES):
+            grouped = ring.tile([P, PACK * PASS], BF16, name="grouped", align_bytes=64, bufs=3)
+            nc.scalar.copy(
+                out=grouped[:].rearrange("p (t m j) -> p m j t", t=PACK, j=PACK),
+                in_=wd_raw[a][:].rearrange("p j (m t) -> p m j t", t=PACK),
+            )
+            nc.vector.quantize_mx(out=wd_w[a][:].bitcast(FP8X4), scales=wd_s[a][:], in_=grouped[:])
+
+        work = [[held([P, PACK, HALF], F32, f"work{h}_{a}") for a in range(R_PASSES)] for h in range(HALVES)]
+        for h in range(HALVES):
+            for a in range(R_PASSES):
+                for t in range(PACK):
+                    c = PACK * a + t
+                    bank = banks[c % 8]
+                    nc.tensor.matmul_mx(
+                        out=bank[:],
+                        lhsT=wc_w[:, 2 * P * c : 2 * P * (c + 1)].bitcast(FP4X4),
+                        lhsT_scale=wc_s[:, P * c : P * (c + 1)],
+                        rhs=v_w[h][:].bitcast(FP8X4),
+                        rhs_scale=v_s[h][:],
+                        start=True,
+                        stop=True,
+                    )
+                    nc.scalar.copy(out=work[h][a][:, t, :], in_=bank[:])
+
+        def interleave(dst, src):
+            nc.scalar.copy(
+                out=dst.rearrange("p (c i t) -> p c t i", i=4, t=PACK),
+                in_=src.rearrange("p t (c i) -> p c t i", i=4),
+            )
+
+        x_w = [held([P, HALF], U32, f"x_w{h}") for h in range(HALVES)]
+        x_s = [held([P, HALF], U8, f"x_s{h}") for h in range(HALVES)]
+        for h in range(HALVES):
+            grouped = ring.tile([P, PACK * HALF], BF16, name="grouped", align_bytes=64, bufs=3)
+            interleave(grouped[:], x_diff[h][:])
+            nc.vector.quantize_mx(out=x_w[h][:].bitcast(FP8X4), scales=x_s[h][:], in_=grouped[:])
+
+        h_w = [[held([P, HALF], U32, f"h_w{h}_{a}") for a in range(R_PASSES)] for h in range(HALVES)]
+        h_s = [[held([P, HALF], U8, f"h_s{h}_{a}") for a in range(R_PASSES)] for h in range(HALVES)]
+
+        def unit(h, a, first_bank, on_vector):
+            w = work[h][a]
+            planes = ring.tile([P, PACK, HALF], BF16, name="h_planes")
+            grouped = ring.tile([P, PACK * HALF], BF16, name="grouped", align_bytes=64, bufs=3)
+            for t in range(PACK):
+                bank = banks[first_bank + t]
+                nc.tensor.matmul_mx(
+                    out=bank[:],
+                    lhsT=wd_w[a][:, P * t : P * (t + 1)].bitcast(FP8X4),
+                    lhsT_scale=wd_s[a][:, P * t : P * (t + 1)],
+                    rhs=x_w[h][:].bitcast(FP8X4),
+                    rhs_scale=x_s[h][:],
+                    start=True,
+                    stop=True,
+                )
+                nc.vector.tensor_tensor(out=w[:, t, :], in0=bank[:], in1=w[:, t, :], op=MULT)
+                nc.scalar.activation(out=w[:, t, :], in_=w[:, t, :], func=TANH)
+            for t in range(PACK):
+                nc.vector.tensor_scalar(
+                    out=planes[:, t, :], in0=w[:, t, :], scalar1=gains[:, a, t : t + 1], scalar2=None, op0=MULT
+                )
+            interleave(grouped[:], planes[:])
+            nc.vector.quantize_mx(out=h_w[h][a][:].bitcast(FP8X4), scales=h_s[h][a][:], in_=grouped[:])
+
+        def corr_pass(h, n, a, bank):
+            nc.tensor.matmul_mx(
+                out=bank[:],
+                lhsT=wo_w[:, a, P * n : P * (n + 1)].bitcast(FP8X4),
+                lhsT_scale=wo_s[:, a, P * n : P * (n + 1)],
+                rhs=h_w[h][a][:].bitcast(FP8X4),
+                rhs_scale=h_s[h][a][:],
+                start=(a == 0),
+                stop=(a == R_PASSES - 1),
+            )
+
+        def finish(h, n, bank):
+            cols = slice(h * HALF, (h + 1) * HALF)
+            nc.vector.tensor_tensor(out=obs_sb[n][:, cols], in0=obs_sb[n][:, cols], in1=bank[:], op=SUBTRACT)
+            nc.sync.dma_start(out=out[n * P : (n + 1) * P, cols], in_=obs_sb[n][:, cols])
+
+        unit(0, 0, 0, False)
+        unit(0, 1, 4, False)
+        unit(0, 2, 0, False)
+        unit(1, 0, 4, False)
+        for n in range(4):
+            for a in range(R_PASSES):
+                corr_pass(0, n, a, banks[n])
+        unit(1, 1, 4, False)
+        for n in range(2):
+            finish(0, n, banks[n])
+            for a in range(R_PASSES):
+                corr_pass(0, 4 + n, a, banks[n])
+        unit(1, 2, 4, False)
+        for n in range(2, N_TILES):
+            finish(0, n, banks[n % 4])
+        last_banks = [2, 3, 0, 1, 4, 5]
+        for a in range(R_PASSES):
+            for n in range(N_TILES):
+                corr_pass(1, n, a, banks[last_banks[n]])
+        for n in range(N_TILES):
+            finish(1, n, banks[last_banks[n]])

@@ -14,6 +14,7 @@ U8 = mybir.dt.uint8
 FP8X4 = mybir.dt.float8_e4m3fn_x4
 FP4X4 = mybir.dt.float4_e2m1fn_x4
 MULT = mybir.AluOpType.mult
+ADD = mybir.AluOpType.add
 SUBTRACT = mybir.AluOpType.subtract
 TANH = mybir.ActivationFunctionType.Tanh
 
@@ -55,7 +56,6 @@ def tile_list_argo_cast_check_kernel(
         gains = held([P, R_PASSES, PACK], F32, "gains")
         x_planes = [held([P, T], F32, f"x_plane{t}") for t in range(PACK)]
         wd_raw = [held([P, PACK, PASS], F32, f"wd_raw{a}") for a in range(R_PASSES)]
-        obs_sb = [held([P, S], F32, f"obs{n}") for n in range(N_TILES)]
 
         nc.vector.memset(wc_s_raw[:].bitcast(I32), 0)
         nc.vector.memset(tab_s[:].bitcast(I32), 0)
@@ -83,22 +83,33 @@ def tile_list_argo_cast_check_kernel(
         def load_wd(a):
             nc.sync.dma_start(out=wd_raw[a][:], in_=wd_rows[:, :, a * PASS : (a + 1) * PASS])
 
-        load_x(0)
+        chunks = [(0, 512), (512, 256), (768, 256)]
+        obs_rows = obs.rearrange("(n p) j -> p n j", p=P)
+        out_rows = out.rearrange("(n p) j -> p n j", p=P)
+        obs_sb = {}
+        for c, (j0, width) in enumerate(chunks):
+            per_bank = HALF // width
+            for g in range(N_TILES // per_bank):
+                obs_sb[c, g] = held([P, per_bank, width], F32, f"obs{c}_{g}")
+
         load_wd(0)
-        load_x(1)
+        for t in range(PACK):
+            load_x(t)
         load_wd(1)
-        load_x(2)
-        load_x(3)
-        load_wd(2)
         nc.sync.dma_start(out=gains[:], in_=gain.rearrange("(a p t) -> p a t", p=P, t=PACK))
+        load_wd(2)
         for q in range(4):
             nc.sync.dma_start(
                 out=wo_s[32 * q : 32 * q + 4, :, :].bitcast(I32),
                 in_=wo_scales[:, 4 * q : 4 * q + 4, :].rearrange("a r n -> r a n").bitcast(I32),
             )
         nc.sync.dma_start(out=wo_w[:], in_=wo_words.rearrange("a p c i -> p a (c i)").bitcast(I32))
-        for n in range(N_TILES):
-            nc.sync.dma_start(out=obs_sb[n][:], in_=obs[n * P : (n + 1) * P, :])
+        for c, (j0, width) in enumerate(chunks):
+            per_bank = HALF // width
+            for g in range(N_TILES // per_bank):
+                nc.sync.dma_start(
+                    out=obs_sb[c, g][:], in_=obs_rows[:, g * per_bank : (g + 1) * per_bank, j0 : j0 + width]
+                )
 
         nc.vector.tensor_copy(
             out=wc_w[:].bitcast(U16).rearrange("p (a t m) -> p a t m", a=R_PASSES, t=PACK),
@@ -118,18 +129,18 @@ def tile_list_argo_cast_check_kernel(
             nc.vector.tensor_copy(out=v_w[h][:], in_=tab_w[:].bitcast(U32).indirect(list_half(list1, h)))
             nc.vector.tensor_copy(out=v_s[h][:], in_=tab_s[:].indirect(list_half(list1, h)))
 
-        x_diff = [held([P, PACK, HALF], F32, f"x_diff{h}") for h in range(HALVES)]
-        for t in range(PACK):
-            for h in range(HALVES):
+        def gather_x(h, dst):
+            for t in range(PACK):
                 before = ring.tile([P, HALF], F32, name="before")
                 nc.vector.tensor_copy(out=before[:], in_=x_planes[t][:].indirect(list_half(list3, h)))
                 nc.vector.tensor_tensor(
-                    out=x_diff[h][:, t, :], in0=x_planes[t][:].indirect(list_half(list2, h)), in1=before[:], op=SUBTRACT
+                    out=dst[:, t, :], in0=x_planes[t][:].indirect(list_half(list2, h)), in1=before[:], op=SUBTRACT
                 )
 
         wd_w = [held([P, PASS], U32, f"wd_w{a}") for a in range(R_PASSES)]
         wd_s = [held([P, PASS], U8, f"wd_s{a}") for a in range(R_PASSES)]
-        for a in range(R_PASSES):
+
+        def quantise_wd(a):
             grouped = ring.tile([P, PACK * PASS], BF16, name="grouped", align_bytes=64, bufs=3)
             nc.scalar.copy(
                 out=grouped[:].rearrange("p (t m j) -> p m j t", t=PACK, j=PACK),
@@ -137,97 +148,197 @@ def tile_list_argo_cast_check_kernel(
             )
             nc.vector.quantize_mx(out=wd_w[a][:].bitcast(FP8X4), scales=wd_s[a][:], in_=grouped[:])
 
-        work = [[held([P, PACK, HALF], F32, f"work{h}_{a}") for a in range(R_PASSES)] for h in range(HALVES)]
-        for h in range(HALVES):
-            for a in range(R_PASSES):
-                for t in range(PACK):
-                    c = PACK * a + t
-                    bank = banks[c % 8]
-                    nc.tensor.matmul_mx(
-                        out=bank[:],
-                        lhsT=wc_w[:, 2 * P * c : 2 * P * (c + 1)].bitcast(FP4X4),
-                        lhsT_scale=wc_s[:, P * c : P * (c + 1)],
-                        rhs=v_w[h][:].bitcast(FP8X4),
-                        rhs_scale=v_s[h][:],
-                        start=True,
-                        stop=True,
-                    )
-                    nc.scalar.copy(out=work[h][a][:, t, :], in_=bank[:])
+        work = [[held([P, PACK * HALF], F32, f"work{h}_{a}") for a in range(R_PASSES)] for h in range(HALVES)]
+        half_width = [512, 256]
 
-        def interleave(dst, src):
-            nc.scalar.copy(
-                out=dst.rearrange("p (c i t) -> p c t i", i=4, t=PACK),
-                in_=src.rearrange("p t (c i) -> p c t i", i=4),
-            )
+        def clim(h, a):
+            dst = work[h][a][:].rearrange("p (c t j) -> p t c j", t=PACK, j=half_width[h])
+            for t in range(PACK):
+                c = PACK * a + t
+                bank = banks[5 + c % 3]
+                nc.tensor.matmul_mx(
+                    out=bank[:],
+                    lhsT=wc_w[:, 2 * P * c : 2 * P * (c + 1)].bitcast(FP4X4),
+                    lhsT_scale=wc_s[:, P * c : P * (c + 1)],
+                    rhs=v_w[h][:].bitcast(FP8X4),
+                    rhs_scale=v_s[h][:],
+                    start=True,
+                    stop=True,
+                )
+                nc.scalar.copy(out=dst[:, t, :, :], in_=bank[:].rearrange("p (c j) -> p c j", j=half_width[h]))
+
+        def walk_out(dst):
+            return dst.rearrange("p (c i t) -> p c t i", i=4, t=PACK)
+
+        def walk_in(src):
+            return src.rearrange("p (t c i) -> p c t i", i=4, t=PACK)
+
+        def interleave(engine, dst, src):
+            if engine == "S":
+                nc.scalar.copy(out=walk_out(dst), in_=walk_in(src))
+            else:
+                nc.vector.tensor_copy(out=walk_out(dst), in_=walk_in(src))
 
         x_w = [held([P, HALF], U32, f"x_w{h}") for h in range(HALVES)]
         x_s = [held([P, HALF], U8, f"x_s{h}") for h in range(HALVES)]
-        for h in range(HALVES):
+
+        def quantise_x(h, src, engine):
             grouped = ring.tile([P, PACK * HALF], BF16, name="grouped", align_bytes=64, bufs=3)
-            interleave(grouped[:], x_diff[h][:])
+            interleave(engine, grouped[:], src)
             nc.vector.quantize_mx(out=x_w[h][:].bitcast(FP8X4), scales=x_s[h][:], in_=grouped[:])
 
         h_w = [[held([P, HALF], U32, f"h_w{h}_{a}") for a in range(R_PASSES)] for h in range(HALVES)]
         h_s = [[held([P, HALF], U8, f"h_s{h}_{a}") for a in range(R_PASSES)] for h in range(HALVES)]
 
-        def unit(h, a, first_bank, on_vector):
-            w = work[h][a]
-            planes = ring.tile([P, PACK, HALF], BF16, name="h_planes")
-            grouped = ring.tile([P, PACK * HALF], BF16, name="grouped", align_bytes=64, bufs=3)
-            for t in range(PACK):
-                bank = banks[first_bank + t]
-                nc.tensor.matmul_mx(
-                    out=bank[:],
-                    lhsT=wd_w[a][:, P * t : P * (t + 1)].bitcast(FP8X4),
-                    lhsT_scale=wd_s[a][:, P * t : P * (t + 1)],
-                    rhs=x_w[h][:].bitcast(FP8X4),
-                    rhs_scale=x_s[h][:],
-                    start=True,
-                    stop=True,
-                )
-                nc.vector.tensor_tensor(out=w[:, t, :], in0=bank[:], in1=w[:, t, :], op=MULT)
-                nc.scalar.activation(out=w[:, t, :], in_=w[:, t, :], func=TANH)
-            for t in range(PACK):
-                nc.vector.tensor_scalar(
-                    out=planes[:, t, :], in0=w[:, t, :], scalar1=gains[:, a, t : t + 1], scalar2=None, op0=MULT
-                )
-            interleave(grouped[:], planes[:])
-            nc.vector.quantize_mx(out=h_w[h][a][:].bitcast(FP8X4), scales=h_s[h][a][:], in_=grouped[:])
+        def place(c):
+            j0, width = chunks[c]
+            return j0 // HALF, j0 % HALF, width
 
-        def corr_pass(h, n, a, bank):
-            nc.tensor.matmul_mx(
-                out=bank[:],
-                lhsT=wo_w[:, a, P * n : P * (n + 1)].bitcast(FP8X4),
-                lhsT_scale=wo_s[:, a, P * n : P * (n + 1)],
-                rhs=h_w[h][a][:].bitcast(FP8X4),
-                rhs_scale=h_s[h][a][:],
-                start=(a == 0),
-                stop=(a == R_PASSES - 1),
+        def region(c, a):
+            h, o, width = place(c)
+            return work[h][a][:, PACK * o : PACK * (o + width)]
+
+        def product(c, a, drift_banks):
+            h, o, width = place(c)
+            per_bank = HALF // width
+            w = region(c, a)
+            for b, bank in enumerate(drift_banks):
+                for s in range(per_bank):
+                    t = b * per_bank + s
+                    nc.tensor.matmul_mx(
+                        out=bank[:, s * width : (s + 1) * width],
+                        lhsT=wd_w[a][:, P * t : P * (t + 1)].bitcast(FP8X4),
+                        lhsT_scale=wd_s[a][:, P * t : P * (t + 1)],
+                        rhs=x_w[h][:, o : o + width].bitcast(FP8X4),
+                        rhs_scale=x_s[h][:, o : o + width],
+                        start=True,
+                        stop=True,
+                    )
+                cols = slice(b * HALF, (b + 1) * HALF)
+                nc.vector.tensor_tensor(out=w[:, cols], in0=bank[:], in1=w[:, cols], op=MULT)
+                nc.scalar.activation(out=w[:, cols], in_=w[:, cols], func=TANH)
+
+        grouped_h = {}
+
+        def scale(c, a, mode):
+            h, o, width = place(c)
+            w = region(c, a)
+            grouped = ring.tile([P, PACK * width], BF16, name="grouped", align_bytes=64, bufs=3)
+            grouped_h[c, a] = grouped
+            if mode == "A":
+                nc.vector.tensor_tensor(
+                    out=walk_out(grouped[:]),
+                    in0=walk_in(w),
+                    in1=gains[:, a, :].unsqueeze(1).unsqueeze(3).to_broadcast([P, width // 4, PACK, 4]),
+                    op=MULT,
+                )
+                return
+            planes = ring.tile([P, PACK * width], BF16, name="h_planes")
+            for t in range(PACK):
+                cols = slice(t * width, (t + 1) * width)
+                if mode[0] == "G":
+                    nc.gpsimd.tensor_scalar(
+                        out=planes[:, cols], in0=w[:, cols], scalar1=gains[:, a, t : t + 1], scalar2=0.0, op0=MULT, op1=ADD
+                    )
+                else:
+                    nc.vector.tensor_scalar(
+                        out=planes[:, cols], in0=w[:, cols], scalar1=gains[:, a, t : t + 1], scalar2=None, op0=MULT
+                    )
+            interleave(mode[1], grouped[:], planes[:])
+
+        def quantise_h(c, a):
+            h, o, width = place(c)
+            nc.vector.quantize_mx(
+                out=h_w[h][a][:, o : o + width].bitcast(FP8X4), scales=h_s[h][a][:, o : o + width], in_=grouped_h[c, a][:]
             )
 
-        def finish(h, n, bank):
-            cols = slice(h * HALF, (h + 1) * HALF)
-            nc.vector.tensor_tensor(out=obs_sb[n][:, cols], in0=obs_sb[n][:, cols], in1=bank[:], op=SUBTRACT)
-            nc.sync.dma_start(out=out[n * P : (n + 1) * P, cols], in_=obs_sb[n][:, cols])
+        def corr_passes(c, g, a, bank):
+            h, o, width = place(c)
+            per_bank = HALF // width
+            for s in range(per_bank):
+                n = g * per_bank + s
+                nc.tensor.matmul_mx(
+                    out=bank[:, s * width : (s + 1) * width],
+                    lhsT=wo_w[:, a, P * n : P * (n + 1)].bitcast(FP8X4),
+                    lhsT_scale=wo_s[:, a, P * n : P * (n + 1)],
+                    rhs=h_w[h][a][:, o : o + width].bitcast(FP8X4),
+                    rhs_scale=h_s[h][a][:, o : o + width],
+                    start=(a == 0 and s == 0),
+                    stop=(a == R_PASSES - 1 and s == per_bank - 1),
+                )
 
-        unit(0, 0, 0, False)
-        unit(0, 1, 4, False)
-        unit(0, 2, 0, False)
-        unit(1, 0, 4, False)
-        for n in range(4):
-            for a in range(R_PASSES):
-                corr_pass(0, n, a, banks[n])
-        unit(1, 1, 4, False)
-        for n in range(2):
-            finish(0, n, banks[n])
-            for a in range(R_PASSES):
-                corr_pass(0, 4 + n, a, banks[n])
-        unit(1, 2, 4, False)
-        for n in range(2, N_TILES):
-            finish(0, n, banks[n % 4])
-        last_banks = [2, 3, 0, 1, 4, 5]
+        def finish(c, g, bank):
+            j0, width = chunks[c]
+            per_bank = HALF // width
+            tile = obs_sb[c, g]
+            flat = tile[:].rearrange("p s j -> p (s j)")
+            nc.vector.tensor_tensor(out=flat, in0=flat, in1=bank[:], op=SUBTRACT)
+            nc.sync.dma_start(out=out_rows[:, g * per_bank : (g + 1) * per_bank, j0 : j0 + width], in_=tile[:])
+
+        def pick(*idx):
+            return [banks[b] for b in idx]
+
+        x_diff = held([P, PACK, HALF], F32, "x_diff")
+        quantise_wd(0)
+        gather_x(0, x_diff)
         for a in range(R_PASSES):
-            for n in range(N_TILES):
-                corr_pass(1, n, a, banks[last_banks[n]])
-        for n in range(N_TILES):
-            finish(1, n, banks[last_banks[n]])
+            clim(0, a)
+        quantise_x(0, x_diff[:].rearrange("p t j -> p (t j)"), "V")
+        quantise_wd(1)
+        clim(1, 0)
+        clim(1, 1)
+        product(0, 0, pick(0, 1, 2, 3))
+        product(0, 1, pick(4, 0, 1, 2))
+        scale(0, 0, "GS")
+        gather_x(1, work[0][0][:].rearrange("p (t j) -> p t j", t=PACK))
+        quantise_wd(2)
+        clim(1, 2)
+        quantise_h(0, 0)
+        product(0, 2, pick(3, 4, 0, 1))
+        scale(0, 1, "GS")
+        quantise_x(1, work[0][0][:], "S")
+        quantise_h(0, 1)
+        product(1, 0, pick(4, 5))
+        scale(0, 2, "GS")
+        product(1, 1, pick(6, 7))
+        scale(1, 0, "GS")
+        quantise_h(0, 2)
+        for g in range(4):
+            for a in range(R_PASSES):
+                corr_passes(0, g, a, banks[g])
+        product(1, 2, pick(4, 5))
+        scale(1, 1, "GS")
+        quantise_h(1, 0)
+        for g in range(2):
+            finish(0, g, banks[g])
+            for a in range(R_PASSES):
+                corr_passes(0, 4 + g, a, banks[g])
+        product(2, 0, pick(6, 7))
+        scale(1, 2, "GS")
+        quantise_h(1, 1)
+        finish(0, 2, banks[2])
+        finish(0, 3, banks[3])
+        product(2, 1, pick(4, 5))
+        scale(2, 0, "GS")
+        quantise_h(1, 2)
+        finish(0, 4, banks[0])
+        for g, b in enumerate((2, 3, 0)):
+            for a in range(R_PASSES):
+                corr_passes(1, g, a, banks[b])
+        product(2, 2, pick(6, 7))
+        scale(2, 1, "GS")
+        quantise_h(2, 0)
+        finish(0, 5, banks[1])
+        finish(1, 0, banks[2])
+        scale(2, 2, "A")
+        quantise_h(2, 1)
+        for a in range(2):
+            for g, b in enumerate((4, 5, 1)):
+                corr_passes(2, g, a, banks[b])
+        finish(1, 1, banks[3])
+        quantise_h(2, 2)
+        finish(1, 2, banks[0])
+        for g, b in enumerate((4, 5, 1)):
+            corr_passes(2, g, 2, banks[b])
+        for g, b in enumerate((4, 5, 1)):
+            finish(2, g, banks[b])

@@ -93,9 +93,11 @@ def tile_list_argo_cast_check_kernel(
                 obs_sb[c, g] = held([P, per_bank, width], F32, f"obs{c}_{g}")
 
         load_wd(0)
-        for t in range(PACK):
-            load_x(t)
+        load_x(0)
+        load_x(1)
         load_wd(1)
+        load_x(2)
+        load_x(3)
         nc.sync.dma_start(out=gains[:], in_=gain.rearrange("(a p t) -> p a t", p=P, t=PACK))
         load_wd(2)
         for q in range(4):
@@ -129,12 +131,13 @@ def tile_list_argo_cast_check_kernel(
             nc.vector.tensor_copy(out=v_w[h][:], in_=tab_w[:].bitcast(U32).indirect(list_half(list1, h)))
             nc.vector.tensor_copy(out=v_s[h][:], in_=tab_s[:].indirect(list_half(list1, h)))
 
-        def gather_x(h, dst):
-            for t in range(PACK):
+        x_diff = [held([P, PACK, HALF], F32, f"x_diff{h}") for h in range(HALVES)]
+        for t in range(PACK):
+            for h in range(HALVES):
                 before = ring.tile([P, HALF], F32, name="before")
                 nc.vector.tensor_copy(out=before[:], in_=x_planes[t][:].indirect(list_half(list3, h)))
                 nc.vector.tensor_tensor(
-                    out=dst[:, t, :], in0=x_planes[t][:].indirect(list_half(list2, h)), in1=before[:], op=SUBTRACT
+                    out=x_diff[h][:, t, :], in0=x_planes[t][:].indirect(list_half(list2, h)), in1=before[:], op=SUBTRACT
                 )
 
         wd_w = [held([P, PASS], U32, f"wd_w{a}") for a in range(R_PASSES)]
@@ -149,13 +152,14 @@ def tile_list_argo_cast_check_kernel(
             nc.vector.quantize_mx(out=wd_w[a][:].bitcast(FP8X4), scales=wd_s[a][:], in_=grouped[:])
 
         work = [[held([P, PACK * HALF], F32, f"work{h}_{a}") for a in range(R_PASSES)] for h in range(HALVES)]
-        half_width = [512, 256]
+        units = [(0, 0, 0, 512), (0, 1, 0, 512), (0, 2, 0, 512), (1, 0, 0, 512), (1, 1, 0, 512), (1, 2, 0, 256), (1, 2, 256, 256)]
 
         def clim(h, a):
-            dst = work[h][a][:].rearrange("p (c t j) -> p t c j", t=PACK, j=half_width[h])
+            width = min(u[3] for u in units if u[:2] == (h, a))
+            dst = work[h][a][:].rearrange("p (c t j) -> p t c j", t=PACK, j=width)
             for t in range(PACK):
                 c = PACK * a + t
-                bank = banks[5 + c % 3]
+                bank = banks[(PACK * R_PASSES * h + c) % 8]
                 nc.tensor.matmul_mx(
                     out=bank[:],
                     lhsT=wc_w[:, 2 * P * c : 2 * P * (c + 1)].bitcast(FP4X4),
@@ -165,7 +169,7 @@ def tile_list_argo_cast_check_kernel(
                     start=True,
                     stop=True,
                 )
-                nc.scalar.copy(out=dst[:, t, :, :], in_=bank[:].rearrange("p (c j) -> p c j", j=half_width[h]))
+                nc.scalar.copy(out=dst[:, t, :, :], in_=bank[:].rearrange("p (c j) -> p c j", j=width))
 
         def walk_out(dst):
             return dst.rearrange("p (c i t) -> p c t i", i=4, t=PACK)
@@ -194,14 +198,14 @@ def tile_list_argo_cast_check_kernel(
             j0, width = chunks[c]
             return j0 // HALF, j0 % HALF, width
 
-        def region(c, a):
-            h, o, width = place(c)
+        def region(u):
+            h, a, o, width = units[u]
             return work[h][a][:, PACK * o : PACK * (o + width)]
 
-        def product(c, a, drift_banks):
-            h, o, width = place(c)
+        def product(u, drift_banks):
+            h, a, o, width = units[u]
             per_bank = HALF // width
-            w = region(c, a)
+            w = region(u)
             for b, bank in enumerate(drift_banks):
                 for s in range(per_bank):
                     t = b * per_bank + s
@@ -220,11 +224,11 @@ def tile_list_argo_cast_check_kernel(
 
         grouped_h = {}
 
-        def scale(c, a, mode):
-            h, o, width = place(c)
-            w = region(c, a)
+        def scale(u, mode):
+            h, a, o, width = units[u]
+            w = region(u)
             grouped = ring.tile([P, PACK * width], BF16, name="grouped", align_bytes=64, bufs=3)
-            grouped_h[c, a] = grouped
+            grouped_h[u] = grouped
             if mode == "A":
                 nc.vector.tensor_tensor(
                     out=walk_out(grouped[:]),
@@ -246,10 +250,10 @@ def tile_list_argo_cast_check_kernel(
                     )
             interleave(mode[1], grouped[:], planes[:])
 
-        def quantise_h(c, a):
-            h, o, width = place(c)
+        def quantise_h(u):
+            h, a, o, width = units[u]
             nc.vector.quantize_mx(
-                out=h_w[h][a][:, o : o + width].bitcast(FP8X4), scales=h_s[h][a][:, o : o + width], in_=grouped_h[c, a][:]
+                out=h_w[h][a][:, o : o + width].bitcast(FP8X4), scales=h_s[h][a][:, o : o + width], in_=grouped_h[u][:]
             )
 
         def corr_passes(c, g, a, bank):
@@ -278,67 +282,52 @@ def tile_list_argo_cast_check_kernel(
         def pick(*idx):
             return [banks[b] for b in idx]
 
-        x_diff = held([P, PACK, HALF], F32, "x_diff")
-        quantise_wd(0)
-        gather_x(0, x_diff)
         for a in range(R_PASSES):
-            clim(0, a)
-        quantise_x(0, x_diff[:].rearrange("p t j -> p (t j)"), "V")
-        quantise_wd(1)
-        clim(1, 0)
-        clim(1, 1)
-        product(0, 0, pick(0, 1, 2, 3))
-        product(0, 1, pick(4, 0, 1, 2))
-        scale(0, 0, "GS")
-        gather_x(1, work[0][0][:].rearrange("p (t j) -> p t j", t=PACK))
-        quantise_wd(2)
-        clim(1, 2)
-        quantise_h(0, 0)
-        product(0, 2, pick(3, 4, 0, 1))
-        scale(0, 1, "GS")
-        quantise_x(1, work[0][0][:], "S")
-        quantise_h(0, 1)
-        product(1, 0, pick(4, 5))
-        scale(0, 2, "GS")
-        product(1, 1, pick(6, 7))
-        scale(1, 0, "GS")
-        quantise_h(0, 2)
+            quantise_wd(a)
+        for h in range(HALVES):
+            for a in range(R_PASSES):
+                clim(h, a)
+        for h in range(HALVES):
+            quantise_x(h, x_diff[h][:].rearrange("p t j -> p (t j)"), "S")
+        product(0, pick(0, 1, 2, 3))
+        product(1, pick(4, 5, 6, 7))
+        scale(0, "A")
+        product(2, pick(0, 1, 2, 3))
+        scale(1, "GV")
+        quantise_h(0)
+        product(3, pick(4, 5, 6, 7))
+        scale(2, "GS")
+        quantise_h(1)
+        product(4, pick(4, 5, 6, 7))
+        scale(3, "GS")
+        quantise_h(2)
+        product(5, pick(4, 5))
+        product(6, pick(6, 7))
+        scale(4, "GS")
+        quantise_h(3)
         for g in range(4):
             for a in range(R_PASSES):
                 corr_passes(0, g, a, banks[g])
-        product(1, 2, pick(4, 5))
-        scale(1, 1, "GS")
-        quantise_h(1, 0)
         for g in range(2):
             finish(0, g, banks[g])
             for a in range(R_PASSES):
                 corr_passes(0, 4 + g, a, banks[g])
-        product(2, 0, pick(6, 7))
-        scale(1, 2, "GS")
-        quantise_h(1, 1)
-        finish(0, 2, banks[2])
-        finish(0, 3, banks[3])
-        product(2, 1, pick(4, 5))
-        scale(2, 0, "GS")
-        quantise_h(1, 2)
-        finish(0, 4, banks[0])
-        for g, b in enumerate((2, 3, 0)):
-            for a in range(R_PASSES):
+        scale(5, "GS")
+        quantise_h(4)
+        for g in range(2, N_TILES):
+            finish(0, g, banks[g % 4])
+        scale(6, "GS")
+        quantise_h(5)
+        for a in range(R_PASSES):
+            for g, b in enumerate((2, 3, 0)):
                 corr_passes(1, g, a, banks[b])
-        product(2, 2, pick(6, 7))
-        scale(2, 1, "GS")
-        quantise_h(2, 0)
-        finish(0, 5, banks[1])
-        finish(1, 0, banks[2])
-        scale(2, 2, "A")
-        quantise_h(2, 1)
         for a in range(2):
             for g, b in enumerate((4, 5, 1)):
                 corr_passes(2, g, a, banks[b])
-        finish(1, 1, banks[3])
-        quantise_h(2, 2)
-        finish(1, 2, banks[0])
+        quantise_h(6)
         for g, b in enumerate((4, 5, 1)):
             corr_passes(2, g, 2, banks[b])
+        for g, b in enumerate((2, 3, 0)):
+            finish(1, g, banks[b])
         for g, b in enumerate((4, 5, 1)):
             finish(2, g, banks[b])

@@ -288,22 +288,22 @@ def tile_list_argo_cast_check_kernel(
             for a in range(R_PASSES):
                 clim(h, a)
         for h in range(HALVES):
-            quantise_x(h, x_diff[h][:].rearrange("p t j -> p (t j)"), "S")
+            quantise_x(h, x_diff[h][:].rearrange("p t j -> p (t j)"), "VS"[h])
         product(0, pick(0, 1, 2, 3))
         product(1, pick(4, 5, 6, 7))
-        scale(0, "A")
+        scale(0, "VV")
         product(2, pick(0, 1, 2, 3))
-        scale(1, "GV")
+        scale(1, "VS")
         quantise_h(0)
         product(3, pick(4, 5, 6, 7))
-        scale(2, "GS")
+        scale(2, "VS")
         quantise_h(1)
         product(4, pick(4, 5, 6, 7))
-        scale(3, "GS")
+        scale(3, "VS")
         quantise_h(2)
         product(5, pick(4, 5))
         product(6, pick(6, 7))
-        scale(4, "GS")
+        scale(4, "VS")
         quantise_h(3)
         for g in range(4):
             for a in range(R_PASSES):
@@ -312,11 +312,11 @@ def tile_list_argo_cast_check_kernel(
             finish(0, g, banks[g])
             for a in range(R_PASSES):
                 corr_passes(0, 4 + g, a, banks[g])
-        scale(5, "GS")
+        scale(5, "VS")
         quantise_h(4)
         for g in range(2, N_TILES):
             finish(0, g, banks[g % 4])
-        scale(6, "GS")
+        scale(6, "VV")
         quantise_h(5)
         for a in range(R_PASSES):
             for g, b in enumerate((2, 3, 0)):

@@ -14,7 +14,6 @@ U8 = mybir.dt.uint8
 FP8X4 = mybir.dt.float8_e4m3fn_x4
 FP4X4 = mybir.dt.float4_e2m1fn_x4
 MULT = mybir.AluOpType.mult
-ADD = mybir.AluOpType.add
 SUBTRACT = mybir.AluOpType.subtract
 TANH = mybir.ActivationFunctionType.Tanh
 
@@ -23,6 +22,7 @@ PACK = 4
 PASS = P * PACK
 HALF = 512
 HALVES = S // HALF
+QUARTER = 256
 R_PASSES = H // PASS
 N_TILES = N // P
 LIST_COLS = HALF // 16
@@ -49,8 +49,8 @@ def tile_list_argo_cast_check_kernel(
         tab_s = held([P, T], U8, "tab_s")
         wc_w_raw = held([P, 2 * H], U8, "wc_w_raw")
         wc_s_raw = held([P, H], U8, "wc_s_raw")
-        wc_w = held([P, 2 * H], U8, "wc_w")
-        wc_s = held([P, H], U8, "wc_s")
+        wc_w = [held([P, 2 * PASS], U8, f"wc_w{a}") for a in range(R_PASSES)]
+        wc_s = [held([P, PASS], U8, f"wc_s{a}") for a in range(R_PASSES)]
         wo_w = held([P, R_PASSES, N], I32, "wo_w")
         wo_s = held([P, R_PASSES, N], U8, "wo_s")
         gains = held([P, R_PASSES, PACK], F32, "gains")
@@ -63,19 +63,12 @@ def tile_list_argo_cast_check_kernel(
 
         x_rows = xT.rearrange("(p t) c -> p t c", t=PACK)
         wd_rows = wd.rearrange("(p j) c -> p j c", j=PACK)
-        nc.sync.dma_start(out=list1[:], in_=offs)
-        nc.sync.dma_start(out=wc_w_raw[:].bitcast(I32), in_=wc_words[0].bitcast(I32))
-        for q in range(4):
-            nc.sync.dma_start(
-                out=wc_s_raw[32 * q : 32 * q + 4, :].bitcast(I32), in_=wc_scales[0, 4 * q : 4 * q + 4, :].bitcast(I32)
-            )
-        nc.sync.dma_start(out=tab_w[:], in_=tab_words[0].rearrange("p c i -> p (c i)").bitcast(I32))
-        for q in range(4):
-            nc.sync.dma_start(
-                out=tab_s[32 * q : 32 * q + 4, :].bitcast(I32), in_=tab_scales[0, 4 * q : 4 * q + 4, :].bitcast(I32)
-            )
-        nc.sync.dma_start(out=list3[:], in_=offs3)
-        nc.sync.dma_start(out=list2[:], in_=offs2)
+
+        def load_scale_rows(tile, rows):
+            for q in range(4):
+                nc.sync.dma_start(
+                    out=tile[32 * q : 32 * q + 4, :].bitcast(I32), in_=rows[4 * q : 4 * q + 4, :].bitcast(I32)
+                )
 
         def load_x(t):
             nc.sync.dma_start(out=x_planes[t][:], in_=x_rows[:, t, :])
@@ -83,23 +76,30 @@ def tile_list_argo_cast_check_kernel(
         def load_wd(a):
             nc.sync.dma_start(out=wd_raw[a][:], in_=wd_rows[:, :, a * PASS : (a + 1) * PASS])
 
-        chunks = [(0, 512), (512, 256), (768, 256)]
+        chunks = [(0, 256), (256, 256), (512, 256), (768, 256)]
         obs_rows = obs.rearrange("(n p) j -> p n j", p=P)
         out_rows = out.rearrange("(n p) j -> p n j", p=P)
         obs_sb = {}
         for c, (j0, width) in enumerate(chunks):
             per_bank = HALF // width
-            for g in range(N_TILES // per_bank):
-                obs_sb[c, g] = held([P, per_bank, width], F32, f"obs{c}_{g}")
+            for g, n0 in enumerate(range(0, N_TILES, per_bank)):
+                obs_sb[c, g] = held([P, min(per_bank, N_TILES - n0), width], F32, f"obs{c}_{g}")
 
-        load_wd(0)
+        nc.sync.dma_start(out=wc_w_raw[:].bitcast(I32), in_=wc_words[0].bitcast(I32))
+        load_scale_rows(wc_s_raw, wc_scales[0])
+        nc.sync.dma_start(out=tab_w[:], in_=tab_words[0].rearrange("p c i -> p (c i)").bitcast(I32))
+        load_scale_rows(tab_s, tab_scales[0])
+        nc.sync.dma_start(out=list1[:], in_=offs)
+        nc.sync.dma_start(out=list3[:], in_=offs3)
+        nc.sync.dma_start(out=list2[:], in_=offs2)
         load_x(0)
         load_x(1)
-        load_wd(1)
+        load_wd(0)
         load_x(2)
+        load_wd(1)
+        load_wd(2)
         load_x(3)
         nc.sync.dma_start(out=gains[:], in_=gain.rearrange("(a p t) -> p a t", p=P, t=PACK))
-        load_wd(2)
         for q in range(4):
             nc.sync.dma_start(
                 out=wo_s[32 * q : 32 * q + 4, :, :].bitcast(I32),
@@ -108,36 +108,45 @@ def tile_list_argo_cast_check_kernel(
         nc.sync.dma_start(out=wo_w[:], in_=wo_words.rearrange("a p c i -> p a (c i)").bitcast(I32))
         for c, (j0, width) in enumerate(chunks):
             per_bank = HALF // width
-            for g in range(N_TILES // per_bank):
+            for g, n0 in enumerate(range(0, N_TILES, per_bank)):
                 nc.sync.dma_start(
-                    out=obs_sb[c, g][:], in_=obs_rows[:, g * per_bank : (g + 1) * per_bank, j0 : j0 + width]
+                    out=obs_sb[c, g][:], in_=obs_rows[:, n0 : min(n0 + per_bank, N_TILES), j0 : j0 + width]
                 )
 
-        nc.vector.tensor_copy(
-            out=wc_w[:].bitcast(U16).rearrange("p (a t m) -> p a t m", a=R_PASSES, t=PACK),
-            in_=wc_w_raw[:].bitcast(U16).rearrange("p (a m t) -> p a t m", a=R_PASSES, t=PACK),
-        )
-        nc.vector.tensor_copy(
-            out=wc_s[:].rearrange("p (a t m) -> p a t m", a=R_PASSES, t=PACK),
-            in_=wc_s_raw[:].rearrange("p (a m t) -> p a t m", a=R_PASSES, t=PACK),
-        )
+        def deal_wc(a):
+            nc.vector.tensor_copy(
+                out=wc_w[a][:].bitcast(U16).rearrange("p (t m) -> p t m", t=PACK),
+                in_=wc_w_raw[:, 2 * PASS * a : 2 * PASS * (a + 1)].bitcast(U16).rearrange("p (m t) -> p t m", t=PACK),
+            )
+            nc.vector.tensor_copy(
+                out=wc_s[a][:].rearrange("p (t m) -> p t m", t=PACK),
+                in_=wc_s_raw[:, PASS * a : PASS * (a + 1)].rearrange("p (m t) -> p t m", t=PACK),
+            )
 
         def list_half(lst, h):
             return lst[:, h * LIST_COLS : (h + 1) * LIST_COLS]
 
         v_w = [held([P, HALF], U32, f"v_w{h}") for h in range(HALVES)]
         v_s = [held([P, HALF], U8, f"v_s{h}") for h in range(HALVES)]
+        for a in range(R_PASSES):
+            deal_wc(a)
         for h in range(HALVES):
             nc.vector.tensor_copy(out=v_w[h][:], in_=tab_w[:].bitcast(U32).indirect(list_half(list1, h)))
             nc.vector.tensor_copy(out=v_s[h][:], in_=tab_s[:].indirect(list_half(list1, h)))
 
         x_diff = [held([P, PACK, HALF], F32, f"x_diff{h}") for h in range(HALVES)]
         for t in range(PACK):
+            befores = []
             for h in range(HALVES):
                 before = ring.tile([P, HALF], F32, name="before")
                 nc.vector.tensor_copy(out=before[:], in_=x_planes[t][:].indirect(list_half(list3, h)))
+                befores.append(before)
+            for h in range(HALVES):
                 nc.vector.tensor_tensor(
-                    out=x_diff[h][:, t, :], in0=x_planes[t][:].indirect(list_half(list2, h)), in1=before[:], op=SUBTRACT
+                    out=x_diff[h][:, t, :],
+                    in0=x_planes[t][:].indirect(list_half(list2, h)),
+                    in1=befores[h][:],
+                    op=SUBTRACT,
                 )
 
         wd_w = [held([P, PASS], U32, f"wd_w{a}") for a in range(R_PASSES)]
@@ -152,24 +161,33 @@ def tile_list_argo_cast_check_kernel(
             nc.vector.quantize_mx(out=wd_w[a][:].bitcast(FP8X4), scales=wd_s[a][:], in_=grouped[:])
 
         work = [[held([P, PACK * HALF], F32, f"work{h}_{a}") for a in range(R_PASSES)] for h in range(HALVES)]
-        units = [(0, 0, 0, 512), (0, 1, 0, 512), (0, 2, 0, 512), (1, 0, 0, 512), (1, 1, 0, 512), (1, 2, 0, 256), (1, 2, 256, 256)]
+        units = [(j0 // HALF, a, j0 % HALF, width) for j0, width in chunks for a in range(R_PASSES)]
 
         def clim(h, a):
-            width = min(u[3] for u in units if u[:2] == (h, a))
-            dst = work[h][a][:].rearrange("p (c t j) -> p t c j", t=PACK, j=width)
+            runs = []
+            for j0, width in chunks:
+                if j0 // HALF == h:
+                    if runs and runs[-1][1] == width:
+                        runs[-1] = (runs[-1][0], width, runs[-1][2] + width)
+                    else:
+                        runs.append((j0 % HALF, width, width))
             for t in range(PACK):
                 c = PACK * a + t
                 bank = banks[(PACK * R_PASSES * h + c) % 8]
                 nc.tensor.matmul_mx(
                     out=bank[:],
-                    lhsT=wc_w[:, 2 * P * c : 2 * P * (c + 1)].bitcast(FP4X4),
-                    lhsT_scale=wc_s[:, P * c : P * (c + 1)],
+                    lhsT=wc_w[a][:, 2 * P * t : 2 * P * (t + 1)].bitcast(FP4X4),
+                    lhsT_scale=wc_s[a][:, P * t : P * (t + 1)],
                     rhs=v_w[h][:].bitcast(FP8X4),
                     rhs_scale=v_s[h][:],
                     start=True,
                     stop=True,
                 )
-                nc.scalar.copy(out=dst[:, t, :, :], in_=bank[:].rearrange("p (c j) -> p c j", j=width))
+                for o, width, total in runs:
+                    dst = work[h][a][:, PACK * o : PACK * (o + total)].rearrange("p (c t j) -> p t c j", t=PACK, j=width)
+                    nc.scalar.copy(
+                        out=dst[:, t, :, :], in_=bank[:, o : o + total].rearrange("p (c j) -> p c j", j=width)
+                    )
 
         def walk_out(dst):
             return dst.rearrange("p (c i t) -> p c t i", i=4, t=PACK)
@@ -177,19 +195,42 @@ def tile_list_argo_cast_check_kernel(
         def walk_in(src):
             return src.rearrange("p (t c i) -> p c t i", i=4, t=PACK)
 
-        def interleave(engine, dst, src):
+        def interleave(engine, dst, src, width):
             if engine == "S":
                 nc.scalar.copy(out=walk_out(dst), in_=walk_in(src))
-            else:
-                nc.vector.tensor_copy(out=walk_out(dst), in_=walk_in(src))
+                return
+            half = width // 2
+            planes = src.rearrange("p (t j) -> p t j", t=PACK)
+            for s in range(2):
+                nc.vector.tensor_copy(
+                    out=walk_out(dst[:, PACK * half * s : PACK * half * (s + 1)]),
+                    in_=planes[:, :, half * s : half * (s + 1)].rearrange("p t (c i) -> p c t i", i=4),
+                )
+
+        def quantise(engine, words, scales, grouped, width):
+            parts = 1 if engine == "S" else 2
+            part = width // parts
+            for s in range(parts):
+                nc.vector.quantize_mx(
+                    out=words[:, part * s : part * (s + 1)].bitcast(FP8X4),
+                    scales=scales[:, part * s : part * (s + 1)],
+                    in_=grouped[:, PACK * part * s : PACK * part * (s + 1)],
+                )
 
         x_w = [held([P, HALF], U32, f"x_w{h}") for h in range(HALVES)]
         x_s = [held([P, HALF], U8, f"x_s{h}") for h in range(HALVES)]
 
-        def quantise_x(h, src, engine):
-            grouped = ring.tile([P, PACK * HALF], BF16, name="grouped", align_bytes=64, bufs=3)
-            interleave(engine, grouped[:], src)
-            nc.vector.quantize_mx(out=x_w[h][:].bitcast(FP8X4), scales=x_s[h][:], in_=grouped[:])
+        def quantise_x(q, engine):
+            h, o = divmod(q * QUARTER, HALF)
+            grouped = ring.tile([P, PACK * QUARTER], BF16, name="grouped_x", align_bytes=64, bufs=4)
+            src = x_diff[h][:, :, o : o + QUARTER].rearrange("p t (c i) -> p c t i", i=4)
+            if engine == "S":
+                nc.scalar.copy(out=walk_out(grouped[:]), in_=src)
+            else:
+                nc.vector.tensor_copy(out=walk_out(grouped[:]), in_=src)
+            return lambda: nc.vector.quantize_mx(
+                out=x_w[h][:, o : o + QUARTER].bitcast(FP8X4), scales=x_s[h][:, o : o + QUARTER], in_=grouped[:]
+            )
 
         h_w = [[held([P, HALF], U32, f"h_w{h}_{a}") for a in range(R_PASSES)] for h in range(HALVES)]
         h_s = [[held([P, HALF], U8, f"h_s{h}_{a}") for a in range(R_PASSES)] for h in range(HALVES)]
@@ -224,42 +265,29 @@ def tile_list_argo_cast_check_kernel(
 
         grouped_h = {}
 
-        def scale(u, mode):
+        def scale(u, engine):
             h, a, o, width = units[u]
             w = region(u)
             grouped = ring.tile([P, PACK * width], BF16, name="grouped", align_bytes=64, bufs=3)
-            grouped_h[u] = grouped
-            if mode == "A":
-                nc.vector.tensor_tensor(
-                    out=walk_out(grouped[:]),
-                    in0=walk_in(w),
-                    in1=gains[:, a, :].unsqueeze(1).unsqueeze(3).to_broadcast([P, width // 4, PACK, 4]),
-                    op=MULT,
-                )
-                return
-            planes = ring.tile([P, PACK * width], BF16, name="h_planes")
+            grouped_h[u] = (grouped, engine)
+            planes = ring.tile([P, PACK * width], BF16, name="h_planes", bufs=2)
             for t in range(PACK):
                 cols = slice(t * width, (t + 1) * width)
-                if mode[0] == "G":
-                    nc.gpsimd.tensor_scalar(
-                        out=planes[:, cols], in0=w[:, cols], scalar1=gains[:, a, t : t + 1], scalar2=0.0, op0=MULT, op1=ADD
-                    )
-                else:
-                    nc.vector.tensor_scalar(
-                        out=planes[:, cols], in0=w[:, cols], scalar1=gains[:, a, t : t + 1], scalar2=None, op0=MULT
-                    )
-            interleave(mode[1], grouped[:], planes[:])
+                nc.vector.tensor_scalar(
+                    out=planes[:, cols], in0=w[:, cols], scalar1=gains[:, a, t : t + 1], scalar2=None, op0=MULT
+                )
+            interleave(engine, grouped[:], planes[:], width)
 
         def quantise_h(u):
             h, a, o, width = units[u]
-            nc.vector.quantize_mx(
-                out=h_w[h][a][:, o : o + width].bitcast(FP8X4), scales=h_s[h][a][:, o : o + width], in_=grouped_h[u][:]
-            )
+            grouped, engine = grouped_h[u]
+            quantise(engine, h_w[h][a][:, o : o + width], h_s[h][a][:, o : o + width], grouped[:], width)
 
         def corr_passes(c, g, a, bank):
             h, o, width = place(c)
             per_bank = HALF // width
-            for s in range(per_bank):
+            count = min(per_bank, N_TILES - g * per_bank)
+            for s in range(count):
                 n = g * per_bank + s
                 nc.tensor.matmul_mx(
                     out=bank[:, s * width : (s + 1) * width],
@@ -268,7 +296,7 @@ def tile_list_argo_cast_check_kernel(
                     rhs=h_w[h][a][:, o : o + width].bitcast(FP8X4),
                     rhs_scale=h_s[h][a][:, o : o + width],
                     start=(a == 0 and s == 0),
-                    stop=(a == R_PASSES - 1 and s == per_bank - 1),
+                    stop=(a == R_PASSES - 1 and s == count - 1),
                 )
 
         def finish(c, g, bank):
@@ -276,58 +304,70 @@ def tile_list_argo_cast_check_kernel(
             per_bank = HALF // width
             tile = obs_sb[c, g]
             flat = tile[:].rearrange("p s j -> p (s j)")
-            nc.vector.tensor_tensor(out=flat, in0=flat, in1=bank[:], op=SUBTRACT)
-            nc.sync.dma_start(out=out_rows[:, g * per_bank : (g + 1) * per_bank, j0 : j0 + width], in_=tile[:])
+            count = min(per_bank, N_TILES - g * per_bank)
+            nc.vector.tensor_tensor(out=flat, in0=flat, in1=bank[:, : count * width], op=SUBTRACT)
+            nc.sync.dma_start(out=out_rows[:, g * per_bank : g * per_bank + count, j0 : j0 + width], in_=tile[:])
 
         def pick(*idx):
             return [banks[b] for b in idx]
 
         for a in range(R_PASSES):
-            quantise_wd(a)
-        for h in range(HALVES):
+            clim(0, a)
+        quantise_wd(0)
+        clim(1, 0)
+        quantise_wd(1)
+        clim(1, 1)
+        quantise_wd(2)
+        clim(1, 2)
+        later = [quantise_x(q, "VVSS"[q]) for q in range(4)]
+        for f in later:
+            f()
+
+        engines = "SSSSSSSSSSSS"
+        last = len(chunks) - 1
+        drift_banks = []
+        turn = 0
+        for h, a, o, width in units:
+            need = width // P
+            if need == PACK:
+                drift_banks.append(pick(*range(turn % 2 * 4, turn % 2 * 4 + 4)))
+            else:
+                drift_banks.append(pick(*range(4 + turn % 2 * 2, 4 + turn % 2 * 2 + need)))
+            turn += 1
+        pending = []
+        used = 0
+        last_banks = None
+        for step in range(len(units) + 2):
+            if step < len(units):
+                product(step, drift_banks[step])
+            for k in range(1):
+                if pending and step < len(units) + 0:
+                    c, g, bank = pending.pop(0)
+                    for a in range(R_PASSES):
+                        corr_passes(c, g, a, bank)
+                    finish(c, g, bank)
+            if 1 <= step <= len(units):
+                scale(step - 1, engines[step - 1])
+            if step >= 2:
+                u = step - 2
+                quantise_h(u)
+                c, a = divmod(u, R_PASSES)
+                if a == R_PASSES - 1 and c < last:
+                    per_bank = HALF // chunks[c][1]
+                    for g in range(-(-N_TILES // per_bank)):
+                        pending.append((c, g, banks[used % 4]))
+                        used += 1
+        for c, g, bank in pending:
             for a in range(R_PASSES):
-                clim(h, a)
-        for h in range(HALVES):
-            quantise_x(h, x_diff[h][:].rearrange("p t j -> p (t j)"), "VS"[h])
-        product(0, pick(0, 1, 2, 3))
-        product(1, pick(4, 5, 6, 7))
-        scale(0, "VV")
-        product(2, pick(0, 1, 2, 3))
-        scale(1, "VS")
-        quantise_h(0)
-        product(3, pick(4, 5, 6, 7))
-        scale(2, "VS")
-        quantise_h(1)
-        product(4, pick(4, 5, 6, 7))
-        scale(3, "VS")
-        quantise_h(2)
-        product(5, pick(4, 5))
-        product(6, pick(6, 7))
-        scale(4, "VS")
-        quantise_h(3)
-        for g in range(4):
-            for a in range(R_PASSES):
-                corr_passes(0, g, a, banks[g])
-        for g in range(2):
-            finish(0, g, banks[g])
-            for a in range(R_PASSES):
-                corr_passes(0, 4 + g, a, banks[g])
-        scale(5, "VS")
-        quantise_h(4)
-        for g in range(2, N_TILES):
-            finish(0, g, banks[g % 4])
-        scale(6, "VV")
-        quantise_h(5)
+                corr_passes(c, g, a, bank)
+        groups = -(-N_TILES // (HALF // chunks[last][1]))
+        free = drift_banks[-2][0]
+        first = banks.index(free)
+        last_banks = [banks[used % 4], banks[first], banks[first + 1]][-groups:]
         for a in range(R_PASSES):
-            for g, b in enumerate((2, 3, 0)):
-                corr_passes(1, g, a, banks[b])
-        for a in range(2):
-            for g, b in enumerate((4, 5, 1)):
-                corr_passes(2, g, a, banks[b])
-        quantise_h(6)
-        for g, b in enumerate((4, 5, 1)):
-            corr_passes(2, g, 2, banks[b])
-        for g, b in enumerate((2, 3, 0)):
-            finish(1, g, banks[b])
-        for g, b in enumerate((4, 5, 1)):
-            finish(2, g, banks[b])
+            for g in range(groups):
+                corr_passes(last, g, a, last_banks[g])
+        for c, g, bank in pending:
+            finish(c, g, bank)
+        for g in range(groups):
+            finish(last, g, last_banks[g])

@@ -15,6 +15,7 @@ FP8X4 = mybir.dt.float8_e4m3fn_x4
 FP4X4 = mybir.dt.float4_e2m1fn_x4
 MULT = mybir.AluOpType.mult
 SUBTRACT = mybir.AluOpType.subtract
+COPY = mybir.ActivationFunctionType.Copy
 TANH = mybir.ActivationFunctionType.Tanh
 
 P = 128
@@ -195,28 +196,6 @@ def tile_list_argo_cast_check_kernel(
         def walk_in(src):
             return src.rearrange("p (t c i) -> p c t i", i=4, t=PACK)
 
-        def interleave(engine, dst, src, width):
-            if engine == "S":
-                nc.scalar.copy(out=walk_out(dst), in_=walk_in(src))
-                return
-            half = width // 2
-            planes = src.rearrange("p (t j) -> p t j", t=PACK)
-            for s in range(2):
-                nc.vector.tensor_copy(
-                    out=walk_out(dst[:, PACK * half * s : PACK * half * (s + 1)]),
-                    in_=planes[:, :, half * s : half * (s + 1)].rearrange("p t (c i) -> p c t i", i=4),
-                )
-
-        def quantise(engine, words, scales, grouped, width):
-            parts = 1 if engine == "S" else 2
-            part = width // parts
-            for s in range(parts):
-                nc.vector.quantize_mx(
-                    out=words[:, part * s : part * (s + 1)].bitcast(FP8X4),
-                    scales=scales[:, part * s : part * (s + 1)],
-                    in_=grouped[:, PACK * part * s : PACK * part * (s + 1)],
-                )
-
         x_w = [held([P, HALF], U32, f"x_w{h}") for h in range(HALVES)]
         x_s = [held([P, HALF], U8, f"x_s{h}") for h in range(HALVES)]
 
@@ -273,15 +252,23 @@ def tile_list_argo_cast_check_kernel(
             planes = ring.tile([P, PACK * width], BF16, name="h_planes", bufs=2)
             for t in range(PACK):
                 cols = slice(t * width, (t + 1) * width)
-                nc.vector.tensor_scalar(
-                    out=planes[:, cols], in0=w[:, cols], scalar1=gains[:, a, t : t + 1], scalar2=None, op0=MULT
-                )
-            interleave(engine, grouped[:], planes[:], width)
+                if engine == "V":
+                    nc.scalar.activation(out=planes[:, cols], in_=w[:, cols], func=COPY, scale=gains[:, a, t : t + 1])
+                else:
+                    nc.vector.tensor_scalar(
+                        out=planes[:, cols], in0=w[:, cols], scalar1=gains[:, a, t : t + 1], scalar2=None, op0=MULT
+                    )
+            if engine == "V":
+                nc.vector.tensor_copy(out=walk_out(grouped[:]), in_=walk_in(planes[:]))
+            else:
+                nc.scalar.copy(out=walk_out(grouped[:]), in_=walk_in(planes[:]))
 
         def quantise_h(u):
             h, a, o, width = units[u]
             grouped, engine = grouped_h[u]
-            quantise(engine, h_w[h][a][:, o : o + width], h_s[h][a][:, o : o + width], grouped[:], width)
+            nc.vector.quantize_mx(
+                out=h_w[h][a][:, o : o + width].bitcast(FP8X4), scales=h_s[h][a][:, o : o + width], in_=grouped[:]
+            )
 
         def corr_passes(c, g, a, bank):
             h, o, width = place(c)
@@ -323,7 +310,7 @@ def tile_list_argo_cast_check_kernel(
         for f in later:
             f()
 
-        engines = "SSSSSSSSSSSS"
+        engines = "VVVVVVVVVVVV"
         last = len(chunks) - 1
         drift_banks = []
         turn = 0

@@ -14,6 +14,7 @@ U8 = mybir.dt.uint8
 FP8X4 = mybir.dt.float8_e4m3fn_x4
 FP4X4 = mybir.dt.float4_e2m1fn_x4
 MULT = mybir.AluOpType.mult
+ADD = mybir.AluOpType.add
 SUBTRACT = mybir.AluOpType.subtract
 COPY = mybir.ActivationFunctionType.Copy
 TANH = mybir.ActivationFunctionType.Tanh
@@ -55,7 +56,7 @@ def tile_list_argo_cast_check_kernel(
         wo_w = held([P, R_PASSES, N], I32, "wo_w")
         wo_s = held([P, R_PASSES, N], U8, "wo_s")
         gains = held([P, R_PASSES, PACK], F32, "gains")
-        x_planes = [held([P, T], F32, f"x_plane{t}") for t in range(PACK)]
+        x_planes = [keep.tile([P, T], F32, name="big", bufs=PACK, align_bytes=64) for t in range(PACK)]
         wd_raw = [held([P, PACK, PASS], F32, f"wd_raw{a}") for a in range(R_PASSES)]
 
         nc.vector.memset(wc_s_raw[:].bitcast(I32), 0)
@@ -80,12 +81,6 @@ def tile_list_argo_cast_check_kernel(
         chunks = [(0, 256), (256, 256), (512, 256), (768, 256)]
         obs_rows = obs.rearrange("(n p) j -> p n j", p=P)
         out_rows = out.rearrange("(n p) j -> p n j", p=P)
-        obs_sb = {}
-        for c, (j0, width) in enumerate(chunks):
-            per_bank = HALF // width
-            for g, n0 in enumerate(range(0, N_TILES, per_bank)):
-                obs_sb[c, g] = held([P, min(per_bank, N_TILES - n0), width], F32, f"obs{c}_{g}")
-
         nc.sync.dma_start(out=wc_w_raw[:].bitcast(I32), in_=wc_words[0].bitcast(I32))
         load_scale_rows(wc_s_raw, wc_scales[0])
         nc.sync.dma_start(out=tab_w[:], in_=tab_words[0].rearrange("p c i -> p (c i)").bitcast(I32))
@@ -107,12 +102,6 @@ def tile_list_argo_cast_check_kernel(
                 in_=wo_scales[:, 4 * q : 4 * q + 4, :].rearrange("a r n -> r a n").bitcast(I32),
             )
         nc.sync.dma_start(out=wo_w[:], in_=wo_words.rearrange("a p c i -> p a (c i)").bitcast(I32))
-        for c, (j0, width) in enumerate(chunks):
-            per_bank = HALF // width
-            for g, n0 in enumerate(range(0, N_TILES, per_bank)):
-                nc.sync.dma_start(
-                    out=obs_sb[c, g][:], in_=obs_rows[:, n0 : min(n0 + per_bank, N_TILES), j0 : j0 + width]
-                )
 
         def deal_wc(a):
             nc.vector.tensor_copy(
@@ -136,19 +125,31 @@ def tile_list_argo_cast_check_kernel(
             nc.vector.tensor_copy(out=v_s[h][:], in_=tab_s[:].indirect(list_half(list1, h)))
 
         x_diff = [held([P, PACK, HALF], F32, f"x_diff{h}") for h in range(HALVES)]
+        befores = {}
+
+        def pick_before(t, h, slot):
+            befores[t, h] = keep.tile([P, HALF], F32, name=f"before{slot}")
+            nc.vector.tensor_copy(out=befores[t, h][:], in_=x_planes[t][:].indirect(list_half(list3, h)))
+
+        def pick_diff(t, h):
+            nc.vector.tensor_tensor(
+                out=x_diff[h][:, t, :],
+                in0=x_planes[t][:].indirect(list_half(list2, h)),
+                in1=befores[t, h][:],
+                op=SUBTRACT,
+            )
+
         for t in range(PACK):
-            befores = []
             for h in range(HALVES):
-                before = ring.tile([P, HALF], F32, name="before")
-                nc.vector.tensor_copy(out=before[:], in_=x_planes[t][:].indirect(list_half(list3, h)))
-                befores.append(before)
+                pick_before(t, h, h)
             for h in range(HALVES):
-                nc.vector.tensor_tensor(
-                    out=x_diff[h][:, t, :],
-                    in0=x_planes[t][:].indirect(list_half(list2, h)),
-                    in1=befores[h][:],
-                    op=SUBTRACT,
-                )
+                pick_diff(t, h)
+
+        obs_sb = []
+        for g in range(N_TILES // 2):
+            obs_pair = keep.tile([P, 2, S], F32, name="big", bufs=PACK, align_bytes=64)
+            nc.sync.dma_start(out=obs_pair[:], in_=obs_rows[:, 2 * g : 2 * g + 2, :])
+            obs_sb.append(obs_pair)
 
         wd_w = [held([P, PASS], U32, f"wd_w{a}") for a in range(R_PASSES)]
         wd_s = [held([P, PASS], U8, f"wd_s{a}") for a in range(R_PASSES)]
@@ -174,7 +175,7 @@ def tile_list_argo_cast_check_kernel(
                         runs.append((j0 % HALF, width, width))
             for t in range(PACK):
                 c = PACK * a + t
-                bank = banks[(PACK * R_PASSES * h + c) % 8]
+                bank = banks[(PACK * R_PASSES * h + c + PACK) % 8]
                 nc.tensor.matmul_mx(
                     out=bank[:],
                     lhsT=wc_w[a][:, 2 * P * t : 2 * P * (t + 1)].bitcast(FP4X4),
@@ -201,9 +202,18 @@ def tile_list_argo_cast_check_kernel(
 
         def quantise_x(q, engine):
             h, o = divmod(q * QUARTER, HALF)
-            grouped = ring.tile([P, PACK * QUARTER], BF16, name="grouped_x", align_bytes=64, bufs=4)
+            grouped = ring.tile([P, PACK * QUARTER], BF16, name="grouped_x", align_bytes=64, bufs=2)
             src = x_diff[h][:, :, o : o + QUARTER].rearrange("p t (c i) -> p c t i", i=4)
-            if engine == "S":
+            if engine == "G":
+                nc.gpsimd.tensor_scalar(
+                    out=grouped[:].rearrange("p (j t) -> p j t", t=PACK),
+                    in0=x_diff[h][:, :, o : o + QUARTER].rearrange("p t j -> p j t"),
+                    scalar1=1.0,
+                    scalar2=0.0,
+                    op0=MULT,
+                    op1=ADD,
+                )
+            elif engine == "S":
                 nc.scalar.copy(out=walk_out(grouped[:]), in_=src)
             else:
                 nc.vector.tensor_copy(out=walk_out(grouped[:]), in_=src)
@@ -222,10 +232,14 @@ def tile_list_argo_cast_check_kernel(
             h, a, o, width = units[u]
             return work[h][a][:, PACK * o : PACK * (o + width)]
 
+        zs = {}
+
         def product(u, drift_banks):
             h, a, o, width = units[u]
             per_bank = HALF // width
             w = region(u)
+            z = ring.tile([P, PACK * width], F32, name="z", bufs=2)
+            zs[u] = z
             for b, bank in enumerate(drift_banks):
                 for s in range(per_bank):
                     t = b * per_bank + s
@@ -239,27 +253,39 @@ def tile_list_argo_cast_check_kernel(
                         stop=True,
                     )
                 cols = slice(b * HALF, (b + 1) * HALF)
-                nc.vector.tensor_tensor(out=w[:, cols], in0=bank[:], in1=w[:, cols], op=MULT)
-                nc.scalar.activation(out=w[:, cols], in_=w[:, cols], func=TANH)
+                nc.vector.tensor_tensor(out=z[:, cols], in0=bank[:], in1=w[:, cols], op=MULT)
+                nc.scalar.activation(out=z[:, cols], in_=z[:, cols], func=TANH)
 
         grouped_h = {}
 
         def scale(u, engine):
             h, a, o, width = units[u]
-            w = region(u)
-            grouped = ring.tile([P, PACK * width], BF16, name="grouped", align_bytes=64, bufs=3)
+            w = zs[u]
+            if engine == "G":
+                grouped = ring.tile([P, PACK * width], BF16, name="grouped_g", align_bytes=64, bufs=2)
+            else:
+                grouped = ring.tile([P, PACK * width], BF16, name="grouped_h", align_bytes=64, bufs=2)
             grouped_h[u] = (grouped, engine)
-            planes = ring.tile([P, PACK * width], BF16, name="h_planes", bufs=2)
+            planes = ring.tile([P, PACK * width], BF16, name="h_planes", bufs=3)
             for t in range(PACK):
                 cols = slice(t * width, (t + 1) * width)
-                if engine == "V":
+                if engine in "VGT":
                     nc.scalar.activation(out=planes[:, cols], in_=w[:, cols], func=COPY, scale=gains[:, a, t : t + 1])
                 else:
                     nc.vector.tensor_scalar(
                         out=planes[:, cols], in0=w[:, cols], scalar1=gains[:, a, t : t + 1], scalar2=None, op0=MULT
                     )
-            if engine == "V":
+            if engine in "VW":
                 nc.vector.tensor_copy(out=walk_out(grouped[:]), in_=walk_in(planes[:]))
+            elif engine == "G":
+                nc.gpsimd.tensor_scalar(
+                    out=grouped[:].rearrange("p (j t) -> p j t", t=PACK),
+                    in0=planes[:].rearrange("p (t j) -> p j t", t=PACK),
+                    scalar1=1.0,
+                    scalar2=0.0,
+                    op0=MULT,
+                    op1=ADD,
+                )
             else:
                 nc.scalar.copy(out=walk_out(grouped[:]), in_=walk_in(planes[:]))
 
@@ -289,11 +315,11 @@ def tile_list_argo_cast_check_kernel(
         def finish(c, g, bank):
             j0, width = chunks[c]
             per_bank = HALF // width
-            tile = obs_sb[c, g]
-            flat = tile[:].rearrange("p s j -> p (s j)")
-            count = min(per_bank, N_TILES - g * per_bank)
-            nc.vector.tensor_tensor(out=flat, in0=flat, in1=bank[:, : count * width], op=SUBTRACT)
-            nc.sync.dma_start(out=out_rows[:, g * per_bank : g * per_bank + count, j0 : j0 + width], in_=tile[:])
+            part = obs_sb[g][:, :, j0 : j0 + width]
+            nc.vector.tensor_tensor(
+                out=part, in0=part, in1=bank[:].rearrange("p (s j) -> p s j", j=width), op=SUBTRACT
+            )
+            nc.sync.dma_start(out=out_rows[:, 2 * g : 2 * g + 2, j0 : j0 + width], in_=part)
 
         def pick(*idx):
             return [banks[b] for b in idx]
@@ -306,11 +332,11 @@ def tile_list_argo_cast_check_kernel(
         clim(1, 1)
         quantise_wd(2)
         clim(1, 2)
-        later = [quantise_x(q, "VVSS"[q]) for q in range(4)]
-        for f in later:
-            f()
+        first = [quantise_x(q, "S") for q in range(2)]
+        first[0]()
+        later = []
 
-        engines = "VVVVVVVVVVVV"
+        engines = "GGGGGGGGGGGV"
         last = len(chunks) - 1
         drift_banks = []
         turn = 0
@@ -327,14 +353,22 @@ def tile_list_argo_cast_check_kernel(
         for step in range(len(units) + 2):
             if step < len(units):
                 product(step, drift_banks[step])
+            if step == 0:
+                first[1]()
+            if step == 0:
+                later = [quantise_x(q, "V") for q in (2, 3)]
+            if step == 2:
+                later[0]()
+            if step == 2:
+                later[1]()
             for k in range(1):
                 if pending and step < len(units) + 0:
                     c, g, bank = pending.pop(0)
                     for a in range(R_PASSES):
                         corr_passes(c, g, a, bank)
                     finish(c, g, bank)
-            if 1 <= step <= len(units):
-                scale(step - 1, engines[step - 1])
+            if step < len(units):
+                scale(step, engines[step])
             if step >= 2:
                 u = step - 2
                 quantise_h(u)

@@ -83,9 +83,9 @@ def tile_list_argo_cast_check_kernel(
         out_rows = out.rearrange("(n p) j -> p n j", p=P)
         nc.sync.dma_start(out=wc_w_raw[:].bitcast(I32), in_=wc_words[0].bitcast(I32))
         load_scale_rows(wc_s_raw, wc_scales[0])
-        nc.sync.dma_start(out=tab_w[:], in_=tab_words[0].rearrange("p c i -> p (c i)").bitcast(I32))
-        load_scale_rows(tab_s, tab_scales[0])
         nc.sync.dma_start(out=list1[:], in_=offs)
+        load_scale_rows(tab_s, tab_scales[0])
+        nc.sync.dma_start(out=tab_w[:], in_=tab_words[0].rearrange("p c i -> p (c i)").bitcast(I32))
         nc.sync.dma_start(out=list3[:], in_=offs3)
         nc.sync.dma_start(out=list2[:], in_=offs2)
         load_x(0)
@@ -151,7 +151,7 @@ def tile_list_argo_cast_check_kernel(
             nc.sync.dma_start(out=obs_pair[:], in_=obs_rows[:, 2 * g : 2 * g + 2, :])
             obs_sb.append(obs_pair)
 
-        wd_w = [held([P, PASS], U32, f"wd_w{a}") for a in range(R_PASSES)]
+        wd_w = [held([P, PASS], U32, f"wd_w{a}") for a in range(R_PASSES - 1)]
         wd_s = [held([P, PASS], U8, f"wd_s{a}") for a in range(R_PASSES)]
 
         def quantise_wd(a):
@@ -160,36 +160,32 @@ def tile_list_argo_cast_check_kernel(
                 out=grouped[:].rearrange("p (t m j) -> p m j t", t=PACK, j=PACK),
                 in_=wd_raw[a][:].rearrange("p j (m t) -> p m j t", t=PACK),
             )
-            nc.vector.quantize_mx(out=wd_w[a][:].bitcast(FP8X4), scales=wd_s[a][:], in_=grouped[:])
+            return lambda: nc.vector.quantize_mx(out=wd_w[a][:].bitcast(FP8X4), scales=wd_s[a][:], in_=grouped[:])
 
         work = [[held([P, PACK * HALF], F32, f"work{h}_{a}") for a in range(R_PASSES)] for h in range(HALVES)]
         units = [(j0 // HALF, a, j0 % HALF, width) for j0, width in chunks for a in range(R_PASSES)]
 
+        def clim_plane(h, a, t, engine):
+            bank = banks[(PACK * (R_PASSES * h + a + 1) + t) % 8]
+            nc.tensor.matmul_mx(
+                out=bank[:],
+                lhsT=wc_w[a][:, 2 * P * t : 2 * P * (t + 1)].bitcast(FP4X4),
+                lhsT_scale=wc_s[a][:, P * t : P * (t + 1)],
+                rhs=v_w[h][:].bitcast(FP8X4),
+                rhs_scale=v_s[h][:],
+                start=True,
+                stop=True,
+            )
+            dst = work[h][a][:].rearrange("p (c t j) -> p t c j", t=PACK, j=QUARTER)[:, t, :, :]
+            src = bank[:].rearrange("p (c j) -> p c j", j=QUARTER)
+            if engine == "S":
+                nc.scalar.copy(out=dst, in_=src)
+            else:
+                nc.vector.tensor_copy(out=dst, in_=src)
+
         def clim(h, a):
-            runs = []
-            for j0, width in chunks:
-                if j0 // HALF == h:
-                    if runs and runs[-1][1] == width:
-                        runs[-1] = (runs[-1][0], width, runs[-1][2] + width)
-                    else:
-                        runs.append((j0 % HALF, width, width))
             for t in range(PACK):
-                c = PACK * a + t
-                bank = banks[(PACK * R_PASSES * h + c + PACK) % 8]
-                nc.tensor.matmul_mx(
-                    out=bank[:],
-                    lhsT=wc_w[a][:, 2 * P * t : 2 * P * (t + 1)].bitcast(FP4X4),
-                    lhsT_scale=wc_s[a][:, P * t : P * (t + 1)],
-                    rhs=v_w[h][:].bitcast(FP8X4),
-                    rhs_scale=v_s[h][:],
-                    start=True,
-                    stop=True,
-                )
-                for o, width, total in runs:
-                    dst = work[h][a][:, PACK * o : PACK * (o + total)].rearrange("p (c t j) -> p t c j", t=PACK, j=width)
-                    nc.scalar.copy(
-                        out=dst[:, t, :, :], in_=bank[:, o : o + total].rearrange("p (c j) -> p c j", j=width)
-                    )
+                clim_plane(h, a, t, "S")
 
         def walk_out(dst):
             return dst.rearrange("p (c i t) -> p c t i", i=4, t=PACK)
@@ -202,7 +198,7 @@ def tile_list_argo_cast_check_kernel(
 
         def quantise_x(q, engine):
             h, o = divmod(q * QUARTER, HALF)
-            grouped = ring.tile([P, PACK * QUARTER], BF16, name="grouped_x", align_bytes=64, bufs=2)
+            grouped = held([P, PACK * QUARTER], BF16, f"grouped_x{(0, 1, 2, 1)[q]}")
             src = x_diff[h][:, :, o : o + QUARTER].rearrange("p t (c i) -> p c t i", i=4)
             if engine == "G":
                 nc.gpsimd.tensor_scalar(
@@ -296,12 +292,9 @@ def tile_list_argo_cast_check_kernel(
                 out=h_w[h][a][:, o : o + width].bitcast(FP8X4), scales=h_s[h][a][:, o : o + width], in_=grouped[:]
             )
 
-        def corr_passes(c, g, a, bank):
-            h, o, width = place(c)
-            per_bank = HALF // width
-            count = min(per_bank, N_TILES - g * per_bank)
-            for s in range(count):
-                n = g * per_bank + s
+        def corr_passes(j0, width, tiles, a, bank):
+            h, o = divmod(j0, HALF)
+            for s, n in enumerate(tiles):
                 nc.tensor.matmul_mx(
                     out=bank[:, s * width : (s + 1) * width],
                     lhsT=wo_w[:, a, P * n : P * (n + 1)].bitcast(FP8X4),
@@ -309,86 +302,96 @@ def tile_list_argo_cast_check_kernel(
                     rhs=h_w[h][a][:, o : o + width].bitcast(FP8X4),
                     rhs_scale=h_s[h][a][:, o : o + width],
                     start=(a == 0 and s == 0),
-                    stop=(a == R_PASSES - 1 and s == count - 1),
+                    stop=(a == R_PASSES - 1 and s == len(tiles) - 1),
                 )
 
-        def finish(c, g, bank):
-            j0, width = chunks[c]
-            per_bank = HALF // width
-            part = obs_sb[g][:, :, j0 : j0 + width]
-            nc.vector.tensor_tensor(
-                out=part, in0=part, in1=bank[:].rearrange("p (s j) -> p s j", j=width), op=SUBTRACT
+        def finish(j0, width, tiles, bank):
+            for s in range(0, len(tiles), 2):
+                n = tiles[s]
+                part = obs_sb[n // 2][:, :, j0 : j0 + width]
+                sums = bank[:, s * width : (s + 2) * width].rearrange("p (s j) -> p s j", j=width)
+                nc.vector.tensor_tensor(out=part, in0=part, in1=sums, op=SUBTRACT)
+                nc.sync.dma_start(out=out_rows[:, n : n + 2, j0 : j0 + width], in_=part)
+
+        def last_unit_part(u, part):
+            h, a, o, width = units[u]
+            cols = slice(part * P, (part + 1) * P)
+            tanh_planes = zs[u][:].rearrange("p (t j) -> p t j", t=PACK)
+            planes = ring.tile([P, PACK * P], BF16, name="end_planes")
+            grouped = ring.tile([P, PACK * P], BF16, name="end_grouped", align_bytes=64)
+            for t in range(PACK):
+                nc.scalar.activation(
+                    out=planes[:, t * P : (t + 1) * P], in_=tanh_planes[:, t, cols], func=COPY, scale=gains[:, a, t : t + 1]
+                )
+            nc.vector.tensor_copy(out=walk_out(grouped[:]), in_=walk_in(planes[:]))
+            entries = slice(o + part * P, o + (part + 1) * P)
+            return lambda: nc.vector.quantize_mx(
+                out=h_w[h][a][:, entries].bitcast(FP8X4), scales=h_s[h][a][:, entries], in_=grouped[:]
             )
-            nc.sync.dma_start(out=out_rows[:, 2 * g : 2 * g + 2, j0 : j0 + width], in_=part)
 
         def pick(*idx):
             return [banks[b] for b in idx]
 
         for a in range(R_PASSES):
             clim(0, a)
-        quantise_wd(0)
+        quantise_wd(0)()
         clim(1, 0)
-        quantise_wd(1)
+        quantise_wd(1)()
         clim(1, 1)
-        quantise_wd(2)
+        quantise_last_wd = quantise_wd(2)
         clim(1, 2)
         first = [quantise_x(q, "S") for q in range(2)]
         first[0]()
+        wd_w.append(held([P, PASS], U32, "grouped_x0"))
+        quantise_last_wd()
         later = []
 
-        engines = "GGGGGGGGGGGV"
-        last = len(chunks) - 1
-        drift_banks = []
-        turn = 0
-        for h, a, o, width in units:
-            need = width // P
-            if need == PACK:
-                drift_banks.append(pick(*range(turn % 2 * 4, turn % 2 * 4 + 4)))
-            else:
-                drift_banks.append(pick(*range(4 + turn % 2 * 2, 4 + turn % 2 * 2 + need)))
-            turn += 1
+        last = len(units) - 1
         pending = []
         used = 0
-        last_banks = None
-        for step in range(len(units) + 2):
-            if step < len(units):
-                product(step, drift_banks[step])
+
+        def put_out():
+            j0, tiles, bank = pending.pop(0)
+            for a in range(R_PASSES):
+                corr_passes(j0, QUARTER, tiles, a, bank)
+            finish(j0, QUARTER, tiles, bank)
+
+        for step in range(len(units) + 1):
+            if step <= last:
+                product(step, pick(4 + step % 2 * 2, 5 + step % 2 * 2))
             if step == 0:
                 first[1]()
             if step == 0:
-                later = [quantise_x(q, "V") for q in (2, 3)]
+                later = [quantise_x(q, "SV"[q - 2]) for q in (2, 3)]
             if step == 2:
                 later[0]()
             if step == 2:
                 later[1]()
-            for k in range(1):
-                if pending and step < len(units) + 0:
-                    c, g, bank = pending.pop(0)
-                    for a in range(R_PASSES):
-                        corr_passes(c, g, a, bank)
-                    finish(c, g, bank)
-            if step < len(units):
-                scale(step, engines[step])
+            if pending and step <= last:
+                put_out()
+            if step < last:
+                scale(step, "GGGGGGGGGGG"[step])
             if step >= 2:
                 u = step - 2
                 quantise_h(u)
                 c, a = divmod(u, R_PASSES)
-                if a == R_PASSES - 1 and c < last:
-                    per_bank = HALF // chunks[c][1]
-                    for g in range(-(-N_TILES // per_bank)):
-                        pending.append((c, g, banks[used % 4]))
+                if a == R_PASSES - 1:
+                    for g in range(N_TILES // 2):
+                        pending.append((chunks[c][0], (2 * g, 2 * g + 1), banks[used % 4]))
                         used += 1
-        for c, g, bank in pending:
-            for a in range(R_PASSES):
-                corr_passes(c, g, a, bank)
-        groups = -(-N_TILES // (HALF // chunks[last][1]))
-        free = drift_banks[-2][0]
-        first = banks.index(free)
-        last_banks = [banks[used % 4], banks[first], banks[first + 1]][-groups:]
-        for a in range(R_PASSES):
-            for g in range(groups):
-                corr_passes(last, g, a, last_banks[g])
-        for c, g, bank in pending:
-            finish(c, g, bank)
-        for g in range(groups):
-            finish(last, g, last_banks[g])
+        ends = [(S - 2 * P, pick(1, 4)), (S - P, pick(5, 6))]
+        groups = ((0, 1, 2, 3), (4, 5))
+        for a in range(R_PASSES - 1):
+            for j0, pair in ends:
+                for tiles, bank in zip(groups, pair):
+                    corr_passes(j0, P, tiles, a, bank)
+        quantise_end = [last_unit_part(last, part) for part in range(2)]
+        for (j0, pair), quantise in zip(ends, quantise_end):
+            quantise()
+            for tiles, bank in zip(groups, pair):
+                corr_passes(j0, P, tiles, R_PASSES - 1, bank)
+        while pending:
+            put_out()
+        for j0, pair in ends:
+            for tiles, bank in zip(groups, pair):
+                finish(j0, P, tiles, bank)

@@ -27,7 +27,16 @@ HALVES = S // HALF
 QUARTER = 256
 R_PASSES = H // PASS
 N_TILES = N // P
-LIST_COLS = HALF // 16
+
+
+def rotation(items):
+    turns = []
+
+    def take():
+        turns.append(None)
+        return items[(len(turns) - 1) % len(items)]
+
+    return take
 
 
 def tile_list_argo_cast_check_kernel(
@@ -37,6 +46,7 @@ def tile_list_argo_cast_check_kernel(
     with ExitStack() as ctx:
         keep = ctx.enter_context(tc.tile_pool(name="keep", bufs=1))
         ring = ctx.enter_context(tc.tile_pool(name="ring", bufs=2))
+        placed = ctx.enter_context(tc.tile_pool(name="placed", bufs=1))
         psum = ctx.enter_context(tc.psum_pool(name="psum", bufs=1))
 
         def held(shape, dtype, name):
@@ -50,7 +60,7 @@ def tile_list_argo_cast_check_kernel(
         tab_w = held([P, T], I32, "tab_w")
         tab_s = held([P, T], U8, "tab_s")
         wc_w_raw = held([P, 2 * H], U8, "wc_w_raw")
-        wc_s_raw = held([P, H], U8, "wc_s_raw")
+        wc_s_raw = placed.tile([P, H], U8, name="wc_s_raw", align_bytes=64, offset=4 * (S - 512) - 512)
         wc_w = [held([P, 2 * PASS], U8, f"wc_w{a}") for a in range(R_PASSES)]
         wc_s = [held([P, PASS], U8, f"wc_s{a}") for a in range(R_PASSES)]
         wo_w = held([P, R_PASSES, N], I32, "wo_w")
@@ -59,8 +69,8 @@ def tile_list_argo_cast_check_kernel(
         x_planes = [keep.tile([P, T], F32, name="big", bufs=PACK, align_bytes=64) for t in range(PACK)]
         wd_raw = [held([P, PACK, PASS], F32, f"wd_raw{a}") for a in range(R_PASSES)]
 
-        nc.vector.memset(wc_s_raw[:].bitcast(I32), 0)
         nc.vector.memset(tab_s[:].bitcast(I32), 0)
+        nc.vector.memset(wc_s_raw[:].bitcast(I32), 0)
         nc.vector.memset(wo_s[:].rearrange("p a n -> p (a n)").bitcast(I32), 0)
 
         x_rows = xT.rearrange("(p t) c -> p t c", t=PACK)
@@ -78,14 +88,13 @@ def tile_list_argo_cast_check_kernel(
         def load_wd(a):
             nc.sync.dma_start(out=wd_raw[a][:], in_=wd_rows[:, :, a * PASS : (a + 1) * PASS])
 
-        chunks = [(0, 256), (256, 256), (512, 256), (768, 256)]
         obs_rows = obs.rearrange("(n p) j -> p n j", p=P)
         out_rows = out.rearrange("(n p) j -> p n j", p=P)
         nc.sync.dma_start(out=wc_w_raw[:].bitcast(I32), in_=wc_words[0].bitcast(I32))
-        load_scale_rows(wc_s_raw, wc_scales[0])
-        nc.sync.dma_start(out=list1[:], in_=offs)
         load_scale_rows(tab_s, tab_scales[0])
+        nc.sync.dma_start(out=list1[:], in_=offs)
         nc.sync.dma_start(out=tab_w[:], in_=tab_words[0].rearrange("p c i -> p (c i)").bitcast(I32))
+        load_scale_rows(wc_s_raw, wc_scales[0])
         nc.sync.dma_start(out=list3[:], in_=offs3)
         nc.sync.dma_start(out=list2[:], in_=offs2)
         load_x(0)
@@ -103,47 +112,95 @@ def tile_list_argo_cast_check_kernel(
             )
         nc.sync.dma_start(out=wo_w[:], in_=wo_words.rearrange("a p c i -> p a (c i)").bitcast(I32))
 
-        def deal_wc(a):
+        def deal_words(a):
             nc.vector.tensor_copy(
                 out=wc_w[a][:].bitcast(U16).rearrange("p (t m) -> p t m", t=PACK),
                 in_=wc_w_raw[:, 2 * PASS * a : 2 * PASS * (a + 1)].bitcast(U16).rearrange("p (m t) -> p t m", t=PACK),
             )
+
+        def deal_scales(a):
             nc.vector.tensor_copy(
                 out=wc_s[a][:].rearrange("p (t m) -> p t m", t=PACK),
                 in_=wc_s_raw[:, PASS * a : PASS * (a + 1)].rearrange("p (m t) -> p t m", t=PACK),
             )
 
-        def list_half(lst, h):
-            return lst[:, h * LIST_COLS : (h + 1) * LIST_COLS]
+        def entries(lst, j0, width):
+            return lst[:, j0 // 16 : (j0 + width) // 16]
 
-        v_w = [held([P, HALF], U32, f"v_w{h}") for h in range(HALVES)]
-        v_s = [held([P, HALF], U8, f"v_s{h}") for h in range(HALVES)]
-        for a in range(R_PASSES):
-            deal_wc(a)
-        for h in range(HALVES):
-            nc.vector.tensor_copy(out=v_w[h][:], in_=tab_w[:].bitcast(U32).indirect(list_half(list1, h)))
-            nc.vector.tensor_copy(out=v_s[h][:], in_=tab_s[:].indirect(list_half(list1, h)))
+        spans = ((0, 512), (512, S - 512))
+        v_w0 = held([P, 512], U32, "v_w0")
+        v_s0 = held([P, 512], U8, "v_s0")
+        v_w1 = placed.tile([P, S - 512], U32, name="v_w1", align_bytes=64, offset=0)
+        v_s1 = placed.tile([P, S - 512], U8, name="v_s1", align_bytes=64, offset=4 * (S - 512))
 
-        x_diff = [held([P, PACK, HALF], F32, f"x_diff{h}") for h in range(HALVES)]
-        befores = {}
+        def span_of(j0):
+            h = int(j0 >= 512)
+            return h, j0 - spans[h][0]
 
-        def pick_before(t, h, slot):
-            befores[t, h] = keep.tile([P, HALF], F32, name=f"before{slot}")
-            nc.vector.tensor_copy(out=befores[t, h][:], in_=x_planes[t][:].indirect(list_half(list3, h)))
+        def table_columns(j0, width):
+            h, o = span_of(j0)
+            return (v_w0, v_w1)[h][:, o : o + width], (v_s0, v_s1)[h][:, o : o + width]
 
-        def pick_diff(t, h):
+        def pick_words(dst, j0, width):
+            nc.vector.tensor_copy(out=dst[:], in_=tab_w[:].bitcast(U32).indirect(entries(list1, j0, width)))
+
+        def pick_scales(dst, j0, width):
+            nc.vector.tensor_copy(out=dst[:], in_=tab_s[:].indirect(entries(list1, j0, width)))
+
+        deal_words(0)
+        pick_scales(v_s0, *spans[0])
+        pick_words(v_w0, *spans[0])
+        deal_scales(0)
+        for a in range(1, R_PASSES):
+            deal_words(a)
+            deal_scales(a)
+        pick_words(v_w1, *spans[1])
+        pick_scales(v_s1, *spans[1])
+
+        x_diff = [held([P, PACK, width], F32, f"x_diff{h}") for h, (j0, width) in enumerate(spans)]
+
+        def pick_before(t, j0, width, dst):
+            nc.vector.tensor_copy(out=dst, in_=x_planes[t][:].indirect(entries(list3, j0, width)))
+
+        def pick_diff(t, j0, width, before):
+            h, o = span_of(j0)
             nc.vector.tensor_tensor(
-                out=x_diff[h][:, t, :],
-                in0=x_planes[t][:].indirect(list_half(list2, h)),
-                in1=befores[t, h][:],
+                out=x_diff[h][:, t, o : o + width],
+                in0=x_planes[t][:].indirect(entries(list2, j0, width)),
+                in1=before,
                 op=SUBTRACT,
             )
 
-        for t in range(PACK):
+        wd_w = []
+        wd_s = [held([P, PASS], U8, f"wd_s{a}") for a in range(R_PASSES)]
+
+        def weave_wd(a, engine):
+            grouped = held([P, PACK * PASS], BF16, f"wd_woven{a}")
+            dst = grouped[:].rearrange("p (t m j) -> p m j t", t=PACK, j=PACK)
+            src = wd_raw[a][:].rearrange("p j (m t) -> p m j t", t=PACK)
+            if engine == "G":
+                nc.gpsimd.tensor_scalar(out=dst, in0=src, scalar1=1.0, scalar2=0.0, op0=MULT, op1=ADD)
+            else:
+                nc.scalar.copy(out=dst, in_=src)
+            return grouped
+
+        def quantise_wd(a, grouped, slot):
+            wd_w.append(held([P, PASS], U32, slot))
+            nc.vector.quantize_mx(out=wd_w[a][:].bitcast(FP8X4), scales=wd_s[a][:], in_=grouped[:])
+
+        for t in range(PACK - 1):
+            slots = ("before0", "wd_w0" if t == 1 else "before1")
+            befores = [held([P, width], F32, slot) for slot, (j0, width) in zip(slots, spans)]
             for h in range(HALVES):
-                pick_before(t, h, h)
+                pick_before(t, *spans[h], befores[h][:])
             for h in range(HALVES):
-                pick_diff(t, h)
+                pick_diff(t, *spans[h], befores[h][:])
+        befores = [held([P, QUARTER], F32, slot) for slot in ("wd_w1", "wd_w2")]
+        for c in range(2):
+            pick_before(PACK - 1, c * QUARTER, QUARTER, befores[c][:])
+        for c in range(2):
+            pick_diff(PACK - 1, c * QUARTER, QUARTER, befores[c][:])
+
 
         obs_sb = []
         for g in range(N_TILES // 2):
@@ -151,247 +208,244 @@ def tile_list_argo_cast_check_kernel(
             nc.sync.dma_start(out=obs_pair[:], in_=obs_rows[:, 2 * g : 2 * g + 2, :])
             obs_sb.append(obs_pair)
 
-        wd_w = [held([P, PASS], U32, f"wd_w{a}") for a in range(R_PASSES - 1)]
-        wd_s = [held([P, PASS], U8, f"wd_s{a}") for a in range(R_PASSES)]
+        widths = (256, 256, 256, 256)
+        chunks = [(sum(widths[:c]), w) for c, w in enumerate(widths)]
+        units = [(c, a) for c in range(len(chunks)) for a in range(R_PASSES)]
+        kinds = "AAAAAAAAAADD"
+        work = [[held([P, HALF], F32, f"work{u}_{b}")[:] for b in range(2)] for u in range(1, len(units) - 1)]
+        work.insert(0, [x_diff[1][:, PACK - 1, :], held([P, HALF], F32, "work0_1")[:]])
 
-        def quantise_wd(a):
-            grouped = ring.tile([P, PACK * PASS], BF16, name="grouped", align_bytes=64, bufs=3)
-            nc.scalar.copy(
-                out=grouped[:].rearrange("p (t m j) -> p m j t", t=PACK, j=PACK),
-                in_=wd_raw[a][:].rearrange("p j (m t) -> p m j t", t=PACK),
-            )
-            return lambda: nc.vector.quantize_mx(out=wd_w[a][:].bitcast(FP8X4), scales=wd_s[a][:], in_=grouped[:])
+        def banks_of(u):
+            return range(PACK * chunks[units[u][0]][1] // HALF)
 
-        work = [[held([P, PACK * HALF], F32, f"work{h}_{a}") for a in range(R_PASSES)] for h in range(HALVES)]
-        units = [(j0 // HALF, a, j0 % HALF, width) for j0, width in chunks for a in range(R_PASSES)]
-
-        def clim_plane(h, a, t, engine):
-            bank = banks[(PACK * (R_PASSES * h + a + 1) + t) % 8]
-            nc.tensor.matmul_mx(
-                out=bank[:],
-                lhsT=wc_w[a][:, 2 * P * t : 2 * P * (t + 1)].bitcast(FP4X4),
-                lhsT_scale=wc_s[a][:, P * t : P * (t + 1)],
-                rhs=v_w[h][:].bitcast(FP8X4),
-                rhs_scale=v_s[h][:],
-                start=True,
-                stop=True,
-            )
-            dst = work[h][a][:].rearrange("p (c t j) -> p t c j", t=PACK, j=QUARTER)[:, t, :, :]
-            src = bank[:].rearrange("p (c j) -> p c j", j=QUARTER)
-            if engine == "S":
-                nc.scalar.copy(out=dst, in_=src)
+        def first_stage(u, b, bank, w_codes, w_scales, rhs_w, rhs_s):
+            width = chunks[units[u][0]][1]
+            if kinds[u] == "A" and width == QUARTER:
+                passes = [(2 * b + s, 0, QUARTER) for s in range(2)]
             else:
-                nc.vector.tensor_copy(out=dst, in_=src)
+                passes = [(t, b * P, P) for t in range(PACK)]
+            for s, (t, o, n) in enumerate(passes):
+                nc.tensor.matmul_mx(
+                    out=bank[:, s * n : (s + 1) * n],
+                    lhsT=w_codes(t),
+                    lhsT_scale=w_scales[:, P * t : P * (t + 1)],
+                    rhs=rhs_w[:, o : o + n].bitcast(FP8X4),
+                    rhs_scale=rhs_s[:, o : o + n],
+                    start=True,
+                    stop=True,
+                )
+            if kinds[u] == "A":
+                return bank[:]
+            return bank[:].rearrange("p (t j) -> p j t", t=PACK)
 
-        def clim(h, a):
-            for t in range(PACK):
-                clim_plane(h, a, t, "S")
+        def part_of(u, cols):
+            if kinds[u] == "A":
+                return cols
+            return cols.rearrange("p (j t) -> p j t", t=PACK)
+
+        clim_bank = rotation(banks)
+
+        def clim(u):
+            c, a = units[u]
+            words, scales = table_columns(*chunks[c])
+            for b in banks_of(u):
+                bank = clim_bank()
+                sums = first_stage(
+                    u, b, bank, lambda t: wc_w[a][:, 2 * P * t : 2 * P * (t + 1)].bitcast(FP4X4), wc_s[a], words, scales
+                )
+                nc.scalar.copy(out=part_of(u, work[u][b]), in_=sums)
 
         def walk_out(dst):
             return dst.rearrange("p (c i t) -> p c t i", i=4, t=PACK)
 
-        def walk_in(src):
-            return src.rearrange("p (t c i) -> p c t i", i=4, t=PACK)
+        x_w = {}
+        x_s = [held([P, w], U8, f"x_s{c}") for c, w in enumerate(widths)]
 
-        x_w = [held([P, HALF], U32, f"x_w{h}") for h in range(HALVES)]
-        x_s = [held([P, HALF], U8, f"x_s{h}") for h in range(HALVES)]
-
-        def quantise_x(q, engine):
-            h, o = divmod(q * QUARTER, HALF)
-            grouped = held([P, PACK * QUARTER], BF16, f"grouped_x{(0, 1, 2, 1)[q]}")
-            src = x_diff[h][:, :, o : o + QUARTER].rearrange("p t (c i) -> p c t i", i=4)
-            if engine == "G":
-                nc.gpsimd.tensor_scalar(
-                    out=grouped[:].rearrange("p (j t) -> p j t", t=PACK),
-                    in0=x_diff[h][:, :, o : o + QUARTER].rearrange("p t j -> p j t"),
-                    scalar1=1.0,
-                    scalar2=0.0,
-                    op0=MULT,
-                    op1=ADD,
-                )
-            elif engine == "S":
+        def weave_x(c, engine, room=None):
+            j0, width = chunks[c]
+            h, o = span_of(j0)
+            grouped = held([P, PACK * width], BF16, room or f"x_woven{c}")
+            src = x_diff[h][:, :, o : o + width].rearrange("p t (c i) -> p c t i", i=4)
+            if engine == "S":
                 nc.scalar.copy(out=walk_out(grouped[:]), in_=src)
+            elif engine == "G":
+                nc.gpsimd.tensor_scalar(out=walk_out(grouped[:]), in0=src, scalar1=1.0, scalar2=0.0, op0=MULT, op1=ADD)
             else:
                 nc.vector.tensor_copy(out=walk_out(grouped[:]), in_=src)
-            return lambda: nc.vector.quantize_mx(
-                out=x_w[h][:, o : o + QUARTER].bitcast(FP8X4), scales=x_s[h][:, o : o + QUARTER], in_=grouped[:]
-            )
 
-        h_w = [[held([P, HALF], U32, f"h_w{h}_{a}") for a in range(R_PASSES)] for h in range(HALVES)]
-        h_s = [[held([P, HALF], U8, f"h_s{h}_{a}") for a in range(R_PASSES)] for h in range(HALVES)]
+            def quantise(slot=None):
+                x_w[c] = held([P, width], U32, slot or f"x_w{c}")
+                nc.vector.quantize_mx(out=x_w[c][:].bitcast(FP8X4), scales=x_s[c][:], in_=grouped[:])
 
-        def place(c):
-            j0, width = chunks[c]
-            return j0 // HALF, j0 % HALF, width
+            return quantise
 
-        def region(u):
-            h, a, o, width = units[u]
-            return work[h][a][:, PACK * o : PACK * (o + width)]
+        h_w = [held([P, chunks[c][1]], U32, f"h_w{u}") for u, (c, a) in enumerate(units)]
+        h_s = [held([P, chunks[c][1]], U8, f"h_s{u}") for u, (c, a) in enumerate(units)]
 
         zs = {}
+        drift_bank = rotation(banks[4:])
 
-        def product(u, drift_banks):
-            h, a, o, width = units[u]
-            per_bank = HALF // width
-            w = region(u)
-            z = ring.tile([P, PACK * width], F32, name="z", bufs=2)
+        def product(u):
+            c, a = units[u]
+            z = ring.tile([P, PACK * chunks[c][1]], F32, name="z", bufs=2)
             zs[u] = z
-            for b, bank in enumerate(drift_banks):
-                for s in range(per_bank):
-                    t = b * per_bank + s
-                    nc.tensor.matmul_mx(
-                        out=bank[:, s * width : (s + 1) * width],
-                        lhsT=wd_w[a][:, P * t : P * (t + 1)].bitcast(FP8X4),
-                        lhsT_scale=wd_s[a][:, P * t : P * (t + 1)],
-                        rhs=x_w[h][:, o : o + width].bitcast(FP8X4),
-                        rhs_scale=x_s[h][:, o : o + width],
-                        start=True,
-                        stop=True,
-                    )
+            for b in banks_of(u):
+                bank = drift_bank()
+                sums = first_stage(
+                    u, b, bank, lambda t: wd_w[a][:, P * t : P * (t + 1)].bitcast(FP8X4), wd_s[a], x_w[c], x_s[c]
+                )
                 cols = slice(b * HALF, (b + 1) * HALF)
-                nc.vector.tensor_tensor(out=z[:, cols], in0=bank[:], in1=w[:, cols], op=MULT)
+                nc.vector.tensor_tensor(out=part_of(u, z[:, cols]), in0=sums, in1=part_of(u, work[u][b]), op=MULT)
                 nc.scalar.activation(out=z[:, cols], in_=z[:, cols], func=TANH)
 
-        grouped_h = {}
+        woven_h = {}
 
-        def scale(u, engine):
-            h, a, o, width = units[u]
-            w = zs[u]
-            if engine == "G":
-                grouped = ring.tile([P, PACK * width], BF16, name="grouped_g", align_bytes=64, bufs=2)
-            else:
-                grouped = ring.tile([P, PACK * width], BF16, name="grouped_h", align_bytes=64, bufs=2)
-            grouped_h[u] = (grouped, engine)
+        def gain_row(a, width):
+            return gains[:, a, :].unsqueeze(1).to_broadcast([P, width, PACK])
+
+        def scale(u):
+            c, a = units[u]
+            width = chunks[c][1]
+            z = zs[u]
             planes = ring.tile([P, PACK * width], BF16, name="h_planes", bufs=3)
             for t in range(PACK):
                 cols = slice(t * width, (t + 1) * width)
-                if engine in "VGT":
-                    nc.scalar.activation(out=planes[:, cols], in_=w[:, cols], func=COPY, scale=gains[:, a, t : t + 1])
-                else:
-                    nc.vector.tensor_scalar(
-                        out=planes[:, cols], in0=w[:, cols], scalar1=gains[:, a, t : t + 1], scalar2=None, op0=MULT
-                    )
-            if engine in "VW":
-                nc.vector.tensor_copy(out=walk_out(grouped[:]), in_=walk_in(planes[:]))
-            elif engine == "G":
-                nc.gpsimd.tensor_scalar(
-                    out=grouped[:].rearrange("p (j t) -> p j t", t=PACK),
-                    in0=planes[:].rearrange("p (t j) -> p j t", t=PACK),
-                    scalar1=1.0,
-                    scalar2=0.0,
-                    op0=MULT,
-                    op1=ADD,
-                )
-            else:
-                nc.scalar.copy(out=walk_out(grouped[:]), in_=walk_in(planes[:]))
-
-        def quantise_h(u):
-            h, a, o, width = units[u]
-            grouped, engine = grouped_h[u]
-            nc.vector.quantize_mx(
-                out=h_w[h][a][:, o : o + width].bitcast(FP8X4), scales=h_s[h][a][:, o : o + width], in_=grouped[:]
+                nc.scalar.activation(out=planes[:, cols], in_=z[:, cols], func=COPY, scale=gains[:, a, t : t + 1])
+            grouped = ring.tile([P, PACK * width], BF16, name="h_woven", align_bytes=64, bufs=1)
+            woven_h[u] = grouped
+            nc.gpsimd.tensor_scalar(
+                out=grouped[:].rearrange("p (j t) -> p j t", t=PACK),
+                in0=planes[:].rearrange("p (t j) -> p j t", t=PACK),
+                scalar1=1.0,
+                scalar2=0.0,
+                op0=MULT,
+                op1=ADD,
             )
 
-        def corr_passes(j0, width, tiles, a, bank):
-            h, o = divmod(j0, HALF)
+        def quantise_h(u):
+            nc.vector.quantize_mx(out=h_w[u][:].bitcast(FP8X4), scales=h_s[u][:], in_=woven_h[u][:])
+
+        def scale_part(u, b, room=None):
+            grouped = ring.tile([P, HALF], BF16, name="end_woven", align_bytes=64, bufs=4) if room is None else room.bitcast(BF16)
+            nc.vector.tensor_tensor(
+                out=grouped[:].rearrange("p (j t) -> p j t", t=PACK),
+                in0=part_of(u, zs[u][:, b * HALF : (b + 1) * HALF]),
+                in1=gain_row(units[u][1], P),
+                op=MULT,
+            )
+            cols = slice(b * P, (b + 1) * P)
+            return lambda: nc.vector.quantize_mx(
+                out=h_w[u][:, cols].bitcast(FP8X4), scales=h_s[u][:, cols], in_=grouped[:]
+            )
+
+        def corr_passes(c, o, width, tiles, a, bank):
+            u = R_PASSES * c + a
             for s, n in enumerate(tiles):
                 nc.tensor.matmul_mx(
                     out=bank[:, s * width : (s + 1) * width],
                     lhsT=wo_w[:, a, P * n : P * (n + 1)].bitcast(FP8X4),
                     lhsT_scale=wo_s[:, a, P * n : P * (n + 1)],
-                    rhs=h_w[h][a][:, o : o + width].bitcast(FP8X4),
-                    rhs_scale=h_s[h][a][:, o : o + width],
+                    rhs=h_w[u][:, o : o + width].bitcast(FP8X4),
+                    rhs_scale=h_s[u][:, o : o + width],
                     start=(a == 0 and s == 0),
                     stop=(a == R_PASSES - 1 and s == len(tiles) - 1),
                 )
 
-        def finish(j0, width, tiles, bank):
+        def finish(c, o, width, tiles, bank, room=None):
+            j0 = chunks[c][0] + o
             for s in range(0, len(tiles), 2):
                 n = tiles[s]
                 part = obs_sb[n // 2][:, :, j0 : j0 + width]
                 sums = bank[:, s * width : (s + 2) * width].rearrange("p (s j) -> p s j", j=width)
-                nc.vector.tensor_tensor(out=part, in0=part, in1=sums, op=SUBTRACT)
-                nc.sync.dma_start(out=out_rows[:, n : n + 2, j0 : j0 + width], in_=part)
+                res = part if room is None else room[:, s * width : (s + 2) * width].rearrange("p (s j) -> p s j", j=width)
+                nc.vector.tensor_tensor(out=res, in0=part, in1=sums, op=SUBTRACT)
+                nc.sync.dma_start(out=out_rows[:, n : n + 2, j0 : j0 + width], in_=res)
 
-        def last_unit_part(u, part):
-            h, a, o, width = units[u]
-            cols = slice(part * P, (part + 1) * P)
-            tanh_planes = zs[u][:].rearrange("p (t j) -> p t j", t=PACK)
-            planes = ring.tile([P, PACK * P], BF16, name="end_planes")
-            grouped = ring.tile([P, PACK * P], BF16, name="end_grouped", align_bytes=64)
-            for t in range(PACK):
-                nc.scalar.activation(
-                    out=planes[:, t * P : (t + 1) * P], in_=tanh_planes[:, t, cols], func=COPY, scale=gains[:, a, t : t + 1]
-                )
-            nc.vector.tensor_copy(out=walk_out(grouped[:]), in_=walk_in(planes[:]))
-            entries = slice(o + part * P, o + (part + 1) * P)
-            return lambda: nc.vector.quantize_mx(
-                out=h_w[h][a][:, entries].bitcast(FP8X4), scales=h_s[h][a][:, entries], in_=grouped[:]
-            )
-
-        def pick(*idx):
-            return [banks[b] for b in idx]
-
-        for a in range(R_PASSES):
-            clim(0, a)
-        quantise_wd(0)()
-        clim(1, 0)
-        quantise_wd(1)()
-        clim(1, 1)
-        quantise_last_wd = quantise_wd(2)
-        clim(1, 2)
-        first = [quantise_x(q, "S") for q in range(2)]
-        first[0]()
-        wd_w.append(held([P, PASS], U32, "grouped_x0"))
-        quantise_last_wd()
-        later = []
-
-        last = len(units) - 1
+        corr_bank = rotation(banks[:4])
         pending = []
-        used = 0
 
-        def put_out():
-            j0, tiles, bank = pending.pop(0)
+        def plan_out(c):
+            width = chunks[c][1]
+            per_bank = HALF // width
+            for n in range(0, N_TILES, per_bank):
+                pending.append((c, tuple(range(n, min(n + per_bank, N_TILES))), corr_bank()))
+
+        def put_out(room=None):
+            c, tiles, bank = pending.pop(0)
             for a in range(R_PASSES):
-                corr_passes(j0, QUARTER, tiles, a, bank)
-            finish(j0, QUARTER, tiles, bank)
+                corr_passes(c, 0, chunks[c][1], tiles, a, bank)
+            finish(c, 0, chunks[c][1], tiles, bank, room)
 
-        for step in range(len(units) + 1):
+        for u in range(6):
+            clim(u)
+        quantise_wd(0, weave_wd(0, "S"), "wd_w0")
+        for u in range(6, 9):
+            clim(u)
+        wd_woven1 = weave_wd(1, "S")
+        wd_woven2 = weave_wd(2, "S")
+        for u in range(9, len(units) - 1):
+            clim(u)
+        quantise_x = [weave_x(c, "S") for c in range(2)]
+        last_work = held([P, 2, HALF], F32, "x_diff0")
+        work.append([last_work[:, b, :] for b in range(2)])
+        clim(len(units) - 1)
+        quantise_x[0]()
+        quantise_wd(1, wd_woven1, "wd_w1")
+        quantise_wd(2, wd_woven2, "wd_w2")
+        late_before = held([P, HALF], F32, "x_woven0")
+        pick_before(PACK - 1, HALF, HALF, late_before[:])
+        last = len(units) - 1
+        lag = 2
+        parts = {}
+        for step in range(last + lag):
             if step <= last:
-                product(step, pick(4 + step % 2 * 2, 5 + step % 2 * 2))
+                product(step)
+            if pending and step <= last + 1:
+                put_out(work[min(step, last)][int(step > last)])
+            if step <= last and kinds[step] == "A":
+                scale(step)
             if step == 0:
-                first[1]()
-            if step == 0:
-                later = [quantise_x(q, "SV"[q - 2]) for q in (2, 3)]
+                quantise_x[1]("work0_1")
+            if step == 1:
+                pick_diff(PACK - 1, HALF, HALF, late_before[:])
             if step == 2:
-                later[0]()
-            if step == 2:
-                later[1]()
-            if pending and step <= last:
-                put_out()
-            if step < last:
-                scale(step, "GGGGGGGGGGG"[step])
-            if step >= 2:
-                u = step - 2
-                quantise_h(u)
-                c, a = divmod(u, R_PASSES)
-                if a == R_PASSES - 1:
-                    for g in range(N_TILES // 2):
-                        pending.append((chunks[c][0], (2 * g, 2 * g + 1), banks[used % 4]))
-                        used += 1
-        ends = [(S - 2 * P, pick(1, 4)), (S - P, pick(5, 6))]
+                quantise_x.append(weave_x(2, "V", "work2_1"))
+            if step == 3:
+                quantise_x[2]("work3_1")
+            if step == 4:
+                quantise_x.append(weave_x(3, "V", "work4_1"))
+            if step == 5:
+                quantise_x[3]("work5_1")
+            u = step - lag
+            if u >= 0:
+                if kinds[u] == "A":
+                    quantise_h(u)
+                for quantise in parts.get(u, ()):
+                    quantise()
+                if units[u][1] == R_PASSES - 1:
+                    plan_out(units[u][0])
+            u = step - lag + 1
+            if 0 <= u < last and kinds[u] == "D":
+                room = None
+                parts[u] = [
+                    scale_part(u, b, None if room is None else room[:, b * QUARTER : (b + 1) * QUARTER])
+                    for b in banks_of(u)
+                ]
+
+        ends = [(0, (banks[1], banks[4])), (P, (banks[5], banks[6]))]
         groups = ((0, 1, 2, 3), (4, 5))
+        c = len(chunks) - 1
         for a in range(R_PASSES - 1):
-            for j0, pair in ends:
+            for o, pair in ends:
                 for tiles, bank in zip(groups, pair):
-                    corr_passes(j0, P, tiles, a, bank)
-        quantise_end = [last_unit_part(last, part) for part in range(2)]
-        for (j0, pair), quantise in zip(ends, quantise_end):
+                    corr_passes(c, o, P, tiles, a, bank)
+        quantise_end = [scale_part(last, b) for b in range(2)]
+        for (o, pair), quantise in zip(ends, quantise_end):
             quantise()
             for tiles, bank in zip(groups, pair):
-                corr_passes(j0, P, tiles, R_PASSES - 1, bank)
+                corr_passes(c, o, P, tiles, R_PASSES - 1, bank)
         while pending:
             put_out()
-        for j0, pair in ends:
+        for o, pair in ends:
             for tiles, bank in zip(groups, pair):
-                finish(j0, P, tiles, bank)
+                finish(c, o, P, tiles, bank)

@@ -47,6 +47,7 @@ def tile_list_argo_cast_check_kernel(
         keep = ctx.enter_context(tc.tile_pool(name="keep", bufs=1))
         ring = ctx.enter_context(tc.tile_pool(name="ring", bufs=2))
         placed = ctx.enter_context(tc.tile_pool(name="placed", bufs=1))
+        arena = ctx.enter_context(tc.tile_pool(name="arena", bufs=1))
         psum = ctx.enter_context(tc.psum_pool(name="psum", bufs=1))
 
         def held(shape, dtype, name):
@@ -102,8 +103,8 @@ def tile_list_argo_cast_check_kernel(
         load_wd(0)
         load_x(2)
         load_wd(1)
-        load_wd(2)
         load_x(3)
+        load_wd(2)
         nc.sync.dma_start(out=gains[:], in_=gain.rearrange("(a p t) -> p a t", p=P, t=PACK))
         for q in range(4):
             nc.sync.dma_start(
@@ -157,70 +158,83 @@ def tile_list_argo_cast_check_kernel(
         pick_words(v_w1, *spans[1])
         pick_scales(v_s1, *spans[1])
 
-        x_diff = [held([P, PACK, width], F32, f"x_diff{h}") for h, (j0, width) in enumerate(spans)]
+        chunks = [(c * QUARTER, QUARTER) for c in range(S // QUARTER)]
+        units = [(c, a) for c in range(len(chunks)) for a in range(R_PASSES)]
+        kinds = "AAAAAAAAAAWD"
+        last = len(units) - 1
 
-        def pick_before(t, j0, width, dst):
-            nc.vector.tensor_copy(out=dst, in_=x_planes[t][:].indirect(entries(list3, j0, width)))
+        def in_arena(shape, dtype, name, u, b, o=0):
+            return arena.tile(shape, dtype, name=name, align_bytes=64, offset=(2 * u + b) * 4 * HALF + o)
 
-        def pick_diff(t, j0, width, before):
-            h, o = span_of(j0)
-            nc.vector.tensor_tensor(
-                out=x_diff[h][:, t, o : o + width],
-                in0=x_planes[t][:].indirect(entries(list2, j0, width)),
-                in1=before,
-                op=SUBTRACT,
-            )
+        late_before = held([P, PACK, QUARTER], F32, "late_before")
+        first_after = held([P, PACK + 2, QUARTER], F32, "first_after")
+        late_after = first_after[:, 2 : PACK + 2, :]
+        lent = {(0, 0): late_after[:, 2:4, :], (1, 0): late_before[:, 0:2, :], (3, 1): late_before[:, 2:4, :]}
 
-        wd_w = []
+        def work_tile(u, b):
+            if (u, b) in lent:
+                return lent[u, b].rearrange("p t j -> p (t j)")
+            return in_arena([P, HALF], F32, f"work{u}_{b}", u, b)
+
+        work = [[work_tile(u, b) for b in range(2)] for u in range(len(units))]
+
+        lists = (list2, list3)
+        picks = {c: [held([P, PACK, QUARTER], F32, f"picks{c}_{i}") for i in range(2)] for c in range(1, 3)}
+        picks[0] = [first_after[:, 0:PACK, :], held([P, PACK, QUARTER], F32, "picks0_1")]
+
+        def pick(c, i, t, dst):
+            nc.vector.tensor_copy(out=dst, in_=x_planes[t][:].indirect(entries(lists[i], *chunks[c])))
+
+        def pick_plane(c, t):
+            for i in range(2):
+                pick(c, i, t, picks[c][i][:, t, :])
+
+        wd_w = [held([P, PASS], U32, f"wd_w{a}") for a in range(R_PASSES)]
         wd_s = [held([P, PASS], U8, f"wd_s{a}") for a in range(R_PASSES)]
 
-        def weave_wd(a, engine):
-            grouped = held([P, PACK * PASS], BF16, f"wd_woven{a}")
+        def weave_wd(a, engine, slot):
+            grouped = held([P, PACK * PASS], BF16, slot)
             dst = grouped[:].rearrange("p (t m j) -> p m j t", t=PACK, j=PACK)
             src = wd_raw[a][:].rearrange("p j (m t) -> p m j t", t=PACK)
             if engine == "G":
+                dst = grouped[:].rearrange("p (t m j) -> p m t j", t=PACK, j=PACK)
+                src = wd_raw[a][:].rearrange("p j (m t) -> p m t j", t=PACK)
                 nc.gpsimd.tensor_scalar(out=dst, in0=src, scalar1=1.0, scalar2=0.0, op0=MULT, op1=ADD)
             else:
                 nc.scalar.copy(out=dst, in_=src)
             return grouped
 
-        def quantise_wd(a, grouped, slot):
-            wd_w.append(held([P, PASS], U32, slot))
+        def quantise_wd(a, grouped, codes=None):
+            if codes is not None:
+                wd_w[a] = codes
             nc.vector.quantize_mx(out=wd_w[a][:].bitcast(FP8X4), scales=wd_s[a][:], in_=grouped[:])
 
-        for t in range(PACK - 1):
-            slots = ("before0", "wd_w0" if t == 1 else "before1")
-            befores = [held([P, width], F32, slot) for slot, (j0, width) in zip(slots, spans)]
-            for h in range(HALVES):
-                pick_before(t, *spans[h], befores[h][:])
-            for h in range(HALVES):
-                pick_diff(t, *spans[h], befores[h][:])
-        befores = [held([P, QUARTER], F32, slot) for slot in ("wd_w1", "wd_w2")]
-        for c in range(2):
-            pick_before(PACK - 1, c * QUARTER, QUARTER, befores[c][:])
-        for c in range(2):
-            pick_diff(PACK - 1, c * QUARTER, QUARTER, befores[c][:])
+        def walk_out(dst):
+            return dst.rearrange("p (c i t) -> p c t i", i=4, t=PACK)
 
+        def walk_in(src):
+            return src.rearrange("p t (c i) -> p c t i", i=4)
 
-        obs_sb = []
-        for g in range(N_TILES // 2):
-            obs_pair = keep.tile([P, 2, S], F32, name="big", bufs=PACK, align_bytes=64)
-            nc.sync.dma_start(out=obs_pair[:], in_=obs_rows[:, 2 * g : 2 * g + 2, :])
-            obs_sb.append(obs_pair)
+        x_w = {}
+        x_s = [held([P, QUARTER], U8, f"x_s{c}") for c in range(len(chunks))]
 
-        widths = (256, 256, 256, 256)
-        chunks = [(sum(widths[:c]), w) for c, w in enumerate(widths)]
-        units = [(c, a) for c in range(len(chunks)) for a in range(R_PASSES)]
-        kinds = "AAAAAAAAAADD"
-        work = [[held([P, HALF], F32, f"work{u}_{b}")[:] for b in range(2)] for u in range(1, len(units) - 1)]
-        work.insert(0, [x_diff[1][:, PACK - 1, :], held([P, HALF], F32, "work0_1")[:]])
+        def weave_x(engine, dst, after, before):
+            engine.tensor_tensor(out=walk_out(dst), in0=walk_in(after), in1=walk_in(before), op=SUBTRACT)
 
-        def banks_of(u):
-            return range(PACK * chunks[units[u][0]][1] // HALF)
+        def weave_chunk(c, slot):
+            grouped = held([P, PACK * QUARTER], BF16, slot)
+            for t in range(0, PACK, 2):
+                after, before = (side[:, t : t + 2, :].rearrange("p t j -> p j t") for side in picks[c])
+                dst = grouped[:].rearrange("p (j t) -> p j t", t=PACK)[:, :, t : t + 2]
+                nc.gpsimd.tensor_tensor(out=dst, in0=after, in1=before, op=SUBTRACT)
+            return grouped
+
+        def quantise_x(c, grouped, codes):
+            x_w[c] = codes
+            nc.vector.quantize_mx(out=codes[:].bitcast(FP8X4), scales=x_s[c][:], in_=grouped[:])
 
         def first_stage(u, b, bank, w_codes, w_scales, rhs_w, rhs_s):
-            width = chunks[units[u][0]][1]
-            if kinds[u] == "A" and width == QUARTER:
+            if kinds[u] != "D":
                 passes = [(2 * b + s, 0, QUARTER) for s in range(2)]
             else:
                 passes = [(t, b * P, P) for t in range(PACK)]
@@ -234,12 +248,12 @@ def tile_list_argo_cast_check_kernel(
                     start=True,
                     stop=True,
                 )
-            if kinds[u] == "A":
+            if kinds[u] != "D":
                 return bank[:]
             return bank[:].rearrange("p (t j) -> p j t", t=PACK)
 
         def part_of(u, cols):
-            if kinds[u] == "A":
+            if kinds[u] != "D":
                 return cols
             return cols.rearrange("p (j t) -> p j t", t=PACK)
 
@@ -248,89 +262,68 @@ def tile_list_argo_cast_check_kernel(
         def clim(u):
             c, a = units[u]
             words, scales = table_columns(*chunks[c])
-            for b in banks_of(u):
+            for b in range(2):
                 bank = clim_bank()
                 sums = first_stage(
                     u, b, bank, lambda t: wc_w[a][:, 2 * P * t : 2 * P * (t + 1)].bitcast(FP4X4), wc_s[a], words, scales
                 )
-                nc.scalar.copy(out=part_of(u, work[u][b]), in_=sums)
+                nc.scalar.copy(out=part_of(u, work[u][b][:]), in_=sums)
 
-        def walk_out(dst):
-            return dst.rearrange("p (c i t) -> p c t i", i=4, t=PACK)
-
-        x_w = {}
-        x_s = [held([P, w], U8, f"x_s{c}") for c, w in enumerate(widths)]
-
-        def weave_x(c, engine, room=None):
-            j0, width = chunks[c]
-            h, o = span_of(j0)
-            grouped = held([P, PACK * width], BF16, room or f"x_woven{c}")
-            src = x_diff[h][:, :, o : o + width].rearrange("p t (c i) -> p c t i", i=4)
-            if engine == "S":
-                nc.scalar.copy(out=walk_out(grouped[:]), in_=src)
-            elif engine == "G":
-                nc.gpsimd.tensor_scalar(out=walk_out(grouped[:]), in0=src, scalar1=1.0, scalar2=0.0, op0=MULT, op1=ADD)
-            else:
-                nc.vector.tensor_copy(out=walk_out(grouped[:]), in_=src)
-
-            def quantise(slot=None):
-                x_w[c] = held([P, width], U32, slot or f"x_w{c}")
-                nc.vector.quantize_mx(out=x_w[c][:].bitcast(FP8X4), scales=x_s[c][:], in_=grouped[:])
-
-            return quantise
-
-        h_w = [held([P, chunks[c][1]], U32, f"h_w{u}") for u, (c, a) in enumerate(units)]
-        h_s = [held([P, chunks[c][1]], U8, f"h_s{u}") for u, (c, a) in enumerate(units)]
-
+        h_w = {}
+        h_s = [held([P, QUARTER], U8, f"h_s{u}") for u in range(len(units))]
         zs = {}
         drift_bank = rotation(banks[4:])
 
         def product(u):
             c, a = units[u]
-            z = ring.tile([P, PACK * chunks[c][1]], F32, name="z", bufs=2)
+            z = ring.tile([P, PACK * QUARTER], F32, name="z", bufs=2)
             zs[u] = z
-            for b in banks_of(u):
+            for b in range(2):
                 bank = drift_bank()
                 sums = first_stage(
                     u, b, bank, lambda t: wd_w[a][:, P * t : P * (t + 1)].bitcast(FP8X4), wd_s[a], x_w[c], x_s[c]
                 )
                 cols = slice(b * HALF, (b + 1) * HALF)
-                nc.vector.tensor_tensor(out=part_of(u, z[:, cols]), in0=sums, in1=part_of(u, work[u][b]), op=MULT)
+                nc.vector.tensor_tensor(out=part_of(u, z[:, cols]), in0=sums, in1=part_of(u, work[u][b][:]), op=MULT)
                 nc.scalar.activation(out=z[:, cols], in_=z[:, cols], func=TANH)
 
+        planes_h = {}
         woven_h = {}
 
-        def gain_row(a, width):
-            return gains[:, a, :].unsqueeze(1).to_broadcast([P, width, PACK])
-
         def scale(u):
-            c, a = units[u]
-            width = chunks[c][1]
-            z = zs[u]
-            planes = ring.tile([P, PACK * width], BF16, name="h_planes", bufs=3)
+            a = units[u][1]
+            planes = ring.tile([P, PACK * QUARTER], BF16, name="h_planes", bufs=4)
+            planes_h[u] = planes
             for t in range(PACK):
-                cols = slice(t * width, (t + 1) * width)
-                nc.scalar.activation(out=planes[:, cols], in_=z[:, cols], func=COPY, scale=gains[:, a, t : t + 1])
-            grouped = ring.tile([P, PACK * width], BF16, name="h_woven", align_bytes=64, bufs=1)
+                cols = slice(t * QUARTER, (t + 1) * QUARTER)
+                nc.scalar.activation(out=planes[:, cols], in_=zs[u][:, cols], func=COPY, scale=gains[:, a, t : t + 1])
+
+        def weave_h(u, grouped):
             woven_h[u] = grouped
-            nc.gpsimd.tensor_scalar(
-                out=grouped[:].rearrange("p (j t) -> p j t", t=PACK),
-                in0=planes[:].rearrange("p (t j) -> p j t", t=PACK),
-                scalar1=1.0,
-                scalar2=0.0,
-                op0=MULT,
-                op1=ADD,
-            )
+            if kinds[u] == "A":
+                nc.gpsimd.tensor_scalar(
+                    out=grouped[:].rearrange("p (j t) -> p j t", t=PACK),
+                    in0=planes_h[u][:].rearrange("p (t j) -> p j t", t=PACK),
+                    scalar1=1.0,
+                    scalar2=0.0,
+                    op0=MULT,
+                    op1=ADD,
+                )
+            else:
+                nc.vector.tensor_copy(
+                    out=walk_out(grouped[:]), in_=walk_in(planes_h[u][:].rearrange("p (t j) -> p t j", t=PACK))
+                )
 
-        def quantise_h(u):
-            nc.vector.quantize_mx(out=h_w[u][:].bitcast(FP8X4), scales=h_s[u][:], in_=woven_h[u][:])
+        def quantise_h(u, codes):
+            h_w[u] = codes
+            nc.vector.quantize_mx(out=codes[:].bitcast(FP8X4), scales=h_s[u][:], in_=woven_h[u][:])
 
-        def scale_part(u, b, room=None):
-            grouped = ring.tile([P, HALF], BF16, name="end_woven", align_bytes=64, bufs=4) if room is None else room.bitcast(BF16)
+        def scale_part(u, b):
+            grouped = ring.tile([P, HALF], BF16, name="end_woven", align_bytes=64)
             nc.vector.tensor_tensor(
                 out=grouped[:].rearrange("p (j t) -> p j t", t=PACK),
                 in0=part_of(u, zs[u][:, b * HALF : (b + 1) * HALF]),
-                in1=gain_row(units[u][1], P),
+                in1=gains[:, units[u][1], :].unsqueeze(1).to_broadcast([P, P, PACK]),
                 op=MULT,
             )
             cols = slice(b * P, (b + 1) * P)
@@ -351,101 +344,101 @@ def tile_list_argo_cast_check_kernel(
                     stop=(a == R_PASSES - 1 and s == len(tiles) - 1),
                 )
 
+        obs_sb = []
+
         def finish(c, o, width, tiles, bank, room=None):
             j0 = chunks[c][0] + o
             for s in range(0, len(tiles), 2):
                 n = tiles[s]
                 part = obs_sb[n // 2][:, :, j0 : j0 + width]
                 sums = bank[:, s * width : (s + 2) * width].rearrange("p (s j) -> p s j", j=width)
-                res = part if room is None else room[:, s * width : (s + 2) * width].rearrange("p (s j) -> p s j", j=width)
+                res = part if room is None else room[:]
                 nc.vector.tensor_tensor(out=res, in0=part, in1=sums, op=SUBTRACT)
                 nc.sync.dma_start(out=out_rows[:, n : n + 2, j0 : j0 + width], in_=res)
 
         corr_bank = rotation(banks[:4])
         pending = []
 
-        def plan_out(c):
-            width = chunks[c][1]
-            per_bank = HALF // width
-            for n in range(0, N_TILES, per_bank):
-                pending.append((c, tuple(range(n, min(n + per_bank, N_TILES))), corr_bank()))
-
         def put_out(room=None):
             c, tiles, bank = pending.pop(0)
             for a in range(R_PASSES):
-                corr_passes(c, 0, chunks[c][1], tiles, a, bank)
-            finish(c, 0, chunks[c][1], tiles, bank, room)
+                corr_passes(c, 0, QUARTER, tiles, a, bank)
+            finish(c, 0, QUARTER, tiles, bank, room)
 
-        for u in range(6):
+        for u in range(len(units)):
             clim(u)
-        quantise_wd(0, weave_wd(0, "S"), "wd_w0")
-        for u in range(6, 9):
-            clim(u)
-        wd_woven1 = weave_wd(1, "S")
-        wd_woven2 = weave_wd(2, "S")
-        for u in range(9, len(units) - 1):
-            clim(u)
-        quantise_x = [weave_x(c, "S") for c in range(2)]
-        last_work = held([P, 2, HALF], F32, "x_diff0")
-        work.append([last_work[:, b, :] for b in range(2)])
-        clim(len(units) - 1)
-        quantise_x[0]()
-        quantise_wd(1, wd_woven1, "wd_w1")
-        quantise_wd(2, wd_woven2, "wd_w2")
-        late_before = held([P, HALF], F32, "x_woven0")
-        pick_before(PACK - 1, HALF, HALF, late_before[:])
-        last = len(units) - 1
-        lag = 2
-        parts = {}
-        for step in range(last + lag):
-            if step <= last:
-                product(step)
-            if pending and step <= last + 1:
-                put_out(work[min(step, last)][int(step > last)])
-            if step <= last and kinds[step] == "A":
+        for t in range(2):
+            for c in range(3):
+                pick_plane(c, t)
+        woven = weave_wd(0, "G", "g_woven")
+        pick_plane(0, 2)
+        quantise_wd(0, woven)
+        woven = weave_wd(1, "G", "g_woven")
+        pick_plane(1, 2)
+        pick_plane(2, 2)
+        pick_plane(0, 3)
+        quantise_wd(1, woven)
+        woven = weave_chunk(0, "g_woven")
+        wd_woven2 = weave_wd(2, "S", "wd_woven2")
+        for g in range(N_TILES // 2):
+            obs_pair = held([P, 2, S], F32, f"wd_raw{g}")
+            nc.sync.dma_start(out=obs_pair[:], in_=obs_rows[:, 2 * g : 2 * g + 2, :])
+            obs_sb.append(obs_pair)
+        pick_plane(1, 3)
+        pick_plane(2, 3)
+        quantise_x(0, woven, held([P, QUARTER], U32, "x_w0"))
+        x_woven1 = weave_chunk(1, "g_woven")
+        for t in range(2):
+            pick(3, 0, t, late_after[:, t, :])
+        for step in range(last + 1):
+            product(step)
+            if kinds[step] != "D":
                 scale(step)
+            if pending:
+                put_out(in_arena([P, 2, QUARTER], F32, f"res{step}", step, 1))
             if step == 0:
-                quantise_x[1]("work0_1")
-            if step == 1:
-                pick_diff(PACK - 1, HALF, HALF, late_before[:])
+                for t in range(2, 4):
+                    pick(3, 0, t, late_after[:, t, :])
+                quantise_wd(2, wd_woven2, in_arena([P, PASS], U32, "wd_w2late", 0, 1))
+                quantise_x(1, x_woven1, held([P, QUARTER], U32, "x_w1"))
+                x_woven2 = weave_chunk(2, "wd_woven2")
+            if step in (1, 3):
+                for t in range(step - 1, step + 1):
+                    pick(3, 1, t, late_before[:, t, :])
             if step == 2:
-                quantise_x.append(weave_x(2, "V", "work2_1"))
-            if step == 3:
-                quantise_x[2]("work3_1")
+                quantise_x(2, x_woven2, in_arena([P, QUARTER], U32, "x_w2", 2, 0))
+            if step >= 3:
+                quantise_h(step - 3, in_arena([P, QUARTER], U32, f"h_w{step - 3}", step, 0))
             if step == 4:
-                quantise_x.append(weave_x(3, "V", "work4_1"))
+                x_woven3 = in_arena([P, PACK * QUARTER], BF16, "x_woven3", 4, 1)
+                weave_x(nc.vector, x_woven3[:], late_after, late_before[:])
             if step == 5:
-                quantise_x[3]("work5_1")
-            u = step - lag
-            if u >= 0:
-                if kinds[u] == "A":
-                    quantise_h(u)
-                for quantise in parts.get(u, ()):
-                    quantise()
-                if units[u][1] == R_PASSES - 1:
-                    plan_out(units[u][0])
-            u = step - lag + 1
-            if 0 <= u < last and kinds[u] == "D":
-                room = None
-                parts[u] = [
-                    scale_part(u, b, None if room is None else room[:, b * QUARTER : (b + 1) * QUARTER])
-                    for b in banks_of(u)
-                ]
-
-        ends = [(0, (banks[1], banks[4])), (P, (banks[5], banks[6]))]
+                quantise_x(3, x_woven3, in_arena([P, QUARTER], U32, "x_w3", 5, 0, 1024))
+            if step >= 2:
+                u = step - 2
+                weave_h(u, held([P, PACK * QUARTER], BF16, ("g_woven", "wd_woven2")[u % 2]))
+            if step >= 3 and units[step - 3][1] == R_PASSES - 1:
+                for n in range(0, N_TILES, 2):
+                    pending.append((units[step - 3][0], (n, n + 1), corr_bank()))
+        while pending:
+            put_out()
+        quantise_h(last - 2, held([P, QUARTER], U32, "h_w9"))
+        weave_h(last - 1, held([P, PACK * QUARTER], BF16, "last_woven"))
+        h_w[last] = held([P, QUARTER], U32, "h_w11")
+        quantise_end = [scale_part(last, 0)]
+        quantise_h(last - 1, held([P, QUARTER], U32, "h_w10"))
+        quantise_end.append(scale_part(last, 1))
+        ends = [(0, (banks[3], banks[4])), (P, (banks[5], banks[6]))]
         groups = ((0, 1, 2, 3), (4, 5))
         c = len(chunks) - 1
         for a in range(R_PASSES - 1):
             for o, pair in ends:
                 for tiles, bank in zip(groups, pair):
                     corr_passes(c, o, P, tiles, a, bank)
-        quantise_end = [scale_part(last, b) for b in range(2)]
         for (o, pair), quantise in zip(ends, quantise_end):
             quantise()
             for tiles, bank in zip(groups, pair):
                 corr_passes(c, o, P, tiles, R_PASSES - 1, bank)
-        while pending:
-            put_out()
         for o, pair in ends:
             for tiles, bank in zip(groups, pair):
                 finish(c, o, P, tiles, bank)

@@ -68,7 +68,8 @@ def tile_list_argo_cast_check_kernel(
         wo_s = held([P, R_PASSES, N], U8, "wo_s")
         gains = held([P, R_PASSES, PACK], F32, "gains")
         x_planes = [keep.tile([P, T], F32, name="big", bufs=PACK, align_bytes=64) for t in range(PACK)]
-        wd_raw = [held([P, PACK, PASS], F32, f"wd_raw{a}") for a in range(R_PASSES)]
+        wd_raw = [held([P, PACK, PASS], F32, f"wd_raw{a}") for a in (0, 2)]
+        wd_raw.insert(1, arena.tile([P, PACK, PASS], F32, name="wd_raw1", align_bytes=64, offset=4096))
 
         nc.vector.memset(tab_s[:].bitcast(I32), 0)
         nc.vector.memset(wc_s_raw[:].bitcast(I32), 0)
@@ -97,13 +98,13 @@ def tile_list_argo_cast_check_kernel(
         nc.sync.dma_start(out=tab_w[:], in_=tab_words[0].rearrange("p c i -> p (c i)").bitcast(I32))
         load_scale_rows(wc_s_raw, wc_scales[0])
         nc.sync.dma_start(out=list3[:], in_=offs3)
-        nc.sync.dma_start(out=list2[:], in_=offs2)
         load_x(0)
-        load_x(1)
         load_wd(0)
+        load_x(1)
         load_x(2)
-        load_wd(1)
         load_x(3)
+        nc.sync.dma_start(out=list2[:], in_=offs2)
+        load_wd(1)
         load_wd(2)
         nc.sync.dma_start(out=gains[:], in_=gain.rearrange("(a p t) -> p a t", p=P, t=PACK))
         for q in range(4):
@@ -160,40 +161,45 @@ def tile_list_argo_cast_check_kernel(
 
         chunks = [(c * QUARTER, QUARTER) for c in range(S // QUARTER)]
         units = [(c, a) for c in range(len(chunks)) for a in range(R_PASSES)]
-        kinds = "AAAAAAAAAAWD"
+        kinds = "AAAAAAAAWWWD"
         last = len(units) - 1
 
-        def in_arena(shape, dtype, name, u, b, o=0):
-            return arena.tile(shape, dtype, name=name, align_bytes=64, offset=(2 * u + b) * 4 * HALF + o)
+        def in_arena(shape, dtype, name, u, o=0):
+            return arena.tile(shape, dtype, name=name, align_bytes=64, offset=12288 + u * 4 * HALF + o)
 
-        late_before = held([P, PACK, QUARTER], F32, "late_before")
-        first_after = held([P, PACK + 2, QUARTER], F32, "first_after")
-        late_after = first_after[:, 2 : PACK + 2, :]
-        lent = {(0, 0): late_after[:, 2:4, :], (1, 0): late_before[:, 0:2, :], (3, 1): late_before[:, 2:4, :]}
+        first_diff = held([P, PACK, HALF], F32, "first_diff")
+        x_diff = [first_diff[:, :, c * QUARTER : (c + 1) * QUARTER] for c in range(2)]
+        x_diff += [held([P, PACK, HALF + QUARTER * (c - 2)], F32, f"x_diff{c}") for c in range(2, 4)]
+        late = [(2, 2), (2, 3), (3, 0), (3, 1), (3, 2), (3, 3)]
 
         def work_tile(u, b):
-            if (u, b) in lent:
-                return lent[u, b].rearrange("p t j -> p (t j)")
-            return in_arena([P, HALF], F32, f"work{u}_{b}", u, b)
+            if b == 1:
+                return in_arena([P, HALF], F32, f"work{u}_1", u)[:]
+            if 1 <= u <= len(late):
+                c, t = late[u - 1]
+                return x_diff[c][:, t, 0:HALF]
+            return held([P, HALF], F32, f"work{u}_{b}")[:]
 
-        work = [[work_tile(u, b) for b in range(2)] for u in range(len(units))]
+        work = [[work_tile(u, b) for b in range(2)] for u in range(last)]
+        befores = {}
 
-        lists = (list2, list3)
-        picks = {c: [held([P, PACK, QUARTER], F32, f"picks{c}_{i}") for i in range(2)] for c in range(1, 3)}
-        picks[0] = [first_after[:, 0:PACK, :], held([P, PACK, QUARTER], F32, "picks0_1")]
+        def pick_before(c, t, dst):
+            befores[c, t] = dst
+            nc.vector.tensor_copy(out=dst, in_=x_planes[t][:].indirect(entries(list3, *chunks[c])))
 
-        def pick(c, i, t, dst):
-            nc.vector.tensor_copy(out=dst, in_=x_planes[t][:].indirect(entries(lists[i], *chunks[c])))
-
-        def pick_plane(c, t):
-            for i in range(2):
-                pick(c, i, t, picks[c][i][:, t, :])
+        def pick_diff(c, t):
+            nc.vector.tensor_tensor(
+                out=x_diff[c][:, t, 0:QUARTER],
+                in0=x_planes[t][:].indirect(entries(list2, *chunks[c])),
+                in1=befores[c, t],
+                op=SUBTRACT,
+            )
 
         wd_w = [held([P, PASS], U32, f"wd_w{a}") for a in range(R_PASSES)]
         wd_s = [held([P, PASS], U8, f"wd_s{a}") for a in range(R_PASSES)]
 
         def weave_wd(a, engine, slot):
-            grouped = held([P, PACK * PASS], BF16, slot)
+            grouped = arena.tile([P, PACK * PASS], BF16, name=f"wd_woven{a}", align_bytes=64, offset=slot)
             dst = grouped[:].rearrange("p (t m j) -> p m j t", t=PACK, j=PACK)
             src = wd_raw[a][:].rearrange("p j (m t) -> p m j t", t=PACK)
             if engine == "G":
@@ -218,15 +224,14 @@ def tile_list_argo_cast_check_kernel(
         x_w = {}
         x_s = [held([P, QUARTER], U8, f"x_s{c}") for c in range(len(chunks))]
 
-        def weave_x(engine, dst, after, before):
-            engine.tensor_tensor(out=walk_out(dst), in0=walk_in(after), in1=walk_in(before), op=SUBTRACT)
+        def woven_tile(name, c):
+            if c < 2:
+                return arena.tile([P, PACK * QUARTER], BF16, name=name, align_bytes=64, offset=4096 + 2048 * c)
+            return held([P, PACK * QUARTER], BF16, f"x_woven{c}")
 
-        def weave_chunk(c, slot):
-            grouped = held([P, PACK * QUARTER], BF16, slot)
-            for t in range(0, PACK, 2):
-                after, before = (side[:, t : t + 2, :].rearrange("p t j -> p j t") for side in picks[c])
-                dst = grouped[:].rearrange("p (j t) -> p j t", t=PACK)[:, :, t : t + 2]
-                nc.gpsimd.tensor_tensor(out=dst, in0=after, in1=before, op=SUBTRACT)
+        def weave_x(c):
+            grouped = woven_tile(f"x_woven{c}", c)
+            nc.scalar.copy(out=walk_out(grouped[:]), in_=walk_in(x_diff[c][:, :, 0:QUARTER]))
             return grouped
 
         def quantise_x(c, grouped, codes):
@@ -276,7 +281,10 @@ def tile_list_argo_cast_check_kernel(
 
         def product(u):
             c, a = units[u]
-            z = ring.tile([P, PACK * QUARTER], F32, name="z", bufs=2)
+            if u == 8:
+                z = held([P, PACK * QUARTER], F32, "x_woven3")
+            else:
+                z = ring.tile([P, PACK * QUARTER], F32, name="z", bufs=2)
             zs[u] = z
             for b in range(2):
                 bank = drift_bank()
@@ -332,7 +340,7 @@ def tile_list_argo_cast_check_kernel(
             )
 
         def corr_passes(c, o, width, tiles, a, bank):
-            u = R_PASSES * c + a
+            u = units.index((c, a))
             for s, n in enumerate(tiles):
                 nc.tensor.matmul_mx(
                     out=bank[:, s * width : (s + 1) * width],
@@ -365,69 +373,76 @@ def tile_list_argo_cast_check_kernel(
                 corr_passes(c, 0, QUARTER, tiles, a, bank)
             finish(c, 0, QUARTER, tiles, bank, room)
 
-        for u in range(len(units)):
+        for u in range(last):
             clim(u)
+        for t in range(PACK):
+            width = HALF + QUARTER if t < 3 else HALF
+            wide = held([P, width], F32, f"before{t}")
+            nc.vector.tensor_copy(out=wide[:], in_=x_planes[t][:].indirect(entries(list3, 0, width)))
+            befores[0, t] = wide[:, 0:HALF]
+            if t < 3:
+                befores[2, t] = wide[:, HALF:width]
+        quantise_wd(0, weave_wd(0, "G", 0))
+        wd_woven1 = weave_wd(1, "S", 0)
+        for t in range(PACK):
+            nc.vector.tensor_tensor(
+                out=first_diff[:, t, :],
+                in0=x_planes[t][:].indirect(entries(list2, 0, HALF)),
+                in1=befores[0, t],
+                op=SUBTRACT,
+            )
+        x_woven = {c: weave_x(c) for c in range(2)}
         for t in range(2):
-            for c in range(3):
-                pick_plane(c, t)
-        woven = weave_wd(0, "G", "g_woven")
-        pick_plane(0, 2)
-        quantise_wd(0, woven)
-        woven = weave_wd(1, "G", "g_woven")
-        pick_plane(1, 2)
-        pick_plane(2, 2)
-        pick_plane(0, 3)
-        quantise_wd(1, woven)
-        woven = weave_chunk(0, "g_woven")
-        wd_woven2 = weave_wd(2, "S", "wd_woven2")
+            pick_diff(2, t)
+        last_work = held([P, 2, HALF], F32, "first_diff")
+        work.append([last_work[:, b, :] for b in range(2)])
+        clim(last)
+        quantise_wd(1, wd_woven1)
+        quantise_x(0, x_woven[0], held([P, QUARTER], U32, "x_w0"))
+        pick_before(*late[1], arena.tile([P, QUARTER], F32, name="late_before", align_bytes=64, offset=5120)[:])
+        wd_woven2 = weave_wd(2, "G", 1024)
         for g in range(N_TILES // 2):
-            obs_pair = held([P, 2, S], F32, f"wd_raw{g}")
+            obs_pair = held([P, 2, S], F32, ("wd_raw0", "obs1", "wd_raw2")[g])
             nc.sync.dma_start(out=obs_pair[:], in_=obs_rows[:, 2 * g : 2 * g + 2, :])
             obs_sb.append(obs_pair)
-        pick_plane(1, 3)
-        pick_plane(2, 3)
-        quantise_x(0, woven, held([P, QUARTER], U32, "x_w0"))
-        x_woven1 = weave_chunk(1, "g_woven")
-        for t in range(2):
-            pick(3, 0, t, late_after[:, t, :])
+
+
         for step in range(last + 1):
             product(step)
             if kinds[step] != "D":
                 scale(step)
+            if 1 <= step < len(late) - 1:
+                pick_before(*late[step + 1], work[step][0][:, QUARTER:HALF])
+            if step >= 2 and kinds[step - 2] == "W":
+                quantise_h(step - 2, held([P, QUARTER], U32, f"h_w{step - 2}"))
             if pending:
-                put_out(in_arena([P, 2, QUARTER], F32, f"res{step}", step, 1))
-            if step == 0:
-                for t in range(2, 4):
-                    pick(3, 0, t, late_after[:, t, :])
-                quantise_wd(2, wd_woven2, in_arena([P, PASS], U32, "wd_w2late", 0, 1))
-                quantise_x(1, x_woven1, held([P, QUARTER], U32, "x_w1"))
-                x_woven2 = weave_chunk(2, "wd_woven2")
-            if step in (1, 3):
-                for t in range(step - 1, step + 1):
-                    pick(3, 1, t, late_before[:, t, :])
-            if step == 2:
-                quantise_x(2, x_woven2, in_arena([P, QUARTER], U32, "x_w2", 2, 0))
-            if step >= 3:
-                quantise_h(step - 3, in_arena([P, QUARTER], U32, f"h_w{step - 3}", step, 0))
-            if step == 4:
-                x_woven3 = in_arena([P, PACK * QUARTER], BF16, "x_woven3", 4, 1)
-                weave_x(nc.vector, x_woven3[:], late_after, late_before[:])
-            if step == 5:
-                quantise_x(3, x_woven3, in_arena([P, QUARTER], U32, "x_w3", 5, 0, 1024))
-            if step >= 2:
-                u = step - 2
-                weave_h(u, held([P, PACK * QUARTER], BF16, ("g_woven", "wd_woven2")[u % 2]))
-            if step >= 3 and units[step - 3][1] == R_PASSES - 1:
+                room = x_diff[3][:, step - 3, QUARTER:] if step <= len(late) else work[step][0]
+                put_out(room.rearrange("p (g j) -> p g j", g=2))
+            if step == 1:
+                wd_s[2] = in_arena([P, PASS], U8, "wd_s2_late", 1)
+                quantise_wd(2, wd_woven2)
+            if step >= 2 and kinds[step - 2] == "A":
+                quantise_h(step - 2, in_arena([P, QUARTER], U32, f"h_w{step - 2}", step))
+            if step in {1: 1, 4: 2, 7: 3}:
+                c = {1: 1, 4: 2, 7: 3}[step]
+                quantise_x(c, x_woven[c], in_arena([P, QUARTER], U32, f"x_w{c}", step, 1024))
+            if 1 <= step <= len(late):
+                c, t = late[step - 1]
+                pick_diff(c, t)
+                if t == PACK - 1:
+                    x_woven[c] = weave_x(c)
+            u = step - 1
+            if u >= 0 and kinds[u] == "A":
+                weave_h(u, woven_tile(f"h_woven_g{u}", 1 if u < 3 else 2))
+            elif u >= 0:
+                weave_h(u, held([P, PACK * QUARTER], BF16, f"h_woven{u % 2}"))
+            if step >= 2 and units[step - 2][1] == R_PASSES - 1:
                 for n in range(0, N_TILES, 2):
-                    pending.append((units[step - 3][0], (n, n + 1), corr_bank()))
-        while pending:
-            put_out()
-        quantise_h(last - 2, held([P, QUARTER], U32, "h_w9"))
-        weave_h(last - 1, held([P, PACK * QUARTER], BF16, "last_woven"))
+                    pending.append((units[step - 2][0], (n, n + 1), corr_bank()))
         h_w[last] = held([P, QUARTER], U32, "h_w11")
-        quantise_end = [scale_part(last, 0)]
+        put_out()
         quantise_h(last - 1, held([P, QUARTER], U32, "h_w10"))
-        quantise_end.append(scale_part(last, 1))
+        quantise_end = [scale_part(last, b) for b in range(2)]
         ends = [(0, (banks[3], banks[4])), (P, (banks[5], banks[6]))]
         groups = ((0, 1, 2, 3), (4, 5))
         c = len(chunks) - 1
@@ -439,6 +454,7 @@ def tile_list_argo_cast_check_kernel(
             quantise()
             for tiles, bank in zip(groups, pair):
                 corr_passes(c, o, P, tiles, R_PASSES - 1, bank)
+        put_out(held([P, 2, QUARTER], F32, "h_woven0"))
         for o, pair in ends:
             for tiles, bank in zip(groups, pair):
                 finish(c, o, P, tiles, bank)

@@ -27,6 +27,7 @@ HALVES = S // HALF
 QUARTER = 256
 R_PASSES = H // PASS
 N_TILES = N // P
+WORK = 56 * 1024
 
 
 def rotation(items):
@@ -68,8 +69,10 @@ def tile_list_argo_cast_check_kernel(
         wo_s = held([P, R_PASSES, N], U8, "wo_s")
         gains = held([P, R_PASSES, PACK], F32, "gains")
         x_planes = [keep.tile([P, T], F32, name="big", bufs=PACK, align_bytes=64) for t in range(PACK)]
-        wd_raw = [held([P, PACK, PASS], F32, f"wd_raw{a}") for a in (0, 2)]
-        wd_raw.insert(1, arena.tile([P, PACK, PASS], F32, name="wd_raw1", align_bytes=64, offset=4096))
+        def at(shape, dtype, name, kib):
+            return arena.tile(shape, dtype, name=name, align_bytes=64, offset=int(1024 * kib))
+
+        wd_raw = [at([P, PACK, PASS], F32, "wd_raw0", 0), at([P, PACK, PASS], F32, "wd_raw1", 16.25), held([P, PACK, PASS], F32, "wd_raw2")]
 
         nc.vector.memset(tab_s[:].bitcast(I32), 0)
         nc.vector.memset(wc_s_raw[:].bitcast(I32), 0)
@@ -98,12 +101,12 @@ def tile_list_argo_cast_check_kernel(
         nc.sync.dma_start(out=tab_w[:], in_=tab_words[0].rearrange("p c i -> p (c i)").bitcast(I32))
         load_scale_rows(wc_s_raw, wc_scales[0])
         nc.sync.dma_start(out=list3[:], in_=offs3)
+        nc.sync.dma_start(out=list2[:], in_=offs2)
         load_x(0)
         load_wd(0)
         load_x(1)
         load_x(2)
         load_x(3)
-        nc.sync.dma_start(out=list2[:], in_=offs2)
         load_wd(1)
         load_wd(2)
         nc.sync.dma_start(out=gains[:], in_=gain.rearrange("(a p t) -> p a t", p=P, t=PACK))
@@ -161,45 +164,30 @@ def tile_list_argo_cast_check_kernel(
 
         chunks = [(c * QUARTER, QUARTER) for c in range(S // QUARTER)]
         units = [(c, a) for c in range(len(chunks)) for a in range(R_PASSES)]
+        units[2], units[3] = units[3], units[2]
         kinds = "AAAAAAAAWWWD"
         last = len(units) - 1
 
-        def in_arena(shape, dtype, name, u, o=0):
-            return arena.tile(shape, dtype, name=name, align_bytes=64, offset=12288 + u * 4 * HALF + o)
+        def in_arena(shape, dtype, name, u, b, o=0):
+            return arena.tile(shape, dtype, name=name, align_bytes=64, offset=WORK + (2 * u + b) * 4 * HALF + o)
 
-        first_diff = held([P, PACK, HALF], F32, "first_diff")
-        x_diff = [first_diff[:, :, c * QUARTER : (c + 1) * QUARTER] for c in range(2)]
-        x_diff += [held([P, PACK, HALF + QUARTER * (c - 2)], F32, f"x_diff{c}") for c in range(2, 4)]
-        late = [(2, 2), (2, 3), (3, 0), (3, 1), (3, 2), (3, 3)]
+        work = [[in_arena([P, HALF], F32, f"work{u}_{b}", u, b)[:] for b in range(2)] for u in range(len(units))]
+        EARLY = S - QUARTER
+        early_diff = at([P, PACK, EARLY], F32, "early_diff", 0)
+        x_diff = [early_diff[:, :, c * QUARTER : (c + 1) * QUARTER] for c in range(3)]
+        x_diff.append(None)
 
-        def work_tile(u, b):
-            if b == 1:
-                return in_arena([P, HALF], F32, f"work{u}_1", u)[:]
-            if 1 <= u <= len(late):
-                c, t = late[u - 1]
-                return x_diff[c][:, t, 0:HALF]
-            return held([P, HALF], F32, f"work{u}_{b}")[:]
+        def pick(dst, t, lst, j0, width):
+            nc.vector.tensor_copy(out=dst, in_=x_planes[t][:].indirect(entries(lst, j0, width)))
 
-        work = [[work_tile(u, b) for b in range(2)] for u in range(last)]
-        befores = {}
-
-        def pick_before(c, t, dst):
-            befores[c, t] = dst
-            nc.vector.tensor_copy(out=dst, in_=x_planes[t][:].indirect(entries(list3, *chunks[c])))
-
-        def pick_diff(c, t):
-            nc.vector.tensor_tensor(
-                out=x_diff[c][:, t, 0:QUARTER],
-                in0=x_planes[t][:].indirect(entries(list2, *chunks[c])),
-                in1=befores[c, t],
-                op=SUBTRACT,
-            )
+        def subtract(dst, after, before):
+            nc.gpsimd.tensor_tensor(out=dst, in0=after, in1=before, op=SUBTRACT)
 
         wd_w = [held([P, PASS], U32, f"wd_w{a}") for a in range(R_PASSES)]
         wd_s = [held([P, PASS], U8, f"wd_s{a}") for a in range(R_PASSES)]
 
         def weave_wd(a, engine, slot):
-            grouped = arena.tile([P, PACK * PASS], BF16, name=f"wd_woven{a}", align_bytes=64, offset=slot)
+            grouped = at([P, PACK * PASS], BF16, f"wd_woven{a}", slot)
             dst = grouped[:].rearrange("p (t m j) -> p m j t", t=PACK, j=PACK)
             src = wd_raw[a][:].rearrange("p j (m t) -> p m j t", t=PACK)
             if engine == "G":
@@ -224,14 +212,8 @@ def tile_list_argo_cast_check_kernel(
         x_w = {}
         x_s = [held([P, QUARTER], U8, f"x_s{c}") for c in range(len(chunks))]
 
-        def woven_tile(name, c):
-            if c < 2:
-                return arena.tile([P, PACK * QUARTER], BF16, name=name, align_bytes=64, offset=4096 + 2048 * c)
-            return held([P, PACK * QUARTER], BF16, f"x_woven{c}")
-
-        def weave_x(c):
-            grouped = woven_tile(f"x_woven{c}", c)
-            nc.scalar.copy(out=walk_out(grouped[:]), in_=walk_in(x_diff[c][:, :, 0:QUARTER]))
+        def weave_x(c, grouped):
+            nc.scalar.copy(out=walk_out(grouped[:]), in_=walk_in(x_diff[c]))
             return grouped
 
         def quantise_x(c, grouped, codes):
@@ -281,10 +263,7 @@ def tile_list_argo_cast_check_kernel(
 
         def product(u):
             c, a = units[u]
-            if u == 8:
-                z = held([P, PACK * QUARTER], F32, "x_woven3")
-            else:
-                z = ring.tile([P, PACK * QUARTER], F32, name="z", bufs=2)
+            z = ring.tile([P, PACK * QUARTER], F32, name="z", bufs=2)
             zs[u] = z
             for b in range(2):
                 bank = drift_bank()
@@ -373,77 +352,118 @@ def tile_list_argo_cast_check_kernel(
                 corr_passes(c, 0, QUARTER, tiles, a, bank)
             finish(c, 0, QUARTER, tiles, bank, room)
 
-        for u in range(last):
+        for u in range(len(units)):
             clim(u)
-        for t in range(PACK):
-            width = HALF + QUARTER if t < 3 else HALF
-            wide = held([P, width], F32, f"before{t}")
-            nc.vector.tensor_copy(out=wide[:], in_=x_planes[t][:].indirect(entries(list3, 0, width)))
-            befores[0, t] = wide[:, 0:HALF]
-            if t < 3:
-                befores[2, t] = wide[:, HALF:width]
-        quantise_wd(0, weave_wd(0, "G", 0))
-        wd_woven1 = weave_wd(1, "S", 0)
-        for t in range(PACK):
+        wd_woven0 = weave_wd(0, "G", 50)
+        for t in range(PACK - 1):
+            before = at([P, EARLY], F32, f"before{t}", 28 + 3 * t)
+            after = at([P, EARLY], F32, f"after{t}", 40 + 3 * t)
+            pick(before[:], t, list3, 0, EARLY)
+            pick(after[:], t, list2, 0, EARLY)
+            subtract(early_diff[:, t, :], after[:], before[:])
+        t = PACK - 1
+        ends_of_plane = []
+        for j0, width, kib in ((0, QUARTER, 49), (QUARTER, HALF, 37)):
+            before = at([P, width], F32, f"before3_{j0}", kib)
+            pick(before[:], t, list3, j0, width)
+            ends_of_plane.append((j0, width, before))
+        for j0, width, before in ends_of_plane:
             nc.vector.tensor_tensor(
-                out=first_diff[:, t, :],
-                in0=x_planes[t][:].indirect(entries(list2, 0, HALF)),
-                in1=befores[0, t],
+                out=early_diff[:, t, j0 : j0 + width],
+                in0=x_planes[t][:].indirect(entries(list2, j0, width)),
+                in1=before[:],
                 op=SUBTRACT,
             )
-        x_woven = {c: weave_x(c) for c in range(2)}
-        for t in range(2):
-            pick_diff(2, t)
-        last_work = held([P, 2, HALF], F32, "first_diff")
-        work.append([last_work[:, b, :] for b in range(2)])
-        clim(last)
-        quantise_wd(1, wd_woven1)
+        wd_woven1 = weave_wd(1, "S", 12)
+        x_woven = {c: weave_x(c, at([P, PACK * QUARTER], BF16, f"x_woven{c}", (19, 22, 24)[c])) for c in range(3)}
+        for a, grouped in enumerate((wd_woven0, wd_woven1)):
+            wd_s[a] = arena.tile([P, PASS], U8, name=f"wd_s_late{a}", align_bytes=64, offset=49 * 1024 + PASS * a)
+            quantise_wd(a, grouped)
         quantise_x(0, x_woven[0], held([P, QUARTER], U32, "x_w0"))
-        pick_before(*late[1], arena.tile([P, QUARTER], F32, name="late_before", align_bytes=64, offset=5120)[:])
-        wd_woven2 = weave_wd(2, "G", 1024)
-        for g in range(N_TILES // 2):
-            obs_pair = held([P, 2, S], F32, ("wd_raw0", "obs1", "wd_raw2")[g])
+        wd_woven2 = weave_wd(2, "G", 15.5)
+        for obs_pair in (at([P, 2, S], F32, "obs0", 28), at([P, 2, S], F32, "obs1", 40), held([P, 2, S], F32, "wd_raw2")):
+            g = len(obs_sb)
             nc.sync.dma_start(out=obs_pair[:], in_=obs_rows[:, 2 * g : 2 * g + 2, :])
             obs_sb.append(obs_pair)
 
+        def pick_pair(pair, lst, first):
+            for i in range(2):
+                pick(pair[:, i, :], first + i, lst, EARLY, QUARTER)
+            return pair
 
+        def codes(name, step, o=0):
+            return in_arena([P, QUARTER], U32, name, step, 1, o)
+
+        def gain_on_vector(u, grouped):
+            woven_h[u] = grouped
+            for b in range(2):
+                cols = slice(b * HALF, (b + 1) * HALF)
+                nc.vector.tensor_tensor(
+                    out=part_of(u, grouped[:, cols]),
+                    in0=part_of(u, zs[u][:, cols]),
+                    in1=gains[:, units[u][1], :].unsqueeze(1).to_broadcast([P, P, PACK]),
+                    op=MULT,
+                )
+
+        before01 = pick_pair(at([P, 2, QUARTER], F32, "before01", 20), list3, 0)
         for step in range(last + 1):
             product(step)
             if kinds[step] != "D":
                 scale(step)
-            if 1 <= step < len(late) - 1:
-                pick_before(*late[step + 1], work[step][0][:, QUARTER:HALF])
-            if step >= 2 and kinds[step - 2] == "W":
-                quantise_h(step - 2, held([P, QUARTER], U32, f"h_w{step - 2}"))
+            done = [step - 2] if step >= 10 else []
+            for u in done:
+                quantise_h(u, held([P, QUARTER], U32, f"h_w{u}"))
             if pending:
-                room = x_diff[3][:, step - 3, QUARTER:] if step <= len(late) else work[step][0]
-                put_out(room.rearrange("p (g j) -> p g j", g=2))
+                put_out(work[step][0].rearrange("p (g j) -> p g j", g=2))
+            if step == 8:
+                put_out(work[step][1].rearrange("p (g j) -> p g j", g=2))
+            if step == 0:
+                after01 = pick_pair(in_arena([P, 2, QUARTER], F32, "after01", 0, 0), list2, 0)
             if step == 1:
-                wd_s[2] = in_arena([P, PASS], U8, "wd_s2_late", 1)
+                quantise_x(1, x_woven[1], codes("x_w1", 1, 1024))
+                wd_s[2] = in_arena([P, PASS], U8, "wd_s_late2", 1, 1)
                 quantise_wd(2, wd_woven2)
-            if step >= 2 and kinds[step - 2] == "A":
-                quantise_h(step - 2, in_arena([P, QUARTER], U32, f"h_w{step - 2}", step))
-            if step in {1: 1, 4: 2, 7: 3}:
-                c = {1: 1, 4: 2, 7: 3}[step]
-                quantise_x(c, x_woven[c], in_arena([P, QUARTER], U32, f"x_w{c}", step, 1024))
-            if 1 <= step <= len(late):
-                c, t = late[step - 1]
-                pick_diff(c, t)
-                if t == PACK - 1:
-                    x_woven[c] = weave_x(c)
-            u = step - 1
-            if u >= 0 and kinds[u] == "A":
-                weave_h(u, woven_tile(f"h_woven_g{u}", 1 if u < 3 else 2))
-            elif u >= 0:
-                weave_h(u, held([P, PACK * QUARTER], BF16, f"h_woven{u % 2}"))
-            if step >= 2 and units[step - 2][1] == R_PASSES - 1:
-                for n in range(0, N_TILES, 2):
-                    pending.append((units[step - 2][0], (n, n + 1), corr_bank()))
+                pair = at([P, 2 * PACK * QUARTER], BF16, "pair0", 16)
+                weave_h(0, pair[:, 0 : PACK * QUARTER])
+                late_diff = at([P, PACK, QUARTER], F32, "late_diff", 12)
+                x_diff[3] = late_diff[:]
+                subtract(late_diff[:, 0:2, :], after01[:], before01[:])
+            if step == 2:
+                before23 = pick_pair(in_arena([P, 2, QUARTER], F32, "before23", 2, 0), list3, 2)
+                weave_h(1, pair[:, PACK * QUARTER :])
+            if step == 3:
+                after23 = pick_pair(in_arena([P, 2, QUARTER], F32, "after23", 3, 0), list2, 2)
+                subtract(late_diff[:, 2:4, :], after23[:], before23[:])
+            if step == 4:
+                x_woven[3] = weave_x(3, at([P, PACK * QUARTER], BF16, "x_woven3", 54))
+            if step in {3: 2, 7: 3}:
+                c = {3: 2, 7: 3}[step]
+                x_s[c] = in_arena([P, QUARTER], U8, f"x_s_late{c}", step, 1, 1536)
+                quantise_x(c, x_woven[c], held([P, QUARTER], U32, f"x_w{c}"))
+            if step in (3, 5, 7, 9):
+                pair_w = held([P, HALF], U32, f"pair_w{step}")
+                pair_s = in_arena([P, HALF], U8, f"pair_s{step}", step, 1)
+                nc.vector.quantize_mx(out=pair_w[:].bitcast(FP8X4), scales=pair_s[:], in_=pair[:])
+                for i in range(2):
+                    cols = slice(i * QUARTER, (i + 1) * QUARTER)
+                    h_w[step - 3 + i], h_s[step - 3 + i] = pair_w[:, cols], pair_s[:, cols]
+                    done.append(step - 3 + i)
+                pair = at([P, 2 * PACK * QUARTER], BF16, f"pair{step}", 16)
+                weave_h(step - 1, pair[:, 0 : PACK * QUARTER])
+            if step in (4, 6, 8):
+                weave_h(step - 1, pair[:, PACK * QUARTER :])
+            if step >= 10:
+                weave_h(step - 1, held([P, PACK * QUARTER], BF16, f"h_woven{step % 2}"))
+            for u in done:
+                if units[u][1] == R_PASSES - 1:
+                    for n in range(0, N_TILES, 2):
+                        pending.append((units[u][0], (n, n + 1), corr_bank()))
         h_w[last] = held([P, QUARTER], U32, "h_w11")
-        put_out()
+        while len(pending) > 1:
+            put_out()
         quantise_h(last - 1, held([P, QUARTER], U32, "h_w10"))
         quantise_end = [scale_part(last, b) for b in range(2)]
-        ends = [(0, (banks[3], banks[4])), (P, (banks[5], banks[6]))]
+        ends = [(0, (banks[1], banks[4])), (P, (banks[5], banks[6]))]
         groups = ((0, 1, 2, 3), (4, 5))
         c = len(chunks) - 1
         for a in range(R_PASSES - 1):
@@ -454,7 +474,7 @@ def tile_list_argo_cast_check_kernel(
             quantise()
             for tiles, bank in zip(groups, pair):
                 corr_passes(c, o, P, tiles, R_PASSES - 1, bank)
-        put_out(held([P, 2, QUARTER], F32, "h_woven0"))
+        put_out(held([P, 2, QUARTER], F32, "h_woven1"))
         for o, pair in ends:
             for tiles, bank in zip(groups, pair):
                 finish(c, o, P, tiles, bank)

@@ -136,7 +136,7 @@ def tile_list_argo_cast_check_kernel(
         v_w0 = held([P, 512], U32, "v_w0")
         v_s0 = held([P, 512], U8, "v_s0")
         v_w1 = placed.tile([P, S - 512], U32, name="v_w1", align_bytes=64, offset=0)
-        v_s1 = placed.tile([P, S - 512], U8, name="v_s1", align_bytes=64, offset=4 * (S - 512))
+        v_s1 = held([P, S - 512], U8, "v_s1")
 
         def span_of(j0):
             h = int(j0 >= 512)
@@ -165,17 +165,25 @@ def tile_list_argo_cast_check_kernel(
         chunks = [(c * QUARTER, QUARTER) for c in range(S // QUARTER)]
         units = [(c, a) for c in range(len(chunks)) for a in range(R_PASSES)]
         units[2], units[3] = units[3], units[2]
-        kinds = "AAAAAAAAWWWD"
+        kinds = "AAAAAAAAWWWE"
         last = len(units) - 1
 
         def in_arena(shape, dtype, name, u, b, o=0):
             return arena.tile(shape, dtype, name=name, align_bytes=64, offset=WORK + (2 * u + b) * 4 * HALF + o)
 
-        work = [[in_arena([P, HALF], F32, f"work{u}_{b}", u, b)[:] for b in range(2)] for u in range(len(units))]
+        first_diff = at([P, PACK, HALF], F32, "first_diff", 2)
+        x_diff = [first_diff[:, :, c * QUARTER : (c + 1) * QUARTER] for c in range(2)]
+        x_diff += [held([P, PACK, QUARTER], F32, f"late_diff{c}")[:] for c in (2, 3)]
+        late = {1: (2, 2), 3: (3, 0), 5: (3, 2)}
+
+        def work_tile(u, b):
+            if u in late and b == int(u == 1):
+                c, t = late[u]
+                return x_diff[c][:, t : t + 2, :].rearrange("p t j -> p (t j)")
+            return in_arena([P, HALF], F32, f"work{u}_{b}", u, b)[:]
+
+        work = [[work_tile(u, b) for b in range(2)] for u in range(last - 1)]
         EARLY = S - QUARTER
-        early_diff = at([P, PACK, EARLY], F32, "early_diff", 0)
-        x_diff = [early_diff[:, :, c * QUARTER : (c + 1) * QUARTER] for c in range(3)]
-        x_diff.append(None)
 
         def pick(dst, t, lst, j0, width):
             nc.vector.tensor_copy(out=dst, in_=x_planes[t][:].indirect(entries(lst, j0, width)))
@@ -244,7 +252,7 @@ def tile_list_argo_cast_check_kernel(
                 return cols
             return cols.rearrange("p (j t) -> p j t", t=PACK)
 
-        clim_bank = rotation(banks)
+        clim_bank = rotation(banks[4:] + banks[:4])
 
         def clim(u):
             c, a = units[u]
@@ -306,14 +314,15 @@ def tile_list_argo_cast_check_kernel(
             nc.vector.quantize_mx(out=codes[:].bitcast(FP8X4), scales=h_s[u][:], in_=woven_h[u][:])
 
         def scale_part(u, b):
-            grouped = ring.tile([P, HALF], BF16, name="end_woven", align_bytes=64)
-            nc.vector.tensor_tensor(
-                out=grouped[:].rearrange("p (j t) -> p j t", t=PACK),
-                in0=part_of(u, zs[u][:, b * HALF : (b + 1) * HALF]),
-                in1=gains[:, units[u][1], :].unsqueeze(1).to_broadcast([P, P, PACK]),
-                op=MULT,
-            )
             cols = slice(b * P, (b + 1) * P)
+            tanh_planes = zs[u][:].rearrange("p (t j) -> p t j", t=PACK)
+            planes = ring.tile([P, PACK, P], BF16, name="end_planes")
+            grouped = ring.tile([P, HALF], BF16, name="end_woven", align_bytes=64)
+            for t in range(PACK):
+                nc.scalar.activation(
+                    out=planes[:, t, :], in_=tanh_planes[:, t, cols], func=COPY, scale=gains[:, units[u][1], t : t + 1]
+                )
+            nc.vector.tensor_copy(out=walk_out(grouped[:]), in_=walk_in(planes[:]))
             return lambda: nc.vector.quantize_mx(
                 out=h_w[u][:, cols].bitcast(FP8X4), scales=h_s[u][:, cols], in_=grouped[:]
             )
@@ -352,30 +361,45 @@ def tile_list_argo_cast_check_kernel(
                 corr_passes(c, 0, QUARTER, tiles, a, bank)
             finish(c, 0, QUARTER, tiles, bank, room)
 
-        for u in range(len(units)):
+        for u in range(last - 1):
             clim(u)
         wd_woven0 = weave_wd(0, "G", 50)
+        third_before = at([P, 2, QUARTER], F32, "third_before", 10)
+        third_after = at([P, 2, QUARTER], F32, "third_after", 46)
         for t in range(PACK - 1):
-            before = at([P, EARLY], F32, f"before{t}", 28 + 3 * t)
-            after = at([P, EARLY], F32, f"after{t}", 40 + 3 * t)
-            pick(before[:], t, list3, 0, EARLY)
-            pick(after[:], t, list2, 0, EARLY)
-            subtract(early_diff[:, t, :], after[:], before[:])
+            before = at([P, HALF], F32, f"before{t}", 28 + 2 * t)
+            if t == 0:
+                after = x_diff[2][:, 0:2, :].rearrange("p t j -> p (t j)")
+            else:
+                after = at([P, HALF], F32, f"after{t}", 40 + 2 * t)[:]
+            pick(before[:], t, list3, 0, HALF)
+            pick(after, t, list2, 0, HALF)
+            subtract(first_diff[:, t, :], after, before[:])
+            if t < 2:
+                pick(third_before[:, t, :], t, list3, HALF, QUARTER)
+            if t == 1:
+                for i in range(2):
+                    pick(third_after[:, i, :], i, list2, HALF, QUARTER)
+                subtract(x_diff[2][:, 0:2, :], third_after[:], third_before[:])
         t = PACK - 1
         ends_of_plane = []
-        for j0, width, kib in ((0, QUARTER, 49), (QUARTER, HALF, 37)):
+        for j0, width, kib in ((0, QUARTER, 49), (QUARTER, QUARTER, 37)):
             before = at([P, width], F32, f"before3_{j0}", kib)
             pick(before[:], t, list3, j0, width)
             ends_of_plane.append((j0, width, before))
         for j0, width, before in ends_of_plane:
             nc.vector.tensor_tensor(
-                out=early_diff[:, t, j0 : j0 + width],
+                out=first_diff[:, t, j0 : j0 + width],
                 in0=x_planes[t][:].indirect(entries(list2, j0, width)),
                 in1=before[:],
                 op=SUBTRACT,
             )
         wd_woven1 = weave_wd(1, "S", 12)
-        x_woven = {c: weave_x(c, at([P, PACK * QUARTER], BF16, f"x_woven{c}", (19, 22, 24)[c])) for c in range(3)}
+        x_woven = {c: weave_x(c, at([P, PACK * QUARTER], BF16, f"x_woven{c}", (19, 22)[c])) for c in range(2)}
+        for i in range(2):
+            last_work = at([P, 2, HALF], F32, f"last_work{i}", 2 + 4 * i)
+            work.append([last_work[:, b, :] for b in range(2)])
+            clim(last - 1 + i)
         for a, grouped in enumerate((wd_woven0, wd_woven1)):
             wd_s[a] = arena.tile([P, PASS], U8, name=f"wd_s_late{a}", align_bytes=64, offset=49 * 1024 + PASS * a)
             quantise_wd(a, grouped)
@@ -386,10 +410,21 @@ def tile_list_argo_cast_check_kernel(
             nc.sync.dma_start(out=obs_pair[:], in_=obs_rows[:, 2 * g : 2 * g + 2, :])
             obs_sb.append(obs_pair)
 
-        def pick_pair(pair, lst, first):
+        befores = {}
+
+        def pick_befores(c, first, pair):
             for i in range(2):
-                pick(pair[:, i, :], first + i, lst, EARLY, QUARTER)
-            return pair
+                pick(pair[:, i, :], first + i, list3, *chunks[c])
+            befores[c, first] = pair
+
+        def pick_diffs(c, first):
+            for i in range(2):
+                nc.vector.tensor_tensor(
+                    out=x_diff[c][:, first + i, :],
+                    in0=x_planes[first + i][:].indirect(entries(list2, *chunks[c])),
+                    in1=befores[c, first][:, i, :],
+                    op=SUBTRACT,
+                )
 
         def codes(name, step, o=0):
             return in_arena([P, QUARTER], U32, name, step, 1, o)
@@ -405,10 +440,10 @@ def tile_list_argo_cast_check_kernel(
                     op=MULT,
                 )
 
-        before01 = pick_pair(at([P, 2, QUARTER], F32, "before01", 20), list3, 0)
+        pick_befores(2, 2, at([P, 2, QUARTER], F32, "before_late0", 20))
         for step in range(last + 1):
             product(step)
-            if kinds[step] != "D":
+            if step < last:
                 scale(step)
             done = [step - 2] if step >= 10 else []
             for u in done:
@@ -417,25 +452,24 @@ def tile_list_argo_cast_check_kernel(
                 put_out(work[step][0].rearrange("p (g j) -> p g j", g=2))
             if step == 8:
                 put_out(work[step][1].rearrange("p (g j) -> p g j", g=2))
-            if step == 0:
-                after01 = pick_pair(in_arena([P, 2, QUARTER], F32, "after01", 0, 0), list2, 0)
-            if step == 1:
-                quantise_x(1, x_woven[1], codes("x_w1", 1, 1024))
-                wd_s[2] = in_arena([P, PASS], U8, "wd_s_late2", 1, 1)
-                quantise_wd(2, wd_woven2)
-                pair = at([P, 2 * PACK * QUARTER], BF16, "pair0", 16)
-                weave_h(0, pair[:, 0 : PACK * QUARTER])
-                late_diff = at([P, PACK, QUARTER], F32, "late_diff", 12)
-                x_diff[3] = late_diff[:]
-                subtract(late_diff[:, 0:2, :], after01[:], before01[:])
             if step == 2:
-                before23 = pick_pair(in_arena([P, 2, QUARTER], F32, "before23", 2, 0), list3, 2)
-                weave_h(1, pair[:, PACK * QUARTER :])
-            if step == 3:
-                after23 = pick_pair(in_arena([P, 2, QUARTER], F32, "after23", 3, 0), list2, 2)
-                subtract(late_diff[:, 2:4, :], after23[:], before23[:])
+                pick_befores(3, 0, in_arena([P, 2, QUARTER], F32, "before_late1", 2, 0))
             if step == 4:
-                x_woven[3] = weave_x(3, at([P, PACK * QUARTER], BF16, "x_woven3", 54))
+                pick_befores(3, 2, in_arena([P, 2, QUARTER], F32, "before_late2", 4, 0))
+            if step == 1:
+                quantise_x(1, x_woven[1], in_arena([P, QUARTER], U32, "x_w1", 1, 0, 1024))
+                wd_s[2] = in_arena([P, PASS], U8, "wd_s_late2", 1, 0)
+                quantise_wd(2, wd_woven2)
+            if step in late:
+                pick_diffs(*late[step])
+            if step == 1:
+                pair = at([P, 2 * PACK * QUARTER], BF16, "pair0", 17)
+                weave_h(0, pair[:, 0 : PACK * QUARTER])
+            if step == 2:
+                weave_h(1, pair[:, PACK * QUARTER :])
+            if step in (1, 5):
+                c = 2 + step // 4
+                x_woven[c] = weave_x(c, at([P, PACK * QUARTER], BF16, f"x_woven{c}", 20 + 2 * c))
             if step in {3: 2, 7: 3}:
                 c = {3: 2, 7: 3}[step]
                 x_s[c] = in_arena([P, QUARTER], U8, f"x_s_late{c}", step, 1, 1536)
@@ -448,7 +482,7 @@ def tile_list_argo_cast_check_kernel(
                     cols = slice(i * QUARTER, (i + 1) * QUARTER)
                     h_w[step - 3 + i], h_s[step - 3 + i] = pair_w[:, cols], pair_s[:, cols]
                     done.append(step - 3 + i)
-                pair = at([P, 2 * PACK * QUARTER], BF16, f"pair{step}", 16)
+                pair = at([P, 2 * PACK * QUARTER], BF16, f"pair{step}", 17)
                 weave_h(step - 1, pair[:, 0 : PACK * QUARTER])
             if step in (4, 6, 8):
                 weave_h(step - 1, pair[:, PACK * QUARTER :])
@@ -474,7 +508,7 @@ def tile_list_argo_cast_check_kernel(
             quantise()
             for tiles, bank in zip(groups, pair):
                 corr_passes(c, o, P, tiles, R_PASSES - 1, bank)
-        put_out(held([P, 2, QUARTER], F32, "h_woven1"))
+        put_out(ring.tile([P, 2, QUARTER], F32, name="end_woven", align_bytes=64))
         for o, pair in ends:
             for tiles, bank in zip(groups, pair):
                 finish(c, o, P, tiles, bank)

@@ -22,12 +22,33 @@ TANH = mybir.ActivationFunctionType.Tanh
 P = 128
 PACK = 4
 PASS = P * PACK
-HALF = 512
-HALVES = S // HALF
-QUARTER = 256
+BANK = 512
+HALF = S // 2
+CHUNK = S // 4
+UNIT = PACK * CHUNK
 R_PASSES = H // PASS
 N_TILES = N // P
-WORK = 56 * 1024
+KIB = 1024
+
+WD_RAW0 = 0
+FIRST_DIFF = 2 * KIB
+LAST_CLIM = FIRST_DIFF
+THIRD_BEFORE = 10 * KIB
+WD_WOVEN1 = 12 * KIB
+WD_WOVEN2 = 15 * KIB + 512
+WD_RAW1 = 16 * KIB + 256
+H_PAIR = 17 * KIB
+X_WOVEN = (19 * KIB, 22 * KIB, 24 * KIB, 26 * KIB)
+LATE_BEFORE = 20 * KIB
+BEFORE = 28 * KIB
+OBS0 = BEFORE
+LAST_BEFORE = (49 * KIB, 37 * KIB)
+WD_SCALES = LAST_BEFORE[0]
+AFTER = 40 * KIB
+OBS1 = AFTER
+THIRD_AFTER = 46 * KIB
+WD_WOVEN0 = 50 * KIB
+CLIM = 56 * KIB
 
 
 def rotation(items):
@@ -54,7 +75,13 @@ def tile_list_argo_cast_check_kernel(
         def held(shape, dtype, name):
             return keep.tile(shape, dtype, name=name, align_bytes=64)
 
-        banks = [psum.tile([P, HALF], F32, name=f"bank{b}") for b in range(8)]
+        def at(shape, dtype, name, offset):
+            return arena.tile(shape, dtype, name=name, align_bytes=64, offset=offset)
+
+        def on_clim(shape, dtype, name, u, b, offset=0):
+            return at(shape, dtype, name, CLIM + (2 * u + b) * 4 * BANK + offset)
+
+        banks = [psum.tile([P, BANK], F32, name=f"bank{b}") for b in range(8)]
 
         list1 = keep.tile([P, S // 16], U16, name="list1")
         list2 = keep.tile([P, S // 16], U16, name="list2")
@@ -62,17 +89,18 @@ def tile_list_argo_cast_check_kernel(
         tab_w = held([P, T], I32, "tab_w")
         tab_s = held([P, T], U8, "tab_s")
         wc_w_raw = held([P, 2 * H], U8, "wc_w_raw")
-        wc_s_raw = placed.tile([P, H], U8, name="wc_s_raw", align_bytes=64, offset=4 * (S - 512) - 512)
+        wc_s_raw = placed.tile([P, H], U8, name="wc_s_raw", align_bytes=64, offset=4 * HALF - 512)
         wc_w = [held([P, 2 * PASS], U8, f"wc_w{a}") for a in range(R_PASSES)]
         wc_s = [held([P, PASS], U8, f"wc_s{a}") for a in range(R_PASSES)]
         wo_w = held([P, R_PASSES, N], I32, "wo_w")
         wo_s = held([P, R_PASSES, N], U8, "wo_s")
         gains = held([P, R_PASSES, PACK], F32, "gains")
-        x_planes = [keep.tile([P, T], F32, name="big", bufs=PACK, align_bytes=64) for t in range(PACK)]
-        def at(shape, dtype, name, kib):
-            return arena.tile(shape, dtype, name=name, align_bytes=64, offset=int(1024 * kib))
-
-        wd_raw = [at([P, PACK, PASS], F32, "wd_raw0", 0), at([P, PACK, PASS], F32, "wd_raw1", 16.25), held([P, PACK, PASS], F32, "wd_raw2")]
+        x_planes = [keep.tile([P, T], F32, name="x_plane", bufs=PACK, align_bytes=64) for t in range(PACK)]
+        wd_raw = [
+            at([P, PACK, PASS], F32, "wd_raw0", WD_RAW0),
+            at([P, PACK, PASS], F32, "wd_raw1", WD_RAW1),
+            held([P, PACK, PASS], F32, "wd_raw2"),
+        ]
 
         nc.vector.memset(tab_s[:].bitcast(I32), 0)
         nc.vector.memset(wc_s_raw[:].bitcast(I32), 0)
@@ -80,6 +108,8 @@ def tile_list_argo_cast_check_kernel(
 
         x_rows = xT.rearrange("(p t) c -> p t c", t=PACK)
         wd_rows = wd.rearrange("(p j) c -> p j c", j=PACK)
+        obs_rows = obs.rearrange("(n p) j -> p n j", p=P)
+        out_rows = out.rearrange("(n p) j -> p n j", p=P)
 
         def load_scale_rows(tile, rows):
             for q in range(4):
@@ -93,8 +123,6 @@ def tile_list_argo_cast_check_kernel(
         def load_wd(a):
             nc.sync.dma_start(out=wd_raw[a][:], in_=wd_rows[:, :, a * PASS : (a + 1) * PASS])
 
-        obs_rows = obs.rearrange("(n p) j -> p n j", p=P)
-        out_rows = out.rearrange("(n p) j -> p n j", p=P)
         nc.sync.dma_start(out=wc_w_raw[:].bitcast(I32), in_=wc_words[0].bitcast(I32))
         load_scale_rows(tab_s, tab_scales[0])
         nc.sync.dma_start(out=list1[:], in_=offs)
@@ -104,11 +132,10 @@ def tile_list_argo_cast_check_kernel(
         nc.sync.dma_start(out=list2[:], in_=offs2)
         load_x(0)
         load_wd(0)
-        load_x(1)
-        load_x(2)
-        load_x(3)
-        load_wd(1)
-        load_wd(2)
+        for t in range(1, PACK):
+            load_x(t)
+        for a in range(1, R_PASSES):
+            load_wd(a)
         nc.sync.dma_start(out=gains[:], in_=gain.rearrange("(a p t) -> p a t", p=P, t=PACK))
         for q in range(4):
             nc.sync.dma_start(
@@ -132,84 +159,81 @@ def tile_list_argo_cast_check_kernel(
         def entries(lst, j0, width):
             return lst[:, j0 // 16 : (j0 + width) // 16]
 
-        spans = ((0, 512), (512, S - 512))
-        v_w0 = held([P, 512], U32, "v_w0")
-        v_s0 = held([P, 512], U8, "v_s0")
-        v_w1 = placed.tile([P, S - 512], U32, name="v_w1", align_bytes=64, offset=0)
-        v_s1 = held([P, S - 512], U8, "v_s1")
+        v_w0 = held([P, HALF], U32, "v_w0")
+        v_s0 = held([P, HALF], U8, "v_s0")
+        v_w = (v_w0, placed.tile([P, HALF], U32, name="v_w1", align_bytes=64, offset=0))
+        v_s = (v_s0, held([P, HALF], U8, "v_s1"))
 
-        def span_of(j0):
-            h = int(j0 >= 512)
-            return h, j0 - spans[h][0]
+        def pick_words(half):
+            nc.vector.tensor_copy(out=v_w[half][:], in_=tab_w[:].bitcast(U32).indirect(entries(list1, half * HALF, HALF)))
 
-        def table_columns(j0, width):
-            h, o = span_of(j0)
-            return (v_w0, v_w1)[h][:, o : o + width], (v_s0, v_s1)[h][:, o : o + width]
-
-        def pick_words(dst, j0, width):
-            nc.vector.tensor_copy(out=dst[:], in_=tab_w[:].bitcast(U32).indirect(entries(list1, j0, width)))
-
-        def pick_scales(dst, j0, width):
-            nc.vector.tensor_copy(out=dst[:], in_=tab_s[:].indirect(entries(list1, j0, width)))
+        def pick_scales(half):
+            nc.vector.tensor_copy(out=v_s[half][:], in_=tab_s[:].indirect(entries(list1, half * HALF, HALF)))
 
         deal_words(0)
-        pick_scales(v_s0, *spans[0])
-        pick_words(v_w0, *spans[0])
+        pick_scales(0)
+        pick_words(0)
         deal_scales(0)
         for a in range(1, R_PASSES):
             deal_words(a)
             deal_scales(a)
-        pick_words(v_w1, *spans[1])
-        pick_scales(v_s1, *spans[1])
+        pick_words(1)
+        pick_scales(1)
 
-        chunks = [(c * QUARTER, QUARTER) for c in range(S // QUARTER)]
-        units = [(c, a) for c in range(len(chunks)) for a in range(R_PASSES)]
+        units = [(c, a) for c in range(S // CHUNK) for a in range(R_PASSES)]
         units[2], units[3] = units[3], units[2]
-        kinds = "AAAAAAAAWWWE"
         last = len(units) - 1
+        paired = 8
 
-        def in_arena(shape, dtype, name, u, b, o=0):
-            return arena.tile(shape, dtype, name=name, align_bytes=64, offset=WORK + (2 * u + b) * 4 * HALF + o)
-
-        first_diff = at([P, PACK, HALF], F32, "first_diff", 2)
-        x_diff = [first_diff[:, :, c * QUARTER : (c + 1) * QUARTER] for c in range(2)]
-        x_diff += [held([P, PACK, QUARTER], F32, f"late_diff{c}")[:] for c in (2, 3)]
+        first_diff = at([P, PACK, HALF], F32, "first_diff", FIRST_DIFF)
+        x_diff = [first_diff[:, :, c * CHUNK : (c + 1) * CHUNK] for c in range(2)]
+        x_diff += [held([P, PACK, CHUNK], F32, f"late_diff{c}")[:] for c in (2, 3)]
         late = {1: (2, 2), 3: (3, 0), 5: (3, 2)}
 
-        def work_tile(u, b):
+        def clim_tile(u, b):
             if u in late and b == int(u == 1):
                 c, t = late[u]
                 return x_diff[c][:, t : t + 2, :].rearrange("p t j -> p (t j)")
-            return in_arena([P, HALF], F32, f"work{u}_{b}", u, b)[:]
+            return on_clim([P, BANK], F32, f"clim{u}_{b}", u, b)[:]
 
-        work = [[work_tile(u, b) for b in range(2)] for u in range(last - 1)]
-        EARLY = S - QUARTER
+        clim_sb = [[clim_tile(u, b) for b in range(2)] for u in range(last - 1)]
 
         def pick(dst, t, lst, j0, width):
             nc.vector.tensor_copy(out=dst, in_=x_planes[t][:].indirect(entries(lst, j0, width)))
 
+        def pick_diff(c, t, before):
+            nc.vector.tensor_tensor(
+                out=x_diff[c][:, t, :],
+                in0=x_planes[t][:].indirect(entries(list2, c * CHUNK, CHUNK)),
+                in1=before,
+                op=SUBTRACT,
+            )
+
         def subtract(dst, after, before):
             nc.gpsimd.tensor_tensor(out=dst, in0=after, in1=before, op=SUBTRACT)
 
+        def gpsimd_copy(dst, src):
+            nc.gpsimd.tensor_scalar(out=dst, in0=src, scalar1=1.0, scalar2=0.0, op0=MULT, op1=ADD)
+
+        def quantise(codes, scales, woven):
+            nc.vector.quantize_mx(out=codes.bitcast(FP8X4), scales=scales, in_=woven)
+
         wd_w = [held([P, PASS], U32, f"wd_w{a}") for a in range(R_PASSES)]
-        wd_s = [held([P, PASS], U8, f"wd_s{a}") for a in range(R_PASSES)]
+        wd_s = {}
 
-        def weave_wd(a, engine, slot):
-            grouped = at([P, PACK * PASS], BF16, f"wd_woven{a}", slot)
-            dst = grouped[:].rearrange("p (t m j) -> p m j t", t=PACK, j=PACK)
-            src = wd_raw[a][:].rearrange("p j (m t) -> p m j t", t=PACK)
-            if engine == "G":
-                dst = grouped[:].rearrange("p (t m j) -> p m t j", t=PACK, j=PACK)
-                src = wd_raw[a][:].rearrange("p j (m t) -> p m t j", t=PACK)
-                nc.gpsimd.tensor_scalar(out=dst, in0=src, scalar1=1.0, scalar2=0.0, op0=MULT, op1=ADD)
-            else:
-                nc.scalar.copy(out=dst, in_=src)
-            return grouped
+        def wd_views(a, offset, walk):
+            woven = at([P, PACK * PASS], BF16, f"wd_woven{a}", offset)
+            dst = woven[:].rearrange(f"p (t m j) -> p {walk}", t=PACK, j=PACK)
+            return woven, dst, wd_raw[a][:].rearrange(f"p j (m t) -> p {walk}", t=PACK)
 
-        def quantise_wd(a, grouped, codes=None):
-            if codes is not None:
-                wd_w[a] = codes
-            nc.vector.quantize_mx(out=wd_w[a][:].bitcast(FP8X4), scales=wd_s[a][:], in_=grouped[:])
+        def weave_wd_on_gpsimd(a, offset):
+            woven, dst, src = wd_views(a, offset, "m t j")
+            gpsimd_copy(dst, src)
+            return woven
+
+        def quantise_wd(a, woven, scales):
+            wd_s[a] = scales
+            quantise(wd_w[a][:], scales[:], woven[:])
 
         def walk_out(dst):
             return dst.rearrange("p (c i t) -> p c t i", i=4, t=PACK)
@@ -218,114 +242,112 @@ def tile_list_argo_cast_check_kernel(
             return src.rearrange("p t (c i) -> p c t i", i=4)
 
         x_w = {}
-        x_s = [held([P, QUARTER], U8, f"x_s{c}") for c in range(len(chunks))]
+        x_s = {c: held([P, CHUNK], U8, f"x_s{c}") for c in range(2)}
+        x_woven = {}
 
-        def weave_x(c, grouped):
-            nc.scalar.copy(out=walk_out(grouped[:]), in_=walk_in(x_diff[c]))
-            return grouped
+        def weave_x(c):
+            x_woven[c] = at([P, UNIT], BF16, f"x_woven{c}", X_WOVEN[c])
+            nc.scalar.copy(out=walk_out(x_woven[c][:]), in_=walk_in(x_diff[c]))
 
-        def quantise_x(c, grouped, codes):
+        def quantise_x(c, codes):
             x_w[c] = codes
-            nc.vector.quantize_mx(out=codes[:].bitcast(FP8X4), scales=x_s[c][:], in_=grouped[:])
+            quantise(codes[:], x_s[c][:], x_woven[c][:])
 
-        def first_stage(u, b, bank, w_codes, w_scales, rhs_w, rhs_s):
-            if kinds[u] != "D":
-                passes = [(2 * b + s, 0, QUARTER) for s in range(2)]
-            else:
-                passes = [(t, b * P, P) for t in range(PACK)]
-            for s, (t, o, n) in enumerate(passes):
+        def first_stage(b, bank, w_codes, w_scales, rhs_w, rhs_s):
+            for s in range(2):
+                t = 2 * b + s
                 nc.tensor.matmul_mx(
-                    out=bank[:, s * n : (s + 1) * n],
+                    out=bank[:, s * CHUNK : (s + 1) * CHUNK],
                     lhsT=w_codes(t),
                     lhsT_scale=w_scales[:, P * t : P * (t + 1)],
-                    rhs=rhs_w[:, o : o + n].bitcast(FP8X4),
-                    rhs_scale=rhs_s[:, o : o + n],
+                    rhs=rhs_w.bitcast(FP8X4),
+                    rhs_scale=rhs_s,
                     start=True,
                     stop=True,
                 )
-            if kinds[u] != "D":
-                return bank[:]
-            return bank[:].rearrange("p (t j) -> p j t", t=PACK)
-
-        def part_of(u, cols):
-            if kinds[u] != "D":
-                return cols
-            return cols.rearrange("p (j t) -> p j t", t=PACK)
 
         clim_bank = rotation(banks[4:] + banks[:4])
+        drift_bank = rotation(banks[4:])
+        corr_bank = rotation(banks[:4])
 
         def clim(u):
             c, a = units[u]
-            words, scales = table_columns(*chunks[c])
+            half, o = divmod(c * CHUNK, HALF)
             for b in range(2):
                 bank = clim_bank()
-                sums = first_stage(
-                    u, b, bank, lambda t: wc_w[a][:, 2 * P * t : 2 * P * (t + 1)].bitcast(FP4X4), wc_s[a], words, scales
+                first_stage(
+                    b,
+                    bank,
+                    lambda t: wc_w[a][:, 2 * P * t : 2 * P * (t + 1)].bitcast(FP4X4),
+                    wc_s[a],
+                    v_w[half][:, o : o + CHUNK],
+                    v_s[half][:, o : o + CHUNK],
                 )
-                nc.scalar.copy(out=part_of(u, work[u][b][:]), in_=sums)
+                nc.scalar.copy(out=clim_sb[u][b], in_=bank[:])
 
-        h_w = {}
-        h_s = [held([P, QUARTER], U8, f"h_s{u}") for u in range(len(units))]
-        zs = {}
-        drift_bank = rotation(banks[4:])
+        tanh_sb = {}
 
         def product(u):
             c, a = units[u]
-            z = ring.tile([P, PACK * QUARTER], F32, name="z", bufs=2)
-            zs[u] = z
+            z = ring.tile([P, UNIT], F32, name="z", bufs=2)
+            tanh_sb[u] = z
             for b in range(2):
                 bank = drift_bank()
-                sums = first_stage(
-                    u, b, bank, lambda t: wd_w[a][:, P * t : P * (t + 1)].bitcast(FP8X4), wd_s[a], x_w[c], x_s[c]
+                first_stage(
+                    b, bank, lambda t: wd_w[a][:, P * t : P * (t + 1)].bitcast(FP8X4), wd_s[a], x_w[c][:], x_s[c][:]
                 )
-                cols = slice(b * HALF, (b + 1) * HALF)
-                nc.vector.tensor_tensor(out=part_of(u, z[:, cols]), in0=sums, in1=part_of(u, work[u][b][:]), op=MULT)
+                cols = slice(b * BANK, (b + 1) * BANK)
+                nc.vector.tensor_tensor(out=z[:, cols], in0=bank[:], in1=clim_sb[u][b], op=MULT)
                 nc.scalar.activation(out=z[:, cols], in_=z[:, cols], func=TANH)
 
-        planes_h = {}
-        woven_h = {}
+        h_planes = {}
+        h_woven = {}
+        h_w = {}
+        h_s = {u: held([P, CHUNK], U8, f"h_s{u}") for u in range(paired, last + 1)}
 
-        def scale(u):
-            a = units[u][1]
-            planes = ring.tile([P, PACK * QUARTER], BF16, name="h_planes", bufs=4)
-            planes_h[u] = planes
+        def apply_gain(u):
+            planes = ring.tile([P, UNIT], BF16, name="h_planes", bufs=4)
+            h_planes[u] = planes
             for t in range(PACK):
-                cols = slice(t * QUARTER, (t + 1) * QUARTER)
-                nc.scalar.activation(out=planes[:, cols], in_=zs[u][:, cols], func=COPY, scale=gains[:, a, t : t + 1])
+                cols = slice(t * CHUNK, (t + 1) * CHUNK)
+                nc.scalar.activation(
+                    out=planes[:, cols], in_=tanh_sb[u][:, cols], func=COPY, scale=gains[:, units[u][1], t : t + 1]
+                )
 
-        def weave_h(u, grouped):
-            woven_h[u] = grouped
-            if kinds[u] == "A":
-                nc.gpsimd.tensor_scalar(
-                    out=grouped[:].rearrange("p (j t) -> p j t", t=PACK),
-                    in0=planes_h[u][:].rearrange("p (t j) -> p j t", t=PACK),
-                    scalar1=1.0,
-                    scalar2=0.0,
-                    op0=MULT,
-                    op1=ADD,
+        def weave_h(u, woven):
+            h_woven[u] = woven
+            if u < paired:
+                gpsimd_copy(
+                    woven.rearrange("p (j t) -> p j t", t=PACK), h_planes[u][:].rearrange("p (t j) -> p j t", t=PACK)
                 )
             else:
                 nc.vector.tensor_copy(
-                    out=walk_out(grouped[:]), in_=walk_in(planes_h[u][:].rearrange("p (t j) -> p t j", t=PACK))
+                    out=walk_out(woven), in_=walk_in(h_planes[u][:].rearrange("p (t j) -> p t j", t=PACK))
                 )
 
-        def quantise_h(u, codes):
-            h_w[u] = codes
-            nc.vector.quantize_mx(out=codes[:].bitcast(FP8X4), scales=h_s[u][:], in_=woven_h[u][:])
+        def quantise_h(u):
+            h_w[u] = held([P, CHUNK], U32, f"h_w{u}")
+            quantise(h_w[u][:], h_s[u][:], h_woven[u])
 
-        def scale_part(u, b):
-            cols = slice(b * P, (b + 1) * P)
-            tanh_planes = zs[u][:].rearrange("p (t j) -> p t j", t=PACK)
+        def quantise_pair(u, pair, step):
+            codes = held([P, 2 * CHUNK], U32, f"pair_w{step}")
+            scales = on_clim([P, 2 * CHUNK], U8, f"pair_s{step}", step, 1)
+            quantise(codes[:], scales[:], pair[:])
+            for i in range(2):
+                cols = slice(i * CHUNK, (i + 1) * CHUNK)
+                h_w[u + i], h_s[u + i] = codes[:, cols], scales[:, cols]
+
+        def last_unit_part(part):
+            cols = slice(part * P, (part + 1) * P)
+            tanh_planes = tanh_sb[last][:].rearrange("p (t j) -> p t j", t=PACK)
             planes = ring.tile([P, PACK, P], BF16, name="end_planes")
-            grouped = ring.tile([P, HALF], BF16, name="end_woven", align_bytes=64)
+            woven = ring.tile([P, PACK * P], BF16, name="end_woven", align_bytes=64)
             for t in range(PACK):
                 nc.scalar.activation(
-                    out=planes[:, t, :], in_=tanh_planes[:, t, cols], func=COPY, scale=gains[:, units[u][1], t : t + 1]
+                    out=planes[:, t, :], in_=tanh_planes[:, t, cols], func=COPY, scale=gains[:, units[last][1], t : t + 1]
                 )
-            nc.vector.tensor_copy(out=walk_out(grouped[:]), in_=walk_in(planes[:]))
-            return lambda: nc.vector.quantize_mx(
-                out=h_w[u][:, cols].bitcast(FP8X4), scales=h_s[u][:, cols], in_=grouped[:]
-            )
+            nc.vector.tensor_copy(out=walk_out(woven[:]), in_=walk_in(planes[:]))
+            return lambda: quantise(h_w[last][:, cols], h_s[last][:, cols], woven[:])
 
         def corr_passes(c, o, width, tiles, a, bank):
             u = units.index((c, a))
@@ -343,172 +365,139 @@ def tile_list_argo_cast_check_kernel(
         obs_sb = []
 
         def finish(c, o, width, tiles, bank, room=None):
-            j0 = chunks[c][0] + o
+            j0 = c * CHUNK + o
             for s in range(0, len(tiles), 2):
                 n = tiles[s]
-                part = obs_sb[n // 2][:, :, j0 : j0 + width]
+                given = obs_sb[n // 2][:, :, j0 : j0 + width]
                 sums = bank[:, s * width : (s + 2) * width].rearrange("p (s j) -> p s j", j=width)
-                res = part if room is None else room[:]
-                nc.vector.tensor_tensor(out=res, in0=part, in1=sums, op=SUBTRACT)
+                res = given if room is None else room
+                nc.vector.tensor_tensor(out=res, in0=given, in1=sums, op=SUBTRACT)
                 nc.sync.dma_start(out=out_rows[:, n : n + 2, j0 : j0 + width], in_=res)
 
-        corr_bank = rotation(banks[:4])
         pending = []
 
         def put_out(room=None):
             c, tiles, bank = pending.pop(0)
             for a in range(R_PASSES):
-                corr_passes(c, 0, QUARTER, tiles, a, bank)
-            finish(c, 0, QUARTER, tiles, bank, room)
+                corr_passes(c, 0, CHUNK, tiles, a, bank)
+            finish(c, 0, CHUNK, tiles, bank, room)
+
+        def by_tiles(cols):
+            return cols.rearrange("p (g j) -> p g j", g=2)
 
         for u in range(last - 1):
             clim(u)
-        wd_woven0 = weave_wd(0, "G", 50)
-        third_before = at([P, 2, QUARTER], F32, "third_before", 10)
-        third_after = at([P, 2, QUARTER], F32, "third_after", 46)
+        wd_woven0 = weave_wd_on_gpsimd(0, WD_WOVEN0)
+        third_before = at([P, 2, CHUNK], F32, "third_before", THIRD_BEFORE)
+        third_after = at([P, 2, CHUNK], F32, "third_after", THIRD_AFTER)
         for t in range(PACK - 1):
-            before = at([P, HALF], F32, f"before{t}", 28 + 2 * t)
+            before = at([P, HALF], F32, f"before{t}", BEFORE + 2 * KIB * t)
             if t == 0:
                 after = x_diff[2][:, 0:2, :].rearrange("p t j -> p (t j)")
             else:
-                after = at([P, HALF], F32, f"after{t}", 40 + 2 * t)[:]
+                after = at([P, HALF], F32, f"after{t}", AFTER + 2 * KIB * t)[:]
             pick(before[:], t, list3, 0, HALF)
             pick(after, t, list2, 0, HALF)
             subtract(first_diff[:, t, :], after, before[:])
             if t < 2:
-                pick(third_before[:, t, :], t, list3, HALF, QUARTER)
+                pick(third_before[:, t, :], t, list3, HALF, CHUNK)
             if t == 1:
                 for i in range(2):
-                    pick(third_after[:, i, :], i, list2, HALF, QUARTER)
+                    pick(third_after[:, i, :], i, list2, HALF, CHUNK)
                 subtract(x_diff[2][:, 0:2, :], third_after[:], third_before[:])
-        t = PACK - 1
-        ends_of_plane = []
-        for j0, width, kib in ((0, QUARTER, 49), (QUARTER, QUARTER, 37)):
-            before = at([P, width], F32, f"before3_{j0}", kib)
-            pick(before[:], t, list3, j0, width)
-            ends_of_plane.append((j0, width, before))
-        for j0, width, before in ends_of_plane:
-            nc.vector.tensor_tensor(
-                out=first_diff[:, t, j0 : j0 + width],
-                in0=x_planes[t][:].indirect(entries(list2, j0, width)),
-                in1=before[:],
-                op=SUBTRACT,
-            )
-        wd_woven1 = weave_wd(1, "S", 12)
-        x_woven = {c: weave_x(c, at([P, PACK * QUARTER], BF16, f"x_woven{c}", (19, 22)[c])) for c in range(2)}
+        last_before = [at([P, CHUNK], F32, f"last_before{c}", LAST_BEFORE[c]) for c in range(2)]
+        for c in range(2):
+            pick(last_before[c][:], PACK - 1, list3, c * CHUNK, CHUNK)
+        for c in range(2):
+            pick_diff(c, PACK - 1, last_before[c][:])
+        wd_woven1, dst, src = wd_views(1, WD_WOVEN1, "m j t")
+        nc.scalar.copy(out=dst, in_=src)
+        for c in range(2):
+            weave_x(c)
         for i in range(2):
-            last_work = at([P, 2, HALF], F32, f"last_work{i}", 2 + 4 * i)
-            work.append([last_work[:, b, :] for b in range(2)])
+            both_banks = at([P, 2, BANK], F32, f"last_clim{i}", LAST_CLIM + 4 * KIB * i)
+            clim_sb.append([both_banks[:, b, :] for b in range(2)])
             clim(last - 1 + i)
-        for a, grouped in enumerate((wd_woven0, wd_woven1)):
-            wd_s[a] = arena.tile([P, PASS], U8, name=f"wd_s_late{a}", align_bytes=64, offset=49 * 1024 + PASS * a)
-            quantise_wd(a, grouped)
-        quantise_x(0, x_woven[0], held([P, QUARTER], U32, "x_w0"))
-        wd_woven2 = weave_wd(2, "G", 15.5)
-        for obs_pair in (at([P, 2, S], F32, "obs0", 28), at([P, 2, S], F32, "obs1", 40), held([P, 2, S], F32, "wd_raw2")):
-            g = len(obs_sb)
+        for a, woven in enumerate((wd_woven0, wd_woven1)):
+            quantise_wd(a, woven, at([P, PASS], U8, f"wd_s{a}", WD_SCALES + PASS * a))
+        quantise_x(0, held([P, CHUNK], U32, "x_w0"))
+        wd_woven2 = weave_wd_on_gpsimd(2, WD_WOVEN2)
+        obs_sb.append(at([P, 2, S], F32, "obs0", OBS0))
+        obs_sb.append(at([P, 2, S], F32, "obs1", OBS1))
+        obs_sb.append(held([P, 2, S], F32, "wd_raw2"))
+        for g, obs_pair in enumerate(obs_sb):
             nc.sync.dma_start(out=obs_pair[:], in_=obs_rows[:, 2 * g : 2 * g + 2, :])
-            obs_sb.append(obs_pair)
 
-        befores = {}
+        late_before = {}
 
-        def pick_befores(c, first, pair):
+        def pick_late_before(step, tile):
+            c, first = late[step]
             for i in range(2):
-                pick(pair[:, i, :], first + i, list3, *chunks[c])
-            befores[c, first] = pair
+                pick(tile[:, i, :], first + i, list3, c * CHUNK, CHUNK)
+            late_before[step] = tile
 
-        def pick_diffs(c, first):
-            for i in range(2):
-                nc.vector.tensor_tensor(
-                    out=x_diff[c][:, first + i, :],
-                    in0=x_planes[first + i][:].indirect(entries(list2, *chunks[c])),
-                    in1=befores[c, first][:, i, :],
-                    op=SUBTRACT,
-                )
-
-        def codes(name, step, o=0):
-            return in_arena([P, QUARTER], U32, name, step, 1, o)
-
-        def gain_on_vector(u, grouped):
-            woven_h[u] = grouped
-            for b in range(2):
-                cols = slice(b * HALF, (b + 1) * HALF)
-                nc.vector.tensor_tensor(
-                    out=part_of(u, grouped[:, cols]),
-                    in0=part_of(u, zs[u][:, cols]),
-                    in1=gains[:, units[u][1], :].unsqueeze(1).to_broadcast([P, P, PACK]),
-                    op=MULT,
-                )
-
-        pick_befores(2, 2, at([P, 2, QUARTER], F32, "before_late0", 20))
+        pick_late_before(1, at([P, 2, CHUNK], F32, "late_before1", LATE_BEFORE))
         for step in range(last + 1):
             product(step)
             if step < last:
-                scale(step)
-            done = [step - 2] if step >= 10 else []
-            for u in done:
-                quantise_h(u, held([P, QUARTER], U32, f"h_w{u}"))
+                apply_gain(step)
+            done = []
+            if step - 2 >= paired:
+                quantise_h(step - 2)
+                done.append(step - 2)
             if pending:
-                put_out(work[step][0].rearrange("p (g j) -> p g j", g=2))
-            if step == 8:
-                put_out(work[step][1].rearrange("p (g j) -> p g j", g=2))
-            if step == 2:
-                pick_befores(3, 0, in_arena([P, 2, QUARTER], F32, "before_late1", 2, 0))
-            if step == 4:
-                pick_befores(3, 2, in_arena([P, 2, QUARTER], F32, "before_late2", 4, 0))
+                put_out(by_tiles(clim_sb[step][0]))
+            if step == paired:
+                put_out(by_tiles(clim_sb[step][1]))
+            if step + 1 in late and step > 0:
+                pick_late_before(step + 1, on_clim([P, 2, CHUNK], F32, f"late_before{step + 1}", step, 0))
             if step == 1:
-                quantise_x(1, x_woven[1], in_arena([P, QUARTER], U32, "x_w1", 1, 0, 1024))
-                wd_s[2] = in_arena([P, PASS], U8, "wd_s_late2", 1, 0)
-                quantise_wd(2, wd_woven2)
+                quantise_x(1, on_clim([P, CHUNK], U32, "x_w1", 1, 0, KIB))
+                quantise_wd(2, wd_woven2, on_clim([P, PASS], U8, "wd_s2", 1, 0))
             if step in late:
-                pick_diffs(*late[step])
-            if step == 1:
-                pair = at([P, 2 * PACK * QUARTER], BF16, "pair0", 17)
-                weave_h(0, pair[:, 0 : PACK * QUARTER])
-            if step == 2:
-                weave_h(1, pair[:, PACK * QUARTER :])
-            if step in (1, 5):
-                c = 2 + step // 4
-                x_woven[c] = weave_x(c, at([P, PACK * QUARTER], BF16, f"x_woven{c}", 20 + 2 * c))
-            if step in {3: 2, 7: 3}:
-                c = {3: 2, 7: 3}[step]
-                x_s[c] = in_arena([P, QUARTER], U8, f"x_s_late{c}", step, 1, 1536)
-                quantise_x(c, x_woven[c], held([P, QUARTER], U32, f"x_w{c}"))
-            if step in (3, 5, 7, 9):
-                pair_w = held([P, HALF], U32, f"pair_w{step}")
-                pair_s = in_arena([P, HALF], U8, f"pair_s{step}", step, 1)
-                nc.vector.quantize_mx(out=pair_w[:].bitcast(FP8X4), scales=pair_s[:], in_=pair[:])
+                c, first = late[step]
                 for i in range(2):
-                    cols = slice(i * QUARTER, (i + 1) * QUARTER)
-                    h_w[step - 3 + i], h_s[step - 3 + i] = pair_w[:, cols], pair_s[:, cols]
-                    done.append(step - 3 + i)
-                pair = at([P, 2 * PACK * QUARTER], BF16, f"pair{step}", 17)
-                weave_h(step - 1, pair[:, 0 : PACK * QUARTER])
-            if step in (4, 6, 8):
-                weave_h(step - 1, pair[:, PACK * QUARTER :])
-            if step >= 10:
-                weave_h(step - 1, held([P, PACK * QUARTER], BF16, f"h_woven{step % 2}"))
+                    pick_diff(c, first + i, late_before[step][:, i, :])
+            if step == 1:
+                pair = at([P, 2 * UNIT], BF16, "pair1", H_PAIR)
+                weave_h(0, pair[:, 0:UNIT])
+            if step in late and late[step][1] == 2:
+                weave_x(late[step][0])
+            if step - 2 in late and late[step - 2][1] == 2:
+                c = late[step - 2][0]
+                x_s[c] = on_clim([P, CHUNK], U8, f"x_s{c}", step, 1, 3 * BANK)
+                quantise_x(c, held([P, CHUNK], U32, f"x_w{c}"))
+            if step % 2 == 1 and 3 <= step <= paired + 1:
+                quantise_pair(step - 3, pair, step)
+                done += [step - 3, step - 2]
+                pair = at([P, 2 * UNIT], BF16, f"pair{step}", H_PAIR)
+                weave_h(step - 1, pair[:, 0:UNIT])
+            if step % 2 == 0 and 2 <= step <= paired:
+                weave_h(step - 1, pair[:, UNIT:])
+            if step - 1 > paired:
+                weave_h(step - 1, held([P, UNIT], BF16, f"h_woven{step % 2}")[:])
             for u in done:
-                if units[u][1] == R_PASSES - 1:
+                c, a = units[u]
+                if a == R_PASSES - 1:
                     for n in range(0, N_TILES, 2):
-                        pending.append((units[u][0], (n, n + 1), corr_bank()))
-        h_w[last] = held([P, QUARTER], U32, "h_w11")
-        while len(pending) > 1:
-            put_out()
-        quantise_h(last - 1, held([P, QUARTER], U32, "h_w10"))
-        quantise_end = [scale_part(last, b) for b in range(2)]
-        ends = [(0, (banks[1], banks[4])), (P, (banks[5], banks[6]))]
+                        pending.append((c, (n, n + 1), corr_bank()))
+
+        h_w[last] = held([P, CHUNK], U32, f"h_w{last}")
+        put_out()
+        quantise_h(last - 1)
+        quantise_part = [last_unit_part(part) for part in range(2)]
+        parts = [(0, (banks[1], banks[4])), (P, (banks[5], banks[6]))]
         groups = ((0, 1, 2, 3), (4, 5))
-        c = len(chunks) - 1
+        c = units[last][0]
         for a in range(R_PASSES - 1):
-            for o, pair in ends:
-                for tiles, bank in zip(groups, pair):
+            for o, part_banks in parts:
+                for tiles, bank in zip(groups, part_banks):
                     corr_passes(c, o, P, tiles, a, bank)
-        for (o, pair), quantise in zip(ends, quantise_end):
-            quantise()
-            for tiles, bank in zip(groups, pair):
+        for (o, part_banks), quantise_it in zip(parts, quantise_part):
+            quantise_it()
+            for tiles, bank in zip(groups, part_banks):
                 corr_passes(c, o, P, tiles, R_PASSES - 1, bank)
-        put_out(ring.tile([P, 2, QUARTER], F32, name="end_woven", align_bytes=64))
-        for o, pair in ends:
-            for tiles, bank in zip(groups, pair):
+        put_out(ring.tile([P, 2, CHUNK], F32, name="end_woven", align_bytes=64)[:])
+        for o, part_banks in parts:
+            for tiles, bank in zip(groups, part_banks):
                 finish(c, o, P, tiles, bank)

@@ -30,25 +30,28 @@ R_PASSES = H // PASS
 N_TILES = N // P
 KIB = 1024
 
-WD_RAW0 = 0
-FIRST_DIFF = 2 * KIB
-LAST_CLIM = FIRST_DIFF
-THIRD_BEFORE = 10 * KIB
-WD_WOVEN1 = 12 * KIB
-WD_WOVEN2 = 15 * KIB + 512
-WD_RAW1 = 16 * KIB + 256
-H_PAIR = 17 * KIB
-X_WOVEN = (19 * KIB, 22 * KIB, 24 * KIB, 26 * KIB)
-LATE_BEFORE = 20 * KIB
-BEFORE = 28 * KIB
-OBS0 = BEFORE
-LAST_BEFORE = (49 * KIB, 37 * KIB)
-WD_SCALES = LAST_BEFORE[0]
-AFTER = 40 * KIB
-OBS1 = AFTER
-THIRD_AFTER = 46 * KIB
-WD_WOVEN0 = 50 * KIB
-CLIM = 56 * KIB
+
+TAB_W = 0
+WD_WOVEN = (0, 4 * KIB, 7 * KIB + 768)
+TAB_S = 8 * KIB
+WC_S_RAW = 112 * KIB
+V_W1 = 113 * KIB
+EARLY = 3 * CHUNK
+X_WOVEN = (11 * KIB + 512, 19 * KIB, 0, 2 * KIB)
+LATE_BEFORE = (4 * KIB, 11 * KIB + 768)
+WD_RAW1 = 13 * KIB + 256
+GROUP = 6 * KIB
+PICKS = 22 * KIB
+WD_RAW2 = 38 * KIB
+OBS = PICKS
+BEFORE2 = 46 * KIB
+CLIM = 48 * KIB
+Z = 96 * KIB
+TRIPLE = 6 * KIB - 256
+
+KINDS = "PPPPPPPPPPXQ"
+GROUPS = ((0, 1), (2, 3), (4, 5), (6, 7, 8), (9,))
+Z_RING = 2
 
 
 def rotation(items):
@@ -68,7 +71,6 @@ def tile_list_argo_cast_check_kernel(
     with ExitStack() as ctx:
         keep = ctx.enter_context(tc.tile_pool(name="keep", bufs=1))
         ring = ctx.enter_context(tc.tile_pool(name="ring", bufs=2))
-        placed = ctx.enter_context(tc.tile_pool(name="placed", bufs=1))
         arena = ctx.enter_context(tc.tile_pool(name="arena", bufs=1))
         psum = ctx.enter_context(tc.psum_pool(name="psum", bufs=1))
 
@@ -86,20 +88,21 @@ def tile_list_argo_cast_check_kernel(
         list1 = keep.tile([P, S // 16], U16, name="list1")
         list2 = keep.tile([P, S // 16], U16, name="list2")
         list3 = keep.tile([P, S // 16], U16, name="list3")
-        tab_w = held([P, T], I32, "tab_w")
-        tab_s = held([P, T], U8, "tab_s")
+        tab_w = at([P, T], I32, "tab_w", TAB_W)
+        tab_s = at([P, T], U8, "tab_s", TAB_S)
         wc_w_raw = held([P, 2 * H], U8, "wc_w_raw")
-        wc_s_raw = placed.tile([P, H], U8, name="wc_s_raw", align_bytes=64, offset=4 * HALF - 512)
+        wc_s_raw = at([P, H], U8, "wc_s_raw", WC_S_RAW)
         wc_w = [held([P, 2 * PASS], U8, f"wc_w{a}") for a in range(R_PASSES)]
         wc_s = [held([P, PASS], U8, f"wc_s{a}") for a in range(R_PASSES)]
         wo_w = held([P, R_PASSES, N], I32, "wo_w")
         wo_s = held([P, R_PASSES, N], U8, "wo_s")
         gains = held([P, R_PASSES, PACK], F32, "gains")
-        x_planes = [keep.tile([P, T], F32, name="x_plane", bufs=PACK, align_bytes=64) for t in range(PACK)]
+        x_planes = [held([P, T], F32, f"x_plane{t}") for t in range(PACK)]
+        diff = held([P, PACK, S], F32, "diff")
         wd_raw = [
-            at([P, PACK, PASS], F32, "wd_raw0", WD_RAW0),
-            at([P, PACK, PASS], F32, "wd_raw1", WD_RAW1),
-            held([P, PACK, PASS], F32, "wd_raw2"),
+            diff[:, :, 0:HALF],
+            at([P, PACK, PASS], F32, "wd_raw1", WD_RAW1)[:],
+            at([P, PACK, PASS], F32, "wd_raw2", WD_RAW2)[:],
         ]
 
         nc.vector.memset(tab_s[:].bitcast(I32), 0)
@@ -121,7 +124,7 @@ def tile_list_argo_cast_check_kernel(
             nc.sync.dma_start(out=x_planes[t][:], in_=x_rows[:, t, :])
 
         def load_wd(a):
-            nc.sync.dma_start(out=wd_raw[a][:], in_=wd_rows[:, :, a * PASS : (a + 1) * PASS])
+            nc.sync.dma_start(out=wd_raw[a], in_=wd_rows[:, :, a * PASS : (a + 1) * PASS])
 
         nc.sync.dma_start(out=wc_w_raw[:].bitcast(I32), in_=wc_words[0].bitcast(I32))
         load_scale_rows(tab_s, tab_scales[0])
@@ -145,7 +148,7 @@ def tile_list_argo_cast_check_kernel(
         nc.sync.dma_start(out=wo_w[:], in_=wo_words.rearrange("a p c i -> p a (c i)").bitcast(I32))
 
         def deal_words(a):
-            nc.vector.tensor_copy(
+            nc.scalar.copy(
                 out=wc_w[a][:].bitcast(U16).rearrange("p (t m) -> p t m", t=PACK),
                 in_=wc_w_raw[:, 2 * PASS * a : 2 * PASS * (a + 1)].bitcast(U16).rearrange("p (m t) -> p t m", t=PACK),
             )
@@ -159,44 +162,34 @@ def tile_list_argo_cast_check_kernel(
         def entries(lst, j0, width):
             return lst[:, j0 // 16 : (j0 + width) // 16]
 
-        v_w0 = held([P, HALF], U32, "v_w0")
-        v_s0 = held([P, HALF], U8, "v_s0")
-        v_w = (v_w0, placed.tile([P, HALF], U32, name="v_w1", align_bytes=64, offset=0))
-        v_s = (v_s0, held([P, HALF], U8, "v_s1"))
+        v_w = [held([P, HALF], U32, "v_w0"), at([P, HALF], U32, "v_w1", V_W1)]
+        v_s = held([P, S], U8, "v_s")
+        nc.vector.tensor_copy(out=v_s[:], in_=tab_s[:].indirect(list1[:]))
 
         def pick_words(half):
             nc.vector.tensor_copy(out=v_w[half][:], in_=tab_w[:].bitcast(U32).indirect(entries(list1, half * HALF, HALF)))
 
-        def pick_scales(half):
-            nc.vector.tensor_copy(out=v_s[half][:], in_=tab_s[:].indirect(entries(list1, half * HALF, HALF)))
-
-        deal_words(0)
-        pick_scales(0)
         pick_words(0)
-        deal_scales(0)
-        for a in range(1, R_PASSES):
+        for a in range(R_PASSES):
             deal_words(a)
             deal_scales(a)
         pick_words(1)
-        pick_scales(1)
 
         units = [(c, a) for c in range(S // CHUNK) for a in range(R_PASSES)]
         units[2], units[3] = units[3], units[2]
         last = len(units) - 1
-        paired = 8
-
-        first_diff = at([P, PACK, HALF], F32, "first_diff", FIRST_DIFF)
-        x_diff = [first_diff[:, :, c * CHUNK : (c + 1) * CHUNK] for c in range(2)]
-        x_diff += [held([P, PACK, CHUNK], F32, f"late_diff{c}")[:] for c in (2, 3)]
+        x_diff = [diff[:, :, c * CHUNK : (c + 1) * CHUNK] for c in range(S // CHUNK)]
         late = {1: (2, 2), 3: (3, 0), 5: (3, 2)}
 
         def clim_tile(u, b):
             if u in late and b == int(u == 1):
                 c, t = late[u]
-                return x_diff[c][:, t : t + 2, :].rearrange("p t j -> p (t j)")
-            return on_clim([P, BANK], F32, f"clim{u}_{b}", u, b)[:]
+                return x_diff[c][:, t : t + 2, :]
+            if u >= last - 1:
+                return x_diff[u - last + 1][:, 2 * b : 2 * b + 2, :]
+            return on_clim([P, 2, CHUNK], F32, f"clim{u}_{b}", u, b)[:]
 
-        clim_sb = [[clim_tile(u, b) for b in range(2)] for u in range(last - 1)]
+        clim_sb = [[clim_tile(u, b) for b in range(2)] for u in range(last + 1)]
 
         def pick(dst, t, lst, j0, width):
             nc.vector.tensor_copy(out=dst, in_=x_planes[t][:].indirect(entries(lst, j0, width)))
@@ -209,9 +202,6 @@ def tile_list_argo_cast_check_kernel(
                 op=SUBTRACT,
             )
 
-        def subtract(dst, after, before):
-            nc.gpsimd.tensor_tensor(out=dst, in0=after, in1=before, op=SUBTRACT)
-
         def gpsimd_copy(dst, src):
             nc.gpsimd.tensor_scalar(out=dst, in0=src, scalar1=1.0, scalar2=0.0, op0=MULT, op1=ADD)
 
@@ -220,20 +210,16 @@ def tile_list_argo_cast_check_kernel(
 
         wd_w = [held([P, PASS], U32, f"wd_w{a}") for a in range(R_PASSES)]
         wd_s = {}
+        wd_woven = {}
 
-        def wd_views(a, offset, walk):
-            woven = at([P, PACK * PASS], BF16, f"wd_woven{a}", offset)
-            dst = woven[:].rearrange(f"p (t m j) -> p {walk}", t=PACK, j=PACK)
-            return woven, dst, wd_raw[a][:].rearrange(f"p j (m t) -> p {walk}", t=PACK)
+        def wd_views(a, walk):
+            wd_woven[a] = at([P, PACK * PASS], BF16, f"wd_woven{a}", WD_WOVEN[a])
+            dst = wd_woven[a][:].rearrange(f"p (t m j) -> p {walk}", t=PACK, j=PACK)
+            return dst, wd_raw[a].rearrange(f"p j (m t) -> p {walk}", t=PACK)
 
-        def weave_wd_on_gpsimd(a, offset):
-            woven, dst, src = wd_views(a, offset, "m t j")
-            gpsimd_copy(dst, src)
-            return woven
-
-        def quantise_wd(a, woven, scales):
+        def quantise_wd(a, scales):
             wd_s[a] = scales
-            quantise(wd_w[a][:], scales[:], woven[:])
+            quantise(wd_w[a][:], scales[:], wd_woven[a][:])
 
         def walk_out(dst):
             return dst.rearrange("p (c i t) -> p c t i", i=4, t=PACK)
@@ -242,29 +228,46 @@ def tile_list_argo_cast_check_kernel(
             return src.rearrange("p t (c i) -> p c t i", i=4)
 
         x_w = {}
-        x_s = {c: held([P, CHUNK], U8, f"x_s{c}") for c in range(2)}
+        x_s = {}
         x_woven = {}
 
         def weave_x(c):
             x_woven[c] = at([P, UNIT], BF16, f"x_woven{c}", X_WOVEN[c])
             nc.scalar.copy(out=walk_out(x_woven[c][:]), in_=walk_in(x_diff[c]))
 
-        def quantise_x(c, codes):
-            x_w[c] = codes
-            quantise(codes[:], x_s[c][:], x_woven[c][:])
+        def quantise_x(c, scales):
+            x_w[c] = held([P, CHUNK], U32, f"x_w{c}")
+            x_s[c] = scales
+            quantise(x_w[c][:], scales[:], x_woven[c][:])
 
-        def first_stage(b, bank, w_codes, w_scales, rhs_w, rhs_s):
-            for s in range(2):
-                t = 2 * b + s
+        def first_stage(u, b, bank, w_codes, w_scales, rhs_w, rhs_s):
+            if KINDS[u] in "PX":
+                parts = [(2 * b + s, 0, CHUNK) for s in range(2)]
+            else:
+                parts = [(t, b * P, P) for t in range(PACK)]
+            for s, (t, o, width) in enumerate(parts):
                 nc.tensor.matmul_mx(
-                    out=bank[:, s * CHUNK : (s + 1) * CHUNK],
+                    out=bank[:, s * width : (s + 1) * width],
                     lhsT=w_codes(t),
                     lhsT_scale=w_scales[:, P * t : P * (t + 1)],
-                    rhs=rhs_w.bitcast(FP8X4),
-                    rhs_scale=rhs_s,
+                    rhs=rhs_w[:, o : o + width].bitcast(FP8X4),
+                    rhs_scale=rhs_s[:, o : o + width],
                     start=True,
                     stop=True,
                 )
+
+        def woven_kind(u):
+            return KINDS[u] in "GV"
+
+        def bank_view(u, bank):
+            if woven_kind(u):
+                return bank[:].rearrange("p (t g j) -> p g j t", t=PACK, g=2)
+            return bank[:].rearrange("p (g j) -> p g j", g=2)
+
+        def sb_view(u, two_rows):
+            if woven_kind(u):
+                return two_rows.rearrange("p g (j t) -> p g j t", t=PACK)
+            return two_rows
 
         clim_bank = rotation(banks[4:] + banks[:4])
         drift_bank = rotation(banks[4:])
@@ -276,34 +279,41 @@ def tile_list_argo_cast_check_kernel(
             for b in range(2):
                 bank = clim_bank()
                 first_stage(
+                    u,
                     b,
                     bank,
                     lambda t: wc_w[a][:, 2 * P * t : 2 * P * (t + 1)].bitcast(FP4X4),
                     wc_s[a],
                     v_w[half][:, o : o + CHUNK],
-                    v_s[half][:, o : o + CHUNK],
+                    v_s[:, c * CHUNK : (c + 1) * CHUNK],
                 )
-                nc.scalar.copy(out=clim_sb[u][b], in_=bank[:])
+                nc.scalar.copy(out=sb_view(u, clim_sb[u][b]), in_=bank_view(u, bank))
 
         tanh_sb = {}
+        z_slot = rotation(list(range(Z_RING)))
+        own_slot = rotation([Z_RING, Z_RING + 1])
 
         def product(u):
             c, a = units[u]
-            z = ring.tile([P, UNIT], F32, name="z", bufs=2)
-            tanh_sb[u] = z
+            z = at([P, UNIT], F32, f"z{u}", Z + 4 * UNIT * z_slot())
+            tanh_sb[u] = at([P, UNIT], F32, f"tanh{u}", Z + 4 * UNIT * own_slot()) if KINDS[u] == "G" else z
             for b in range(2):
                 bank = drift_bank()
                 first_stage(
-                    b, bank, lambda t: wd_w[a][:, P * t : P * (t + 1)].bitcast(FP8X4), wd_s[a], x_w[c][:], x_s[c][:]
+                    u, b, bank, lambda t: wd_w[a][:, P * t : P * (t + 1)].bitcast(FP8X4), wd_s[a], x_w[c][:], x_s[c][:]
                 )
-                cols = slice(b * BANK, (b + 1) * BANK)
-                nc.vector.tensor_tensor(out=z[:, cols], in0=bank[:], in1=clim_sb[u][b], op=MULT)
-                nc.scalar.activation(out=z[:, cols], in_=z[:, cols], func=TANH)
+                cols = z[:, b * BANK : (b + 1) * BANK]
+                nc.vector.tensor_tensor(
+                    out=sb_view(u, cols.rearrange("p (g j) -> p g j", g=2)),
+                    in0=bank_view(u, bank),
+                    in1=sb_view(u, clim_sb[u][b]),
+                    op=MULT,
+                )
+                nc.scalar.activation(out=tanh_sb[u][:, b * BANK : (b + 1) * BANK], in_=cols, func=TANH)
 
         h_planes = {}
-        h_woven = {}
         h_w = {}
-        h_s = {u: held([P, CHUNK], U8, f"h_s{u}") for u in range(paired, last + 1)}
+        h_s = {}
 
         def apply_gain(u):
             planes = ring.tile([P, UNIT], BF16, name="h_planes", bufs=4)
@@ -314,39 +324,45 @@ def tile_list_argo_cast_check_kernel(
                     out=planes[:, cols], in_=tanh_sb[u][:, cols], func=COPY, scale=gains[:, units[u][1], t : t + 1]
                 )
 
+        def woven_gain(engine, u, dst, src):
+            width = src.shape[1] // PACK
+            engine.tensor_tensor(
+                out=dst.rearrange("p (j t) -> p j t", t=PACK),
+                in0=src.rearrange("p (j t) -> p j t", t=PACK),
+                in1=gains[:, units[u][1], :].unsqueeze(1).to_broadcast([P, width, PACK]),
+                op=MULT,
+            )
+
         def weave_h(u, woven):
-            h_woven[u] = woven
-            if u < paired:
+            if KINDS[u] == "P":
                 gpsimd_copy(
                     woven.rearrange("p (j t) -> p j t", t=PACK), h_planes[u][:].rearrange("p (t j) -> p j t", t=PACK)
                 )
             else:
-                nc.vector.tensor_copy(
-                    out=walk_out(woven), in_=walk_in(h_planes[u][:].rearrange("p (t j) -> p t j", t=PACK))
-                )
+                woven_gain(nc.gpsimd if KINDS[u] == "G" else nc.vector, u, woven, tanh_sb[u][:])
 
-        def quantise_h(u):
-            h_w[u] = held([P, CHUNK], U32, f"h_w{u}")
-            quantise(h_w[u][:], h_s[u][:], h_woven[u])
-
-        def quantise_pair(u, pair, step):
-            codes = held([P, 2 * CHUNK], U32, f"pair_w{step}")
-            scales = on_clim([P, 2 * CHUNK], U8, f"pair_s{step}", step, 1)
-            quantise(codes[:], scales[:], pair[:])
-            for i in range(2):
+        def quantise_group(group, woven, scales):
+            codes = held([P, len(group) * CHUNK], U32, f"group_w{group[0]}")
+            for i0 in range(0, len(group), 2):
+                i1 = min(i0 + 2, len(group))
+                quantise(codes[:, i0 * CHUNK : i1 * CHUNK], scales[:, i0 * CHUNK : i1 * CHUNK], woven[:, i0 * UNIT : i1 * UNIT])
+            for i, u in enumerate(group):
                 cols = slice(i * CHUNK, (i + 1) * CHUNK)
-                h_w[u + i], h_s[u + i] = codes[:, cols], scales[:, cols]
+                h_w[u], h_s[u] = codes[:, cols], scales[:, cols]
 
         def last_unit_part(part):
+            woven = held([P, PACK * P], BF16, f"end_woven{part}")
+            src = tanh_sb[last][:, part * BANK : (part + 1) * BANK]
+            if KINDS[last] == "V":
+                woven_gain(nc.vector, last, woven[:], src)
+            else:
+                planes = held([P, PACK, P], BF16, f"end_planes{part}")
+                for t in range(PACK):
+                    nc.scalar.activation(
+                        out=planes[:, t, :], in_=src[:, t * P : (t + 1) * P], func=COPY, scale=gains[:, units[last][1], t : t + 1]
+                    )
+                nc.vector.tensor_copy(out=walk_out(woven[:]), in_=walk_in(planes[:]))
             cols = slice(part * P, (part + 1) * P)
-            tanh_planes = tanh_sb[last][:].rearrange("p (t j) -> p t j", t=PACK)
-            planes = ring.tile([P, PACK, P], BF16, name="end_planes")
-            woven = ring.tile([P, PACK * P], BF16, name="end_woven", align_bytes=64)
-            for t in range(PACK):
-                nc.scalar.activation(
-                    out=planes[:, t, :], in_=tanh_planes[:, t, cols], func=COPY, scale=gains[:, units[last][1], t : t + 1]
-                )
-            nc.vector.tensor_copy(out=walk_out(woven[:]), in_=walk_in(planes[:]))
             return lambda: quantise(h_w[last][:, cols], h_s[last][:, cols], woven[:])
 
         def corr_passes(c, o, width, tiles, a, bank):
@@ -362,17 +378,14 @@ def tile_list_argo_cast_check_kernel(
                     stop=(a == R_PASSES - 1 and s == len(tiles) - 1),
                 )
 
-        obs_sb = []
-
         def finish(c, o, width, tiles, bank, room=None):
             j0 = c * CHUNK + o
-            for s in range(0, len(tiles), 2):
-                n = tiles[s]
-                given = obs_sb[n // 2][:, :, j0 : j0 + width]
-                sums = bank[:, s * width : (s + 2) * width].rearrange("p (s j) -> p s j", j=width)
-                res = given if room is None else room
-                nc.vector.tensor_tensor(out=res, in0=given, in1=sums, op=SUBTRACT)
-                nc.sync.dma_start(out=out_rows[:, n : n + 2, j0 : j0 + width], in_=res)
+            rows = slice(tiles[0], tiles[-1] + 1)
+            given = obs_sb[:, rows, j0 : j0 + width]
+            sums = bank[:, 0 : len(tiles) * width].rearrange("p (s j) -> p s j", j=width)
+            res = given if room is None else room
+            nc.vector.tensor_tensor(out=res, in0=given, in1=sums, op=SUBTRACT)
+            nc.sync.dma_start(out=out_rows[:, rows, j0 : j0 + width], in_=res)
 
         pending = []
 
@@ -382,122 +395,160 @@ def tile_list_argo_cast_check_kernel(
                 corr_passes(c, 0, CHUNK, tiles, a, bank)
             finish(c, 0, CHUNK, tiles, bank, room)
 
-        def by_tiles(cols):
-            return cols.rearrange("p (g j) -> p g j", g=2)
-
         for u in range(last - 1):
             clim(u)
-        wd_woven0 = weave_wd_on_gpsimd(0, WD_WOVEN0)
-        third_before = at([P, 2, CHUNK], F32, "third_before", THIRD_BEFORE)
-        third_after = at([P, 2, CHUNK], F32, "third_after", THIRD_AFTER)
-        for t in range(PACK - 1):
-            before = at([P, HALF], F32, f"before{t}", BEFORE + 2 * KIB * t)
-            if t == 0:
-                after = x_diff[2][:, 0:2, :].rearrange("p t j -> p (t j)")
-            else:
-                after = at([P, HALF], F32, f"after{t}", AFTER + 2 * KIB * t)[:]
-            pick(before[:], t, list3, 0, HALF)
-            pick(after, t, list2, 0, HALF)
-            subtract(first_diff[:, t, :], after, before[:])
-            if t < 2:
-                pick(third_before[:, t, :], t, list3, HALF, CHUNK)
-            if t == 1:
-                for i in range(2):
-                    pick(third_after[:, i, :], i, list2, HALF, CHUNK)
-                subtract(x_diff[2][:, 0:2, :], third_after[:], third_before[:])
-        last_before = [at([P, CHUNK], F32, f"last_before{c}", LAST_BEFORE[c]) for c in range(2)]
+        gpsimd_copy(*wd_views(0, "m t j"))
+        for t in range(2):
+            before = at([P, EARLY], F32, f"before{t}", PICKS + 8 * KIB * t)
+            after = at([P, EARLY], F32, f"after{t}", PICKS + 8 * KIB * t + 4 * KIB)
+            pick(before[:], t, list3, 0, EARLY)
+            pick(after[:], t, list2, 0, EARLY)
+            nc.gpsimd.tensor_tensor(out=diff[:, t, 0:EARLY], in0=after[:], in1=before[:], op=SUBTRACT)
+        before2 = [at([P, CHUNK], F32, f"before2_{c}", BEFORE2 + KIB * c) for c in range(2)]
         for c in range(2):
-            pick(last_before[c][:], PACK - 1, list3, c * CHUNK, CHUNK)
+            pick(before2[c][:], 2, list3, c * CHUNK, CHUNK)
+        pick(diff[:, 2, 0:HALF], 3, list3, 0, HALF)
         for c in range(2):
-            pick_diff(c, PACK - 1, last_before[c][:])
-        wd_woven1, dst, src = wd_views(1, WD_WOVEN1, "m j t")
+            pick_diff(c, 3, x_diff[c][:, 2, :])
+        for c in range(2):
+            pick_diff(c, 2, before2[c][:])
+        dst, src = wd_views(1, "m j t")
         nc.scalar.copy(out=dst, in_=src)
         for c in range(2):
             weave_x(c)
-        for i in range(2):
-            both_banks = at([P, 2, BANK], F32, f"last_clim{i}", LAST_CLIM + 4 * KIB * i)
-            clim_sb.append([both_banks[:, b, :] for b in range(2)])
-            clim(last - 1 + i)
-        for a, woven in enumerate((wd_woven0, wd_woven1)):
-            quantise_wd(a, woven, at([P, PASS], U8, f"wd_s{a}", WD_SCALES + PASS * a))
-        quantise_x(0, held([P, CHUNK], U32, "x_w0"))
-        wd_woven2 = weave_wd_on_gpsimd(2, WD_WOVEN2)
-        obs_sb.append(at([P, 2, S], F32, "obs0", OBS0))
-        obs_sb.append(at([P, 2, S], F32, "obs1", OBS1))
-        obs_sb.append(held([P, 2, S], F32, "wd_raw2"))
-        for g, obs_pair in enumerate(obs_sb):
-            nc.sync.dma_start(out=obs_pair[:], in_=obs_rows[:, 2 * g : 2 * g + 2, :])
+        for u in (last - 1, last):
+            clim(u)
+        for a in range(2):
+            quantise_wd(a, at([P, PASS], U8, f"wd_s{a}", BEFORE2 + PASS * a))
+        late_before = [at([P, HALF], F32, f"late_before{i}", LATE_BEFORE[i]) for i in range(2)]
+        pick(late_before[0][:], 2, list3, HALF, HALF)
+        quantise_x(0, held([P, CHUNK], U8, "x_s0"))
+        gpsimd_copy(*wd_views(2, "m t j"))
+        pick(late_before[1][:], 3, list3, HALF, HALF)
+        obs_sb = at([P, N_TILES, S], F32, "obs_sb", OBS)
+        for g in range(N_TILES // 2):
+            nc.sync.dma_start(out=obs_sb[:, 2 * g : 2 * g + 2, :], in_=obs_rows[:, 2 * g : 2 * g + 2, :])
 
-        late_before = {}
-
-        def pick_late_before(step, tile):
-            c, first = late[step]
+        def late_diffs(c, first):
             for i in range(2):
-                pick(tile[:, i, :], first + i, list3, c * CHUNK, CHUNK)
-            late_before[step] = tile
+                if first == 2:
+                    pick_diff(c, 2 + i, late_before[i][:, (c - 2) * CHUNK : (c - 1) * CHUNK])
+                else:
+                    pick_diff(c, i, last_before[:, i, :])
 
-        pick_late_before(1, at([P, 2, CHUNK], F32, "late_before1", LATE_BEFORE))
+        group_of = {u: g for g in GROUPS for u in g}
+        closes = {g[-1] + 2: g for g in GROUPS}
+        woven = {}
+        waiting = []
+        x_due = {3: 2, 7: 3}
+        last_before = on_clim([P, 2, CHUNK], F32, "last_before", 2, 0)
+        open_groups = []
+
+        def open_group(g):
+            woven[g] = at([P, len(g) * UNIT], BF16, f"group{g[0]}", TRIPLE if len(g) > 2 else WD_WOVEN[2])
+            open_groups.append(g)
+
+        def weave_ready(step):
+            while waiting and waiting[0] <= step and group_of[waiting[0]] in open_groups:
+                u = waiting.pop(0)
+                g = group_of[u]
+                i = g.index(u)
+                weave_h(u, woven[g][:, i * UNIT : (i + 1) * UNIT])
+
+        def close_group(g, scales):
+            weave_ready(last)
+            quantise_group(g, woven[g][:], scales)
+            k = GROUPS.index(g)
+            if k + 1 < len(GROUPS):
+                open_group(GROUPS[k + 1])
+            for u in g:
+                ready(u)
+
+        alone = {}
+
+        def ready(u):
+            c, a = units[u]
+            if a == R_PASSES - 1:
+                for n in range(0, N_TILES, 2):
+                    pending.append((c, (n, n + 1), corr_bank()))
+
+        def weave_alone(u):
+            alone[u] = held([P, UNIT], BF16, f"alone{u % 2}")
+            if KINDS[u] == "V":
+                woven_gain(nc.vector, u, alone[u][:], tanh_sb[u][:])
+            else:
+                nc.vector.tensor_copy(
+                    out=walk_out(alone[u][:]), in_=walk_in(h_planes[u][:].rearrange("p (t j) -> p t j", t=PACK))
+                )
+
+        def quantise_alone(u):
+            h_w[u] = held([P, CHUNK], U32, f"h_w{u}")
+            h_s[u] = held([P, CHUNK], U8, f"h_s{u}")
+            quantise(h_w[u][:], h_s[u][:], alone[u][:])
+            ready(u)
+
         for step in range(last + 1):
             product(step)
             if step < last:
-                apply_gain(step)
-            done = []
-            if step - 2 >= paired:
-                quantise_h(step - 2)
-                done.append(step - 2)
-            if pending:
-                put_out(by_tiles(clim_sb[step][0]))
-            if step == paired:
-                put_out(by_tiles(clim_sb[step][1]))
-            if step + 1 in late and step > 0:
-                pick_late_before(step + 1, on_clim([P, 2, CHUNK], F32, f"late_before{step + 1}", step, 0))
+                if KINDS[step] in "PX":
+                    apply_gain(step)
+                if step in group_of:
+                    waiting.append(step)
+            for k in range(2 if step == 8 else 1):
+                if pending:
+                    put_out(clim_sb[step][k])
             if step == 1:
-                quantise_x(1, on_clim([P, CHUNK], U32, "x_w1", 1, 0, KIB))
-                quantise_wd(2, wd_woven2, on_clim([P, PASS], U8, "wd_s2", 1, 0))
-            if step in late:
-                c, first = late[step]
+                quantise_x(1, on_clim([P, CHUNK], U8, "x_s1", 1, 0, KIB))
+                late_diffs(2, 2)
+                quantise_wd(2, on_clim([P, PASS], U8, "wd_s2", 1, 0))
+                open_group(GROUPS[0])
+                weave_x(2)
+            elif step in late:
+                late_diffs(*late[step])
+                if step == 5:
+                    weave_x(3)
+            if step == 2:
                 for i in range(2):
-                    pick_diff(c, first + i, late_before[step][:, i, :])
-            if step == 1:
-                pair = at([P, 2 * UNIT], BF16, "pair1", H_PAIR)
-                weave_h(0, pair[:, 0:UNIT])
-            if step in late and late[step][1] == 2:
-                weave_x(late[step][0])
-            if step - 2 in late and late[step - 2][1] == 2:
-                c = late[step - 2][0]
-                x_s[c] = on_clim([P, CHUNK], U8, f"x_s{c}", step, 1, 3 * BANK)
-                quantise_x(c, held([P, CHUNK], U32, f"x_w{c}"))
-            if step % 2 == 1 and 3 <= step <= paired + 1:
-                quantise_pair(step - 3, pair, step)
-                done += [step - 3, step - 2]
-                pair = at([P, 2 * UNIT], BF16, f"pair{step}", H_PAIR)
-                weave_h(step - 1, pair[:, 0:UNIT])
-            if step % 2 == 0 and 2 <= step <= paired:
-                weave_h(step - 1, pair[:, UNIT:])
-            if step - 1 > paired:
-                weave_h(step - 1, held([P, UNIT], BF16, f"h_woven{step % 2}")[:])
-            for u in done:
-                c, a = units[u]
-                if a == R_PASSES - 1:
-                    for n in range(0, N_TILES, 2):
-                        pending.append((c, (n, n + 1), corr_bank()))
+                    pick(last_before[:, i, :], i, list3, EARLY, CHUNK)
+            if step in x_due:
+                quantise_x(x_due[step], on_clim([P, CHUNK], U8, f"x_s{x_due[step]}", step, 1, KIB))
+            if step in closes:
+                close_group(closes[step], on_clim([P, len(closes[step]) * CHUNK], U8, f"group_s{step}", step, 1)[:])
+            weave_ready(step - 1)
+            if step - 2 in alone:
+                quantise_alone(step - 2)
+            if step > 0 and step - 1 not in group_of:
+                weave_alone(step - 1)
 
         h_w[last] = held([P, CHUNK], U32, f"h_w{last}")
-        put_out()
-        quantise_h(last - 1)
-        quantise_part = [last_unit_part(part) for part in range(2)]
-        parts = [(0, (banks[1], banks[4])), (P, (banks[5], banks[6]))]
-        groups = ((0, 1, 2, 3), (4, 5))
+        h_s[last] = held([P, CHUNK], U8, f"h_s{last}")
         c = units[last][0]
-        for a in range(R_PASSES - 1):
-            for o, part_banks in parts:
-                for tiles, bank in zip(groups, part_banks):
+        parts = [(0, (banks[1], banks[4])), (P, (banks[5], banks[6]))]
+        tile_groups = ((0, 1, 2, 3), (4, 5))
+
+        def last_passes(a, which):
+            for o, part_banks in which:
+                for tiles, bank in zip(tile_groups, part_banks):
                     corr_passes(c, o, P, tiles, a, bank)
-        for (o, part_banks), quantise_it in zip(parts, quantise_part):
-            quantise_it()
-            for tiles, bank in zip(groups, part_banks):
-                corr_passes(c, o, P, tiles, R_PASSES - 1, bank)
-        put_out(ring.tile([P, 2, CHUNK], F32, name="end_woven", align_bytes=64)[:])
-        for o, part_banks in parts:
-            for tiles, bank in zip(groups, part_banks):
-                finish(c, o, P, tiles, bank)
+
+        quantise_part = {}
+        for move in "s q a0 a1 g0 g1 Q0 Q1 s f0 f1".split():
+            if move == "s":
+                put_out()
+            elif move == "G":
+                close_group(GROUPS[-1], held([P, len(GROUPS[-1]) * CHUNK], U8, "group_s_end")[:])
+            elif move == "w":
+                weave_alone(last - 1)
+            elif move == "q":
+                quantise_alone(last - 1)
+            elif move[0] == "a":
+                last_passes(int(move[1]), parts)
+            elif move[0] == "g":
+                quantise_part[move[1]] = last_unit_part(int(move[1]))
+            elif move[0] == "Q":
+                quantise_part[move[1]]()
+                last_passes(R_PASSES - 1, parts[int(move[1]) : int(move[1]) + 1])
+            elif move[0] == "f":
+                o, part_banks = parts[int(move[1])]
+                for tiles, bank in zip(tile_groups, part_banks):
+                    finish(c, o, P, tiles, bank)

@@ -49,7 +49,7 @@ CLIM = 48 * KIB
 Z = 96 * KIB
 TRIPLE = 6 * KIB - 256
 
-KINDS = "PPPPPPPPPPXQ"
+KINDS = "PPPPPPPPPPXV"
 GROUPS = ((0, 1), (2, 3), (4, 5), (6, 7, 8), (9,))
 Z_RING = 2
 
@@ -90,8 +90,8 @@ def tile_list_argo_cast_check_kernel(
         list3 = keep.tile([P, S // 16], U16, name="list3")
         tab_w = at([P, T], I32, "tab_w", TAB_W)
         tab_s = at([P, T], U8, "tab_s", TAB_S)
-        wc_w_raw = held([P, 2 * H], U8, "wc_w_raw")
-        wc_s_raw = at([P, H], U8, "wc_s_raw", WC_S_RAW)
+        wc_w_raw = [held([P, 2 * H], U8, "wc_w_raw0")]
+        wc_s_raw = [at([P, PASS], U8, "wc_s_raw0", V_W1 - 256), held([P, 2 * PASS], U8, "wc_s_raw1")]
         wc_w = [held([P, 2 * PASS], U8, f"wc_w{a}") for a in range(R_PASSES)]
         wc_s = [held([P, PASS], U8, f"wc_s{a}") for a in range(R_PASSES)]
         wo_w = held([P, R_PASSES, N], I32, "wo_w")
@@ -106,7 +106,8 @@ def tile_list_argo_cast_check_kernel(
         ]
 
         nc.vector.memset(tab_s[:].bitcast(I32), 0)
-        nc.vector.memset(wc_s_raw[:].bitcast(I32), 0)
+        for raw in wc_s_raw:
+            nc.vector.memset(raw[:].bitcast(I32), 0)
         nc.vector.memset(wo_s[:].rearrange("p a n -> p (a n)").bitcast(I32), 0)
 
         x_rows = xT.rearrange("(p t) c -> p t c", t=PACK)
@@ -126,14 +127,15 @@ def tile_list_argo_cast_check_kernel(
         def load_wd(a):
             nc.sync.dma_start(out=wd_raw[a], in_=wd_rows[:, :, a * PASS : (a + 1) * PASS])
 
-        nc.sync.dma_start(out=wc_w_raw[:].bitcast(I32), in_=wc_words[0].bitcast(I32))
+        nc.sync.dma_start(out=wc_w_raw[0][:].bitcast(I32), in_=wc_words[0].bitcast(I32))
         load_scale_rows(tab_s, tab_scales[0])
         nc.sync.dma_start(out=list1[:], in_=offs)
         nc.sync.dma_start(out=tab_w[:], in_=tab_words[0].rearrange("p c i -> p (c i)").bitcast(I32))
-        load_scale_rows(wc_s_raw, wc_scales[0])
+        load_scale_rows(wc_s_raw[0], wc_scales[0][:, 0:PASS])
         nc.sync.dma_start(out=list3[:], in_=offs3)
-        nc.sync.dma_start(out=list2[:], in_=offs2)
         load_x(0)
+        nc.sync.dma_start(out=list2[:], in_=offs2)
+        load_scale_rows(wc_s_raw[1], wc_scales[0][:, PASS:])
         load_wd(0)
         for t in range(1, PACK):
             load_x(t)
@@ -150,13 +152,13 @@ def tile_list_argo_cast_check_kernel(
         def deal_words(a):
             nc.scalar.copy(
                 out=wc_w[a][:].bitcast(U16).rearrange("p (t m) -> p t m", t=PACK),
-                in_=wc_w_raw[:, 2 * PASS * a : 2 * PASS * (a + 1)].bitcast(U16).rearrange("p (m t) -> p t m", t=PACK),
+                in_=wc_w_raw[0][:, 2 * PASS * a : 2 * PASS * (a + 1)].bitcast(U16).rearrange("p (m t) -> p t m", t=PACK),
             )
 
         def deal_scales(a):
-            nc.vector.tensor_copy(
+            (nc.gpsimd if a else nc.vector).tensor_copy(
                 out=wc_s[a][:].rearrange("p (t m) -> p t m", t=PACK),
-                in_=wc_s_raw[:, PASS * a : PASS * (a + 1)].rearrange("p (m t) -> p t m", t=PACK),
+                in_=wc_s_raw[min(a, 1)][:, PASS * (a // 2) : PASS * (a // 2 + 1)].rearrange("p (m t) -> p t m", t=PACK),
             )
 
         def entries(lst, j0, width):
@@ -240,16 +242,22 @@ def tile_list_argo_cast_check_kernel(
             x_s[c] = scales
             quantise(x_w[c][:], scales[:], x_woven[c][:])
 
-        def first_stage(u, b, bank, w_codes, w_scales, rhs_w, rhs_s):
+        def bank_work(u, b):
+            a = units[u][1]
+            if u >= last - 2:
+                part, a = divmod(2 * (u - last + 2) + b, R_PASSES)
+                return a, [(t, part * P, P) for t in range(PACK)]
             if KINDS[u] in "PX":
-                parts = [(2 * b + s, 0, CHUNK) for s in range(2)]
-            else:
-                parts = [(t, b * P, P) for t in range(PACK)]
+                return a, [(2 * b + s, 0, CHUNK) for s in range(2)]
+            return a, [(t, b * P, P) for t in range(PACK)]
+
+        def first_stage(u, b, bank, w_codes, w_scales, rhs_w, rhs_s):
+            a, parts = bank_work(u, b)
             for s, (t, o, width) in enumerate(parts):
                 nc.tensor.matmul_mx(
                     out=bank[:, s * width : (s + 1) * width],
-                    lhsT=w_codes(t),
-                    lhsT_scale=w_scales[:, P * t : P * (t + 1)],
+                    lhsT=w_codes(a, t),
+                    lhsT_scale=w_scales[a][:, P * t : P * (t + 1)],
                     rhs=rhs_w[:, o : o + width].bitcast(FP8X4),
                     rhs_scale=rhs_s[:, o : o + width],
                     start=True,
@@ -282,8 +290,8 @@ def tile_list_argo_cast_check_kernel(
                     u,
                     b,
                     bank,
-                    lambda t: wc_w[a][:, 2 * P * t : 2 * P * (t + 1)].bitcast(FP4X4),
-                    wc_s[a],
+                    lambda a, t: wc_w[a][:, 2 * P * t : 2 * P * (t + 1)].bitcast(FP4X4),
+                    wc_s,
                     v_w[half][:, o : o + CHUNK],
                     v_s[:, c * CHUNK : (c + 1) * CHUNK],
                 )
@@ -300,7 +308,7 @@ def tile_list_argo_cast_check_kernel(
             for b in range(2):
                 bank = drift_bank()
                 first_stage(
-                    u, b, bank, lambda t: wd_w[a][:, P * t : P * (t + 1)].bitcast(FP8X4), wd_s[a], x_w[c][:], x_s[c][:]
+                    u, b, bank, lambda a, t: wd_w[a][:, P * t : P * (t + 1)].bitcast(FP8X4), wd_s, x_w[c][:], x_s[c][:]
                 )
                 cols = z[:, b * BANK : (b + 1) * BANK]
                 nc.vector.tensor_tensor(
@@ -318,28 +326,32 @@ def tile_list_argo_cast_check_kernel(
         def apply_gain(u):
             planes = ring.tile([P, UNIT], BF16, name="h_planes", bufs=4)
             h_planes[u] = planes
-            for t in range(PACK):
-                cols = slice(t * CHUNK, (t + 1) * CHUNK)
-                nc.scalar.activation(
-                    out=planes[:, cols], in_=tanh_sb[u][:, cols], func=COPY, scale=gains[:, units[u][1], t : t + 1]
-                )
+            for b in range(2):
+                a, parts = bank_work(u, b)
+                for s, (t, o, width) in enumerate(parts):
+                    cols = slice(b * BANK + s * width, b * BANK + (s + 1) * width)
+                    nc.scalar.activation(
+                        out=planes[:, cols], in_=tanh_sb[u][:, cols], func=COPY, scale=gains[:, a, t : t + 1]
+                    )
 
-        def woven_gain(engine, u, dst, src):
+        def woven_gain(engine, a, dst, src):
             width = src.shape[1] // PACK
             engine.tensor_tensor(
                 out=dst.rearrange("p (j t) -> p j t", t=PACK),
                 in0=src.rearrange("p (j t) -> p j t", t=PACK),
-                in1=gains[:, units[u][1], :].unsqueeze(1).to_broadcast([P, width, PACK]),
+                in1=gains[:, a, :].unsqueeze(1).to_broadcast([P, width, PACK]),
                 op=MULT,
             )
 
         def weave_h(u, woven):
             if KINDS[u] == "P":
+                g = 2 if u >= last - 2 else 1
                 gpsimd_copy(
-                    woven.rearrange("p (j t) -> p j t", t=PACK), h_planes[u][:].rearrange("p (t j) -> p j t", t=PACK)
+                    woven.rearrange("p (g j t) -> p g j t", g=g, t=PACK),
+                    h_planes[u][:].rearrange("p (g t j) -> p g j t", g=g, t=PACK),
                 )
             else:
-                woven_gain(nc.gpsimd if KINDS[u] == "G" else nc.vector, u, woven, tanh_sb[u][:])
+                woven_gain(nc.gpsimd if KINDS[u] == "G" else nc.vector, units[u][1], woven, tanh_sb[u][:])
 
         def quantise_group(group, woven, scales):
             codes = held([P, len(group) * CHUNK], U32, f"group_w{group[0]}")
@@ -354,12 +366,12 @@ def tile_list_argo_cast_check_kernel(
             woven = held([P, PACK * P], BF16, f"end_woven{part}")
             src = tanh_sb[last][:, part * BANK : (part + 1) * BANK]
             if KINDS[last] == "V":
-                woven_gain(nc.vector, last, woven[:], src)
+                woven_gain(nc.vector, part + 1, woven[:], src)
             else:
                 planes = held([P, PACK, P], BF16, f"end_planes{part}")
                 for t in range(PACK):
                     nc.scalar.activation(
-                        out=planes[:, t, :], in_=src[:, t * P : (t + 1) * P], func=COPY, scale=gains[:, units[last][1], t : t + 1]
+                        out=planes[:, t, :], in_=src[:, t * P : (t + 1) * P], func=COPY, scale=gains[:, part + 1, t : t + 1]
                     )
                 nc.vector.tensor_copy(out=walk_out(woven[:]), in_=walk_in(planes[:]))
             cols = slice(part * P, (part + 1) * P)
@@ -395,7 +407,7 @@ def tile_list_argo_cast_check_kernel(
                 corr_passes(c, 0, CHUNK, tiles, a, bank)
             finish(c, 0, CHUNK, tiles, bank, room)
 
-        for u in range(last - 1):
+        for u in sorted(range(last - 1), key=lambda u: units[u][1]):
             clim(u)
         gpsimd_copy(*wd_views(0, "m t j"))
         for t in range(2):
@@ -420,28 +432,30 @@ def tile_list_argo_cast_check_kernel(
             clim(u)
         for a in range(2):
             quantise_wd(a, at([P, PASS], U8, f"wd_s{a}", BEFORE2 + PASS * a))
-        late_before = [at([P, HALF], F32, f"late_before{i}", LATE_BEFORE[i]) for i in range(2)]
-        pick(late_before[0][:], 2, list3, HALF, HALF)
+        late_before = {}
+
+        def pick_late(c, t, tile):
+            late_before[c, t] = tile
+            pick(tile, t, list3, c * CHUNK, CHUNK)
+
         quantise_x(0, held([P, CHUNK], U8, "x_s0"))
         gpsimd_copy(*wd_views(2, "m t j"))
-        pick(late_before[1][:], 3, list3, HALF, HALF)
+        first_late = at([P, 2, CHUNK], F32, "first_late", LATE_BEFORE[1])
+        for i in range(2):
+            pick_late(2, 2 + i, first_late[:, i, :])
         obs_sb = at([P, N_TILES, S], F32, "obs_sb", OBS)
         for g in range(N_TILES // 2):
             nc.sync.dma_start(out=obs_sb[:, 2 * g : 2 * g + 2, :], in_=obs_rows[:, 2 * g : 2 * g + 2, :])
 
         def late_diffs(c, first):
             for i in range(2):
-                if first == 2:
-                    pick_diff(c, 2 + i, late_before[i][:, (c - 2) * CHUNK : (c - 1) * CHUNK])
-                else:
-                    pick_diff(c, i, last_before[:, i, :])
+                pick_diff(c, first + i, late_before[c, first + i])
 
         group_of = {u: g for g in GROUPS for u in g}
         closes = {g[-1] + 2: g for g in GROUPS}
         woven = {}
         waiting = []
         x_due = {3: 2, 7: 3}
-        last_before = on_clim([P, 2, CHUNK], F32, "last_before", 2, 0)
         open_groups = []
 
         def open_group(g):
@@ -475,10 +489,13 @@ def tile_list_argo_cast_check_kernel(
         def weave_alone(u):
             alone[u] = held([P, UNIT], BF16, f"alone{u % 2}")
             if KINDS[u] == "V":
-                woven_gain(nc.vector, u, alone[u][:], tanh_sb[u][:])
+                for b in range(2):
+                    cols = slice(b * BANK, (b + 1) * BANK)
+                    woven_gain(nc.vector, bank_work(u, b)[0], alone[u][:, cols], tanh_sb[u][:, cols])
             else:
                 nc.vector.tensor_copy(
-                    out=walk_out(alone[u][:]), in_=walk_in(h_planes[u][:].rearrange("p (t j) -> p t j", t=PACK))
+                    out=alone[u][:].rearrange("p (g c i t) -> p g c t i", g=2, i=4, t=PACK),
+                    in_=h_planes[u][:].rearrange("p (g t c i) -> p g c t i", g=2, i=4, t=PACK),
                 )
 
         def quantise_alone(u):
@@ -507,9 +524,8 @@ def tile_list_argo_cast_check_kernel(
                 late_diffs(*late[step])
                 if step == 5:
                     weave_x(3)
-            if step == 2:
-                for i in range(2):
-                    pick(last_before[:, i, :], i, list3, EARLY, CHUNK)
+            for i, t in enumerate({0: (0,), 2: (1,), 4: (2, 3)}.get(step, ())):
+                pick_late(3, t, on_clim([P, CHUNK], F32, f"late{t}", step, 0, i * KIB)[:])
             if step in x_due:
                 quantise_x(x_due[step], on_clim([P, CHUNK], U8, f"x_s{x_due[step]}", step, 1, KIB))
             if step in closes:
@@ -524,30 +540,37 @@ def tile_list_argo_cast_check_kernel(
         h_s[last] = held([P, CHUNK], U8, f"h_s{last}")
         c = units[last][0]
         parts = [(0, (banks[1], banks[4])), (P, (banks[5], banks[6]))]
-        tile_groups = ((0, 1, 2, 3), (4, 5))
+        tile_groups = ((0, 1, 2), (3, 4, 5))
 
-        def last_passes(a, which):
-            for o, part_banks in which:
-                for tiles, bank in zip(tile_groups, part_banks):
-                    corr_passes(c, o, P, tiles, a, bank)
+        def last_passes(part, a):
+            u, b = divmod(R_PASSES * part + a, 2)
+            u += last - 2
+            for tiles, bank in zip(tile_groups, parts[part][1]):
+                for s, n in enumerate(tiles):
+                    nc.tensor.matmul_mx(
+                        out=bank[:, s * P : (s + 1) * P],
+                        lhsT=wo_w[:, a, P * n : P * (n + 1)].bitcast(FP8X4),
+                        lhsT_scale=wo_s[:, a, P * n : P * (n + 1)],
+                        rhs=h_w[u][:, b * P : (b + 1) * P].bitcast(FP8X4),
+                        rhs_scale=h_s[u][:, b * P : (b + 1) * P],
+                        start=(a == 0 and s == 0),
+                        stop=(a == R_PASSES - 1 and s == len(tiles) - 1),
+                    )
 
         quantise_part = {}
-        for move in "s q a0 a1 g0 g1 Q0 Q1 s f0 f1".split():
+        for move in "a00 a01 s q a02 a10 g0 s g1 Q0 a11 Q1 a12 f0 f1".split():
             if move == "s":
                 put_out()
-            elif move == "G":
-                close_group(GROUPS[-1], held([P, len(GROUPS[-1]) * CHUNK], U8, "group_s_end")[:])
             elif move == "w":
                 weave_alone(last - 1)
             elif move == "q":
                 quantise_alone(last - 1)
             elif move[0] == "a":
-                last_passes(int(move[1]), parts)
+                last_passes(int(move[1]), int(move[2]))
             elif move[0] == "g":
                 quantise_part[move[1]] = last_unit_part(int(move[1]))
             elif move[0] == "Q":
                 quantise_part[move[1]]()
-                last_passes(R_PASSES - 1, parts[int(move[1]) : int(move[1]) + 1])
             elif move[0] == "f":
                 o, part_banks = parts[int(move[1])]
                 for tiles, bank in zip(tile_groups, part_banks):

@@ -90,8 +90,8 @@ def tile_list_argo_cast_check_kernel(
         list3 = keep.tile([P, S // 16], U16, name="list3")
         tab_w = at([P, T], I32, "tab_w", TAB_W)
         tab_s = at([P, T], U8, "tab_s", TAB_S)
-        wc_w_raw = [held([P, 2 * H], U8, "wc_w_raw0")]
-        wc_s_raw = [at([P, PASS], U8, "wc_s_raw0", V_W1 - 256), held([P, 2 * PASS], U8, "wc_s_raw1")]
+        wc_w_raw = held([P, 2 * H], U8, "wc_w_raw")
+        wc_s_raw = at([P, H], U8, "wc_s_raw", WC_S_RAW)
         wc_w = [held([P, 2 * PASS], U8, f"wc_w{a}") for a in range(R_PASSES)]
         wc_s = [held([P, PASS], U8, f"wc_s{a}") for a in range(R_PASSES)]
         wo_w = held([P, R_PASSES, N], I32, "wo_w")
@@ -106,8 +106,7 @@ def tile_list_argo_cast_check_kernel(
         ]
 
         nc.vector.memset(tab_s[:].bitcast(I32), 0)
-        for raw in wc_s_raw:
-            nc.vector.memset(raw[:].bitcast(I32), 0)
+        nc.vector.memset(wc_s_raw[:].bitcast(I32), 0)
         nc.vector.memset(wo_s[:].rearrange("p a n -> p (a n)").bitcast(I32), 0)
 
         x_rows = xT.rearrange("(p t) c -> p t c", t=PACK)
@@ -127,15 +126,14 @@ def tile_list_argo_cast_check_kernel(
         def load_wd(a):
             nc.sync.dma_start(out=wd_raw[a], in_=wd_rows[:, :, a * PASS : (a + 1) * PASS])
 
-        nc.sync.dma_start(out=wc_w_raw[0][:].bitcast(I32), in_=wc_words[0].bitcast(I32))
+        nc.sync.dma_start(out=wc_w_raw[:].bitcast(I32), in_=wc_words[0].bitcast(I32))
         load_scale_rows(tab_s, tab_scales[0])
         nc.sync.dma_start(out=list1[:], in_=offs)
         nc.sync.dma_start(out=tab_w[:], in_=tab_words[0].rearrange("p c i -> p (c i)").bitcast(I32))
-        load_scale_rows(wc_s_raw[0], wc_scales[0][:, 0:PASS])
+        load_scale_rows(wc_s_raw, wc_scales[0])
         nc.sync.dma_start(out=list3[:], in_=offs3)
-        load_x(0)
         nc.sync.dma_start(out=list2[:], in_=offs2)
-        load_scale_rows(wc_s_raw[1], wc_scales[0][:, PASS:])
+        load_x(0)
         load_wd(0)
         for t in range(1, PACK):
             load_x(t)
@@ -152,13 +150,13 @@ def tile_list_argo_cast_check_kernel(
         def deal_words(a):
             nc.scalar.copy(
                 out=wc_w[a][:].bitcast(U16).rearrange("p (t m) -> p t m", t=PACK),
-                in_=wc_w_raw[0][:, 2 * PASS * a : 2 * PASS * (a + 1)].bitcast(U16).rearrange("p (m t) -> p t m", t=PACK),
+                in_=wc_w_raw[:, 2 * PASS * a : 2 * PASS * (a + 1)].bitcast(U16).rearrange("p (m t) -> p t m", t=PACK),
             )
 
         def deal_scales(a):
-            (nc.gpsimd if a else nc.vector).tensor_copy(
+            nc.vector.tensor_copy(
                 out=wc_s[a][:].rearrange("p (t m) -> p t m", t=PACK),
-                in_=wc_s_raw[min(a, 1)][:, PASS * (a // 2) : PASS * (a // 2 + 1)].rearrange("p (m t) -> p t m", t=PACK),
+                in_=wc_s_raw[:, PASS * a : PASS * (a + 1)].rearrange("p (m t) -> p t m", t=PACK),
             )
 
         def entries(lst, j0, width):
@@ -407,7 +405,7 @@ def tile_list_argo_cast_check_kernel(
                 corr_passes(c, 0, CHUNK, tiles, a, bank)
             finish(c, 0, CHUNK, tiles, bank, room)
 
-        for u in sorted(range(last - 1), key=lambda u: units[u][1]):
+        for u in range(last - 1):
             clim(u)
         gpsimd_copy(*wd_views(0, "m t j"))
         for t in range(2):
@@ -419,7 +417,8 @@ def tile_list_argo_cast_check_kernel(
         before2 = [at([P, CHUNK], F32, f"before2_{c}", BEFORE2 + KIB * c) for c in range(2)]
         for c in range(2):
             pick(before2[c][:], 2, list3, c * CHUNK, CHUNK)
-        pick(diff[:, 2, 0:HALF], 3, list3, 0, HALF)
+        for c in range(2):
+            pick(x_diff[c][:, 2, :], 3, list3, c * CHUNK, CHUNK)
         for c in range(2):
             pick_diff(c, 3, x_diff[c][:, 2, :])
         for c in range(2):
@@ -524,7 +523,7 @@ def tile_list_argo_cast_check_kernel(
                 late_diffs(*late[step])
                 if step == 5:
                     weave_x(3)
-            for i, t in enumerate({0: (0,), 2: (1,), 4: (2, 3)}.get(step, ())):
+            for i, t in enumerate({2: (0, 1), 4: (2, 3)}.get(step, ())):
                 pick_late(3, t, on_clim([P, CHUNK], F32, f"late{t}", step, 0, i * KIB)[:])
             if step in x_due:
                 quantise_x(x_due[step], on_clim([P, CHUNK], U8, f"x_s{x_due[step]}", step, 1, KIB))

from contextlib import ExitStack

import concourse.mybir as mybir

K, T, S, H, N = 512, 2048, 1024, 1536, 768
FLOPS = 2 * S * (2 * K * H + H * N)

F32 = mybir.dt.float32
BF16 = mybir.dt.bfloat16
I32 = mybir.dt.int32
U32 = mybir.dt.uint32
U16 = mybir.dt.uint16
U8 = mybir.dt.uint8
FP8X4 = mybir.dt.float8_e4m3fn_x4
FP4X4 = mybir.dt.float4_e2m1fn_x4
MULT = mybir.AluOpType.mult
ADD = mybir.AluOpType.add
SUBTRACT = mybir.AluOpType.subtract
COPY = mybir.ActivationFunctionType.Copy
TANH = mybir.ActivationFunctionType.Tanh

P = 128
PACK = 4
PASS = P * PACK
BANK = 512
HALF = S // 2
CHUNK = S // 4
UNIT = PACK * CHUNK
R_PASSES = H // PASS
N_TILES = N // P
KIB = 1024


TAB_W = 0
WD_WOVEN = (0, 4 * KIB, 7 * KIB + 768)
TAB_S = 8 * KIB
WC_S_RAW = 112 * KIB
V_W1 = 113 * KIB
EARLY = 3 * CHUNK
X_WOVEN = (11 * KIB + 512, 19 * KIB, 0, 2 * KIB)
LATE_BEFORE = (4 * KIB, 11 * KIB + 768)
WD_RAW1 = 13 * KIB + 256
GROUP = 6 * KIB
PICKS = 22 * KIB
WD_RAW2 = 38 * KIB
OBS = PICKS
BEFORE2 = 46 * KIB
CLIM = 48 * KIB
Z = 96 * KIB
TRIPLE = 6 * KIB - 256

KINDS = "PPPPPPPPPPXV"
GROUPS = ((0, 1), (2, 3), (4, 5), (6, 7, 8), (9,))
Z_RING = 2


def rotation(items):
    turns = []

    def take():
        turns.append(None)
        return items[(len(turns) - 1) % len(items)]

    return take


def tile_list_argo_cast_check_kernel(
    tc, tab_words, tab_scales, wc_words, wc_scales, xT, wd, gain, wo_words, wo_scales, obs, offs, offs2, offs3, out
):
    nc = tc.nc
    with ExitStack() as ctx:
        keep = ctx.enter_context(tc.tile_pool(name="keep", bufs=1))
        ring = ctx.enter_context(tc.tile_pool(name="ring", bufs=2))
        arena = ctx.enter_context(tc.tile_pool(name="arena", bufs=1))
        psum = ctx.enter_context(tc.psum_pool(name="psum", bufs=1))

        def held(shape, dtype, name):
            return keep.tile(shape, dtype, name=name, align_bytes=64)

        def at(shape, dtype, name, offset):
            return arena.tile(shape, dtype, name=name, align_bytes=64, offset=offset)

        def on_clim(shape, dtype, name, u, b, offset=0):
            return at(shape, dtype, name, CLIM + (2 * u + b) * 4 * BANK + offset)

        banks = [psum.tile([P, BANK], F32, name=f"bank{b}") for b in range(8)]

        list1 = keep.tile([P, S // 16], U16, name="list1")
        list2 = keep.tile([P, S // 16], U16, name="list2")
        list3 = keep.tile([P, S // 16], U16, name="list3")
        tab_w = at([P, T], I32, "tab_w", TAB_W)
        tab_s = at([P, T], U8, "tab_s", TAB_S)
        wc_w_raw = held([P, 2 * H], U8, "wc_w_raw")
        wc_s_raw = at([P, H], U8, "wc_s_raw", WC_S_RAW)
        wc_w = [held([P, 2 * PASS], U8, f"wc_w{a}") for a in range(R_PASSES)]
        wc_s = [held([P, PASS], U8, f"wc_s{a}") for a in range(R_PASSES)]
        wo_w = held([P, R_PASSES, N], I32, "wo_w")
        wo_s = held([P, R_PASSES, N], U8, "wo_s")
        gains = held([P, R_PASSES, PACK], F32, "gains")
        x_planes = [held([P, T], F32, f"x_plane{t}") for t in range(PACK)]
        diff = held([P, PACK, S], F32, "diff")
        wd_raw = [
            diff[:, :, 0:HALF],
            at([P, PACK, PASS], F32, "wd_raw1", WD_RAW1)[:],
            at([P, PACK, PASS], F32, "wd_raw2", WD_RAW2)[:],
        ]

        nc.vector.memset(tab_s[:].bitcast(I32), 0)
        nc.vector.memset(wc_s_raw[:].bitcast(I32), 0)
        nc.vector.memset(wo_s[:].rearrange("p a n -> p (a n)").bitcast(I32), 0)

        x_rows = xT.rearrange("(p t) c -> p t c", t=PACK)
        wd_rows = wd.rearrange("(p j) c -> p j c", j=PACK)
        obs_rows = obs.rearrange("(n p) j -> p n j", p=P)
        out_rows = out.rearrange("(n p) j -> p n j", p=P)

        def load_scale_rows(tile, rows):
            for q in range(4):
                nc.sync.dma_start(
                    out=tile[32 * q : 32 * q + 4, :].bitcast(I32), in_=rows[4 * q : 4 * q + 4, :].bitcast(I32)
                )

        def load_x(t):
            nc.sync.dma_start(out=x_planes[t][:], in_=x_rows[:, t, :])

        def load_wd(a):
            nc.sync.dma_start(out=wd_raw[a], in_=wd_rows[:, :, a * PASS : (a + 1) * PASS])

        nc.sync.dma_start(out=wc_w_raw[:].bitcast(I32), in_=wc_words[0].bitcast(I32))
        load_scale_rows(tab_s, tab_scales[0])
        nc.sync.dma_start(out=list1[:], in_=offs)
        nc.sync.dma_start(out=tab_w[:], in_=tab_words[0].rearrange("p c i -> p (c i)").bitcast(I32))
        load_scale_rows(wc_s_raw, wc_scales[0])
        nc.sync.dma_start(out=list3[:], in_=offs3)
        nc.sync.dma_start(out=list2[:], in_=offs2)
        load_x(0)
        load_wd(0)
        for t in range(1, PACK):
            load_x(t)
        for a in range(1, R_PASSES):
            load_wd(a)
        nc.sync.dma_start(out=gains[:], in_=gain.rearrange("(a p t) -> p a t", p=P, t=PACK))
        for q in range(4):
            nc.sync.dma_start(
                out=wo_s[32 * q : 32 * q + 4, :, :].bitcast(I32),
                in_=wo_scales[:, 4 * q : 4 * q + 4, :].rearrange("a r n -> r a n").bitcast(I32),
            )
        nc.sync.dma_start(out=wo_w[:], in_=wo_words.rearrange("a p c i -> p a (c i)").bitcast(I32))

        def deal_words(a):
            nc.scalar.copy(
                out=wc_w[a][:].bitcast(U16).rearrange("p (t m) -> p t m", t=PACK),
                in_=wc_w_raw[:, 2 * PASS * a : 2 * PASS * (a + 1)].bitcast(U16).rearrange("p (m t) -> p t m", t=PACK),
            )

        def deal_scales(a):
            nc.vector.tensor_copy(
                out=wc_s[a][:].rearrange("p (t m) -> p t m", t=PACK),
                in_=wc_s_raw[:, PASS * a : PASS * (a + 1)].rearrange("p (m t) -> p t m", t=PACK),
            )

        def entries(lst, j0, width):
            return lst[:, j0 // 16 : (j0 + width) // 16]

        v_w = [held([P, HALF], U32, "v_w0"), at([P, HALF], U32, "v_w1", V_W1)]
        v_s = held([P, S], U8, "v_s")
        nc.vector.tensor_copy(out=v_s[:], in_=tab_s[:].indirect(list1[:]))

        def pick_words(half):
            nc.vector.tensor_copy(out=v_w[half][:], in_=tab_w[:].bitcast(U32).indirect(entries(list1, half * HALF, HALF)))

        pick_words(0)
        for a in range(R_PASSES):
            deal_words(a)
            deal_scales(a)
        pick_words(1)

        units = [(c, a) for c in range(S // CHUNK) for a in range(R_PASSES)]
        units[2], units[3] = units[3], units[2]
        last = len(units) - 1
        x_diff = [diff[:, :, c * CHUNK : (c + 1) * CHUNK] for c in range(S // CHUNK)]
        late = {1: (2, 2), 3: (3, 0), 5: (3, 2)}

        def clim_tile(u, b):
            if u in late and b == int(u == 1):
                c, t = late[u]
                return x_diff[c][:, t : t + 2, :]
            if u >= last - 1:
                return x_diff[u - last + 1][:, 2 * b : 2 * b + 2, :]
            return on_clim([P, 2, CHUNK], F32, f"clim{u}_{b}", u, b)[:]

        clim_sb = [[clim_tile(u, b) for b in range(2)] for u in range(last + 1)]

        def pick(dst, t, lst, j0, width):
            nc.vector.tensor_copy(out=dst, in_=x_planes[t][:].indirect(entries(lst, j0, width)))

        def pick_diff(c, t, before):
            nc.vector.tensor_tensor(
                out=x_diff[c][:, t, :],
                in0=x_planes[t][:].indirect(entries(list2, c * CHUNK, CHUNK)),
                in1=before,
                op=SUBTRACT,
            )

        def gpsimd_copy(dst, src):
            nc.gpsimd.tensor_scalar(out=dst, in0=src, scalar1=1.0, scalar2=0.0, op0=MULT, op1=ADD)

        def quantise(codes, scales, woven):
            nc.vector.quantize_mx(out=codes.bitcast(FP8X4), scales=scales, in_=woven)

        wd_w = [held([P, PASS], U32, f"wd_w{a}") for a in range(R_PASSES)]
        wd_s = {}
        wd_woven = {}

        def wd_views(a, walk):
            wd_woven[a] = at([P, PACK * PASS], BF16, f"wd_woven{a}", WD_WOVEN[a])
            dst = wd_woven[a][:].rearrange(f"p (t m j) -> p {walk}", t=PACK, j=PACK)
            return dst, wd_raw[a].rearrange(f"p j (m t) -> p {walk}", t=PACK)

        def quantise_wd(a, scales):
            wd_s[a] = scales
            quantise(wd_w[a][:], scales[:], wd_woven[a][:])

        def walk_out(dst):
            return dst.rearrange("p (c i t) -> p c t i", i=4, t=PACK)

        def walk_in(src):
            return src.rearrange("p t (c i) -> p c t i", i=4)

        x_w = {}
        x_s = {}
        x_woven = {}

        def weave_x(c):
            x_woven[c] = at([P, UNIT], BF16, f"x_woven{c}", X_WOVEN[c])
            nc.scalar.copy(out=walk_out(x_woven[c][:]), in_=walk_in(x_diff[c]))

        def quantise_x(c, scales):
            x_w[c] = held([P, CHUNK], U32, f"x_w{c}")
            x_s[c] = scales
            quantise(x_w[c][:], scales[:], x_woven[c][:])

        def bank_work(u, b):
            a = units[u][1]
            if u >= last - 2:
                part, a = divmod(2 * (u - last + 2) + b, R_PASSES)
                return a, [(t, part * P, P) for t in range(PACK)]
            if KINDS[u] in "PX":
                return a, [(2 * b + s, 0, CHUNK) for s in range(2)]
            return a, [(t, b * P, P) for t in range(PACK)]

        def first_stage(u, b, bank, w_codes, w_scales, rhs_w, rhs_s):
            a, parts = bank_work(u, b)
            for s, (t, o, width) in enumerate(parts):
                nc.tensor.matmul_mx(
                    out=bank[:, s * width : (s + 1) * width],
                    lhsT=w_codes(a, t),
                    lhsT_scale=w_scales[a][:, P * t : P * (t + 1)],
                    rhs=rhs_w[:, o : o + width].bitcast(FP8X4),
                    rhs_scale=rhs_s[:, o : o + width],
                    start=True,
                    stop=True,
                )

        def woven_kind(u):
            return KINDS[u] in "GV"

        def bank_view(u, bank):
            if woven_kind(u):
                return bank[:].rearrange("p (t g j) -> p g j t", t=PACK, g=2)
            return bank[:].rearrange("p (g j) -> p g j", g=2)

        def sb_view(u, two_rows):
            if woven_kind(u):
                return two_rows.rearrange("p g (j t) -> p g j t", t=PACK)
            return two_rows

        clim_bank = rotation(banks[4:] + banks[:4])
        drift_bank = rotation(banks[4:])
        corr_bank = rotation(banks[:4])

        def clim(u):
            c, a = units[u]
            half, o = divmod(c * CHUNK, HALF)
            for b in range(2):
                bank = clim_bank()
                first_stage(
                    u,
                    b,
                    bank,
                    lambda a, t: wc_w[a][:, 2 * P * t : 2 * P * (t + 1)].bitcast(FP4X4),
                    wc_s,
                    v_w[half][:, o : o + CHUNK],
                    v_s[:, c * CHUNK : (c + 1) * CHUNK],
                )
                nc.scalar.copy(out=sb_view(u, clim_sb[u][b]), in_=bank_view(u, bank))

        tanh_sb = {}
        z_slot = rotation(list(range(Z_RING)))
        own_slot = rotation([Z_RING, Z_RING + 1])

        def product(u):
            c, a = units[u]
            z = at([P, UNIT], F32, f"z{u}", Z + 4 * UNIT * z_slot())
            tanh_sb[u] = at([P, UNIT], F32, f"tanh{u}", Z + 4 * UNIT * own_slot()) if KINDS[u] == "G" else z
            for b in range(2):
                bank = drift_bank()
                first_stage(
                    u, b, bank, lambda a, t: wd_w[a][:, P * t : P * (t + 1)].bitcast(FP8X4), wd_s, x_w[c][:], x_s[c][:]
                )
                cols = z[:, b * BANK : (b + 1) * BANK]
                nc.vector.tensor_tensor(
                    out=sb_view(u, cols.rearrange("p (g j) -> p g j", g=2)),
                    in0=bank_view(u, bank),
                    in1=sb_view(u, clim_sb[u][b]),
                    op=MULT,
                )
                nc.scalar.activation(out=tanh_sb[u][:, b * BANK : (b + 1) * BANK], in_=cols, func=TANH)

        h_planes = {}
        h_w = {}
        h_s = {}

        def apply_gain(u):
            planes = ring.tile([P, UNIT], BF16, name="h_planes", bufs=4)
            h_planes[u] = planes
            for b in range(2):
                a, parts = bank_work(u, b)
                for s, (t, o, width) in enumerate(parts):
                    cols = slice(b * BANK + s * width, b * BANK + (s + 1) * width)
                    nc.scalar.activation(
                        out=planes[:, cols], in_=tanh_sb[u][:, cols], func=COPY, scale=gains[:, a, t : t + 1]
                    )

        def woven_gain(engine, a, dst, src):
            width = src.shape[1] // PACK
            engine.tensor_tensor(
                out=dst.rearrange("p (j t) -> p j t", t=PACK),
                in0=src.rearrange("p (j t) -> p j t", t=PACK),
                in1=gains[:, a, :].unsqueeze(1).to_broadcast([P, width, PACK]),
                op=MULT,
            )

        def weave_h(u, woven):
            if KINDS[u] == "P":
                g = 2 if u >= last - 2 else 1
                gpsimd_copy(
                    woven.rearrange("p (g j t) -> p g j t", g=g, t=PACK),
                    h_planes[u][:].rearrange("p (g t j) -> p g j t", g=g, t=PACK),
                )
            else:
                woven_gain(nc.gpsimd if KINDS[u] == "G" else nc.vector, units[u][1], woven, tanh_sb[u][:])

        def quantise_group(group, woven, scales):
            codes = held([P, len(group) * CHUNK], U32, f"group_w{group[0]}")
            for i0 in range(0, len(group), 2):
                i1 = min(i0 + 2, len(group))
                quantise(codes[:, i0 * CHUNK : i1 * CHUNK], scales[:, i0 * CHUNK : i1 * CHUNK], woven[:, i0 * UNIT : i1 * UNIT])
            for i, u in enumerate(group):
                cols = slice(i * CHUNK, (i + 1) * CHUNK)
                h_w[u], h_s[u] = codes[:, cols], scales[:, cols]

        def last_unit_part(part):
            woven = held([P, PACK * P], BF16, f"end_woven{part}")
            src = tanh_sb[last][:, part * BANK : (part + 1) * BANK]
            if KINDS[last] == "V":
                woven_gain(nc.vector, part + 1, woven[:], src)
            else:
                planes = held([P, PACK, P], BF16, f"end_planes{part}")
                for t in range(PACK):
                    nc.scalar.activation(
                        out=planes[:, t, :], in_=src[:, t * P : (t + 1) * P], func=COPY, scale=gains[:, part + 1, t : t + 1]
                    )
                nc.vector.tensor_copy(out=walk_out(woven[:]), in_=walk_in(planes[:]))
            cols = slice(part * P, (part + 1) * P)
            return lambda: quantise(h_w[last][:, cols], h_s[last][:, cols], woven[:])

        def corr_passes(c, o, width, tiles, a, bank):
            u = units.index((c, a))
            for s, n in enumerate(tiles):
                nc.tensor.matmul_mx(
                    out=bank[:, s * width : (s + 1) * width],
                    lhsT=wo_w[:, a, P * n : P * (n + 1)].bitcast(FP8X4),
                    lhsT_scale=wo_s[:, a, P * n : P * (n + 1)],
                    rhs=h_w[u][:, o : o + width].bitcast(FP8X4),
                    rhs_scale=h_s[u][:, o : o + width],
                    start=(a == 0 and s == 0),
                    stop=(a == R_PASSES - 1 and s == len(tiles) - 1),
                )

        def finish(c, o, width, tiles, bank, room=None):
            j0 = c * CHUNK + o
            rows = slice(tiles[0], tiles[-1] + 1)
            given = obs_sb[:, rows, j0 : j0 + width]
            sums = bank[:, 0 : len(tiles) * width].rearrange("p (s j) -> p s j", j=width)
            res = given if room is None else room
            nc.vector.tensor_tensor(out=res, in0=given, in1=sums, op=SUBTRACT)
            nc.sync.dma_start(out=out_rows[:, rows, j0 : j0 + width], in_=res)

        pending = []

        def put_out(room=None):
            c, tiles, bank = pending.pop(0)
            for a in range(R_PASSES):
                corr_passes(c, 0, CHUNK, tiles, a, bank)
            finish(c, 0, CHUNK, tiles, bank, room)

        for u in range(last - 1):
            clim(u)
        gpsimd_copy(*wd_views(0, "m t j"))
        for t in range(2):
            before = at([P, EARLY], F32, f"before{t}", PICKS + 8 * KIB * t)
            after = at([P, EARLY], F32, f"after{t}", PICKS + 8 * KIB * t + 4 * KIB)
            pick(before[:], t, list3, 0, EARLY)
            pick(after[:], t, list2, 0, EARLY)
            nc.gpsimd.tensor_tensor(out=diff[:, t, 0:EARLY], in0=after[:], in1=before[:], op=SUBTRACT)
        before2 = [at([P, CHUNK], F32, f"before2_{c}", BEFORE2 + KIB * c) for c in range(2)]
        for c in range(2):
            pick(before2[c][:], 2, list3, c * CHUNK, CHUNK)
        for c in range(2):
            pick(x_diff[c][:, 2, :], 3, list3, c * CHUNK, CHUNK)
        for c in range(2):
            pick_diff(c, 3, x_diff[c][:, 2, :])
        for c in range(2):
            pick_diff(c, 2, before2[c][:])
        dst, src = wd_views(1, "m j t")
        nc.scalar.copy(out=dst, in_=src)
        for c in range(2):
            weave_x(c)
        for u in (last - 1, last):
            clim(u)
        for a in range(2):
            quantise_wd(a, at([P, PASS], U8, f"wd_s{a}", BEFORE2 + PASS * a))
        late_before = {}

        def pick_late(c, t, tile):
            late_before[c, t] = tile
            pick(tile, t, list3, c * CHUNK, CHUNK)

        quantise_x(0, held([P, CHUNK], U8, "x_s0"))
        gpsimd_copy(*wd_views(2, "m t j"))
        first_late = at([P, 2, CHUNK], F32, "first_late", LATE_BEFORE[1])
        for i in range(2):
            pick_late(2, 2 + i, first_late[:, i, :])
        obs_sb = at([P, N_TILES, S], F32, "obs_sb", OBS)
        for g in range(N_TILES // 2):
            nc.sync.dma_start(out=obs_sb[:, 2 * g : 2 * g + 2, :], in_=obs_rows[:, 2 * g : 2 * g + 2, :])

        def late_diffs(c, first):
            for i in range(2):
                pick_diff(c, first + i, late_before[c, first + i])

        group_of = {u: g for g in GROUPS for u in g}
        closes = {g[-1] + 2: g for g in GROUPS}
        woven = {}
        waiting = []
        x_due = {3: 2, 7: 3}
        open_groups = []

        def open_group(g):
            woven[g] = at([P, len(g) * UNIT], BF16, f"group{g[0]}", TRIPLE if len(g) > 2 else WD_WOVEN[2])
            open_groups.append(g)

        def weave_ready(step):
            while waiting and waiting[0] <= step and group_of[waiting[0]] in open_groups:
                u = waiting.pop(0)
                g = group_of[u]
                i = g.index(u)
                weave_h(u, woven[g][:, i * UNIT : (i + 1) * UNIT])

        def close_group(g, scales):
            weave_ready(last)
            quantise_group(g, woven[g][:], scales)
            k = GROUPS.index(g)
            if k + 1 < len(GROUPS):
                open_group(GROUPS[k + 1])
            for u in g:
                ready(u)

        alone = {}

        def ready(u):
            c, a = units[u]
            if a == R_PASSES - 1:
                for n in range(0, N_TILES, 2):
                    pending.append((c, (n, n + 1), corr_bank()))

        def weave_alone(u):
            alone[u] = held([P, UNIT], BF16, f"alone{u % 2}")
            if KINDS[u] == "V":
                for b in range(2):
                    cols = slice(b * BANK, (b + 1) * BANK)
                    woven_gain(nc.vector, bank_work(u, b)[0], alone[u][:, cols], tanh_sb[u][:, cols])
            else:
                nc.vector.tensor_copy(
                    out=alone[u][:].rearrange("p (g c i t) -> p g c t i", g=2, i=4, t=PACK),
                    in_=h_planes[u][:].rearrange("p (g t c i) -> p g c t i", g=2, i=4, t=PACK),
                )

        def quantise_alone(u):
            h_w[u] = held([P, CHUNK], U32, f"h_w{u}")
            h_s[u] = held([P, CHUNK], U8, f"h_s{u}")
            quantise(h_w[u][:], h_s[u][:], alone[u][:])
            ready(u)

        for step in range(last + 1):
            product(step)
            if step < last:
                if KINDS[step] in "PX":
                    apply_gain(step)
                if step in group_of:
                    waiting.append(step)
            for k in range(2 if step == 8 else 1):
                if pending:
                    put_out(clim_sb[step][k])
            if step == 1:
                quantise_x(1, on_clim([P, CHUNK], U8, "x_s1", 1, 0, KIB))
                late_diffs(2, 2)
                quantise_wd(2, on_clim([P, PASS], U8, "wd_s2", 1, 0))
                open_group(GROUPS[0])
                weave_x(2)
            elif step in late:
                late_diffs(*late[step])
                if step == 5:
                    weave_x(3)
            for i, t in enumerate({2: (0, 1), 4: (2, 3)}.get(step, ())):
                pick_late(3, t, on_clim([P, CHUNK], F32, f"late{t}", step, 0, i * KIB)[:])
            if step in x_due:
                quantise_x(x_due[step], on_clim([P, CHUNK], U8, f"x_s{x_due[step]}", step, 1, KIB))
            if step in closes:
                close_group(closes[step], on_clim([P, len(closes[step]) * CHUNK], U8, f"group_s{step}", step, 1)[:])
            weave_ready(step - 1)
            if step - 2 in alone:
                quantise_alone(step - 2)
            if step > 0 and step - 1 not in group_of:
                weave_alone(step - 1)

        h_w[last] = held([P, CHUNK], U32, f"h_w{last}")
        h_s[last] = held([P, CHUNK], U8, f"h_s{last}")
        c = units[last][0]
        parts = [(0, (banks[1], banks[4])), (P, (banks[5], banks[6]))]
        tile_groups = ((0, 1, 2), (3, 4, 5))

        def last_passes(part, a):
            u, b = divmod(R_PASSES * part + a, 2)
            u += last - 2
            for tiles, bank in zip(tile_groups, parts[part][1]):
                for s, n in enumerate(tiles):
                    nc.tensor.matmul_mx(
                        out=bank[:, s * P : (s + 1) * P],
                        lhsT=wo_w[:, a, P * n : P * (n + 1)].bitcast(FP8X4),
                        lhsT_scale=wo_s[:, a, P * n : P * (n + 1)],
                        rhs=h_w[u][:, b * P : (b + 1) * P].bitcast(FP8X4),
                        rhs_scale=h_s[u][:, b * P : (b + 1) * P],
                        start=(a == 0 and s == 0),
                        stop=(a == R_PASSES - 1 and s == len(tiles) - 1),
                    )

        quantise_part = {}
        for move in "a00 a01 s q a02 a10 g0 s g1 Q0 a11 Q1 a12 f0 f1".split():
            if move == "s":
                put_out()
            elif move == "w":
                weave_alone(last - 1)
            elif move == "q":
                quantise_alone(last - 1)
            elif move[0] == "a":
                last_passes(int(move[1]), int(move[2]))
            elif move[0] == "g":
                quantise_part[move[1]] = last_unit_part(int(move[1]))
            elif move[0] == "Q":
                quantise_part[move[1]]()
            elif move[0] == "f":
                o, part_banks = parts[int(move[1])]
                for tiles, bank in zip(tile_groups, part_banks):
                    finish(c, o, P, tiles, bank)
